import numpy as np
import ml_dtypes


def mxq(x, axis, fmt="e4m3"):
    dtype, down = {"e4m3": (ml_dtypes.float8_e4m3fn, 7), "e5m2": (ml_dtypes.float8_e5m2, 14)}[fmt]
    v = np.moveaxis(np.asarray(x, np.float32).astype(ml_dtypes.bfloat16).astype(np.float64), axis, -1)
    blocks = v.reshape(v.shape[:-1] + (-1, 32))
    amax = np.abs(blocks).max(-1, keepdims=True)
    byte = np.maximum(np.where(amax > 0, np.frexp(amax)[1] - 1 + 127, 0) - down, 1)
    scale = np.exp2(byte - 127.0)
    codes = (blocks / scale).astype(np.float32).astype(dtype).astype(np.float64)
    return np.moveaxis((codes * scale).reshape(v.shape), -1, axis)


WIDE = False


def mx_kscale(k):
    if not WIDE:
        return np.ones(k)
    levels = np.array([10, -10, 5, -5, 0])
    if k % 512:
        return np.exp2(np.random.permutation(np.resize(levels, k // 32))).repeat(32)
    a = np.empty((k // 512, 16))
    for p in range(k // 512):
        a[p, :8] = np.random.permutation(np.resize(levels, 8))
        for g in range(8):
            far = levels[np.abs(levels - a[p, g]) >= 10]
            a[p, g + 8] = far[np.random.randint(len(far))]
    return np.exp2(a.ravel()).repeat(32)


def f64(x):
    return np.asarray(x).astype(np.float64)


def striped(idx):
    return np.tile(idx.reshape(-1, 16).T, (8, 1)).astype(np.uint16)


def unstriped(offs):
    return offs[:16].T.reshape(-1).astype(np.int64)


E2M1 = np.array([0.0, 0.5, 1.0, 1.5, 2.0, 3.0, 4.0, 6.0, -0.0, -0.5, -1.0, -1.5, -2.0, -3.0, -4.0, -6.0])


def pack_weight(w, fmt):
    k, n = w.shape
    w = f64(np.asarray(w, np.float32).astype(ml_dtypes.bfloat16)).reshape(k // 32, 32, n)
    amax = np.abs(w).max(1)
    if fmt == "e4m3":
        byte = np.frexp(amax)[1] - 1 + 127 - 7
    else:
        mant, ex = np.frexp(amax / 6.0)
        byte = np.where(mant > 0.5, ex, ex - 1) + 127
    byte = np.clip(np.where(amax > 0, byte, 1), 1, 254)
    scaled = (w * np.exp2(127.0 - byte)[:, None, :]).reshape(k, n).astype(np.float32)
    by_word = np.ascontiguousarray(scaled.reshape(k // 512, 128, 4, n).transpose(0, 1, 3, 2))
    if fmt == "e4m3":
        words = by_word.astype(ml_dtypes.float8_e4m3fn).view(np.uint8)
    else:
        c = by_word.astype(ml_dtypes.float4_e2m1fn).view(np.uint8) & 0xF
        words = (c[..., 0::2] | (c[..., 1::2] << 4)).reshape(k // 512, 128, 2 * n)
    return np.ascontiguousarray(words), np.ascontiguousarray(byte.astype(np.uint8).reshape(k // 512, 16, n))


def unpack_weight(words, scales, fmt):
    g, _, n = scales.shape
    words = np.ascontiguousarray(words).reshape(g, 128, n, -1)
    if fmt == "e4m3":
        vals = words.view(ml_dtypes.float8_e4m3fn).astype(np.float64)
    else:
        nib = np.empty((g, 128, n, 4), np.uint8)
        nib[..., 0::2] = words & 0xF
        nib[..., 1::2] = words >> 4
        vals = E2M1[nib]
    vals = vals * np.repeat(np.exp2(scales.astype(np.float64) - 127.0), 8, axis=1)[..., None]
    return vals.transpose(0, 1, 3, 2).reshape(g * 512, n)


def gelu(v):
    return 0.5 * v * (1.0 + np.tanh(np.sqrt(2.0 / np.pi) * (v + 0.044715 * v**3)))


def bf(x):
    return np.asarray(x, np.float32).astype(ml_dtypes.bfloat16)


def planes(Y):
    n, m = Y.shape
    b = f64(bf(Y)).reshape(n // 32, 32, m)
    amax = np.abs(b).max(1)
    byte = np.clip(np.where(amax > 0, np.frexp(amax)[1] - 1 + 127 - 7, 1), 1, 254)
    codes = (b * np.exp2(127.0 - byte)[:, None, :]).reshape(n, m).astype(np.float32).astype(ml_dtypes.float8_e4m3fn).view(np.uint8)
    words = codes.reshape(n // 512, 128, 4, m).transpose(0, 1, 3, 2)
    return np.ascontiguousarray(words), np.ascontiguousarray(byte.astype(np.uint8).reshape(n // 512, 16, m))


K, H, N, T, S, T2, P, R = 1536, 512, 1024, 2048, 1024, 2048, 1024, 128

def setup_inputs():
    n = np.random.standard_normal
    s = mx_kscale(K)[:, None]
    u = mx_kscale(H)[:, None]
    tab_words, tab_scales = pack_weight(n((K, T)) * s, "e4m3")
    w4_words, w4_scales = pack_weight(n((K, H)) / np.sqrt(K) / s * u.T, "e2m1")
    w8_words, w8_scales = pack_weight(0.7 * n((H, N)) / np.sqrt(H) / u, "e4m3")
    return {
        "tab_words": tab_words, "tab_scales": tab_scales,
        "offs": striped(np.random.permutation(T)[:S]),
        "offs2": striped(np.random.permutation(T2)[:S]),
        "offs3": striped(np.random.permutation(T2)[:P]),
        "w1": (n((K, H)) / np.sqrt(K) / s * u.T).astype(np.float32),
        "w4_words": w4_words, "w4_scales": w4_scales,
        "wgs": np.exp(0.3 * n((R, S))).astype(np.float32),
        "old": (n((H, P)) * u).astype(np.float32),
        "w3": (0.7 * n((H, N)) / np.sqrt(H) / u).astype(np.float32),
        "w8_words": w8_words, "w8_scales": w8_scales,
        "amp": np.exp(0.8 * n(N)).astype(np.float32),
    }

def reference(tab_words, tab_scales, offs, offs2, offs3, w1, w4_words, w4_scales, wgs, old, w3, w8_words, w8_scales, amp):
    v = unpack_weight(tab_words, tab_scales, "e4m3")[:, unstriped(offs)]
    new_enc = mxq(f64(w1), 0, "e4m3").T @ v
    old_enc = unpack_weight(w4_words, w4_scales, "e2m1").T @ v
    h = new_enc - old_enc
    page = np.zeros((H, T2))
    page[:, unstriped(offs2)] = np.tile(f64(wgs), (H // R, 1)) * h
    x = page[:, unstriped(offs3)]
    zq = mxq(f64(old) - x, 0, "e4m3")
    bounded = np.tanh(mxq(f64(w3), 0, "e4m3").T @ zq)
    direct = unpack_weight(w8_words, w8_scales, "e4m3").T @ zq
    y = f64(amp)[:, None] * (bounded + direct)
    words, scales = planes(y)
    return y, words, scales

@@ -1,0 +1,377 @@
+from contextlib import ExitStack
+
+import concourse.mybir as mybir
+from concourse.masks import make_identity
+
+K, H, N, T, S, T2, M = 1536, 512, 1024, 2048, 1024, 2048, 1024
+FLOPS = 2 * (2 * K * H * S + 2 * H * N * M)
+
+F32 = mybir.dt.float32
+BF16 = mybir.dt.bfloat16
+I32 = mybir.dt.int32
+U32 = mybir.dt.uint32
+U16 = mybir.dt.uint16
+U8 = mybir.dt.uint8
+FP8X4 = mybir.dt.float8_e4m3fn_x4
+FP4X4 = mybir.dt.float4_e2m1fn_x4
+ALU = mybir.AluOpType
+ACT = mybir.ActivationFunctionType
+
+P = 128
+PACK = 4
+K_PASS = P * PACK
+PASSES = K // K_PASS
+BLOCKS = H // P
+GROUPS = N // K_PASS
+BANK = 512
+HALVES = S // BANK
+QUADS = 4
+LIST = 16
+BANKS = 8
+ON_SCALAR = 3
+SCALE_ROW0 = P - 16 * PASSES
+CHUNKS = ((0, 256), (256, 512), (768, 256))
+
+
+def tile_list_schema_drift_scores_kernel(
+    tc, tab_words, tab_scales, offs, offs2, offs3, w1, w4_words, w4_scales, wgs, old, w3,
+    w8_words, w8_scales, amp, out_0, out_1, out_2,
+):
+    nc = tc.nc
+    with ExitStack() as ctx:
+        lists = ctx.enter_context(tc.tile_pool(name="lists", bufs=1))
+        keep = ctx.enter_context(tc.tile_pool(name="keep", bufs=1))
+        psum = ctx.enter_context(tc.psum_pool(name="psum", bufs=1))
+
+        def held(shape, dtype, name, tag=None, bufs=1):
+            return keep.tile(shape, dtype, name=name, tag=tag or name, bufs=bufs, align_bytes=64)
+
+        banks_used = []
+
+        def next_bank(shape):
+            tag = "bank%d" % (len(banks_used) % BANKS)
+            banks_used.append(tag)
+            return psum.tile(shape, F32, name=tag, tag=tag)
+
+        def entries(list_tile, first, count):
+            return list_tile[:, first // LIST : (first + count) // LIST]
+
+        def load_scale_rows(queue, plane, rows):
+            for q in range(QUADS):
+                queue.dma_start(
+                    out=plane[32 * q : 32 * q + 4].bitcast(I32),
+                    in_=rows[:, 4 * q : 4 * q + 4, :].rearrange("a r c -> r a c").bitcast(I32),
+                )
+
+        picked_list = lists.tile([P, S // LIST], U16, name="picked_list")
+        slot_list = lists.tile([P, S // LIST], U16, name="slot_list")
+        pinned_list = lists.tile([P, M // LIST], U16, name="pinned_list")
+
+        table_scales = held([P, T], U8, "table_scales")
+        w4_plane = held([P, PASSES, H], U8, "w4_plane")
+        w8_plane_raw = held([P, 1, N], U8, "w8_plane_raw")
+        pages = [held([P, T2], F32, "page%d" % i) for i in range(2)]
+        nc.vector.memset(table_scales[0:64, :].bitcast(I32), 0)
+        nc.vector.memset(table_scales[64:SCALE_ROW0, :].bitcast(I32), 0)
+        nc.gpsimd.memset(w4_plane[:].bitcast(I32), 0)
+        nc.gpsimd.memset(w8_plane_raw[:].bitcast(I32), 0)
+        v_plane = held([P, PASSES, S], U8, "v_plane")
+        nc.vector.memset(v_plane[:].bitcast(I32), 0)
+        for page in pages:
+            nc.vector.memset(page[:], 0.0)
+
+        table = [held([P, T], U32, "table%d" % a) for a in range(PASSES)]
+        w1_raw = [held([P, PACK, H], F32, "w1_raw%d" % a, tag="wide%d" % a) for a in range(PASSES)]
+
+        def load_table(a):
+            nc.sync.dma_start(
+                out=table[a][:].bitcast(I32),
+                in_=tab_words[a].rearrange("p t i -> p (t i)").bitcast(I32),
+            )
+
+        def load_w1(a):
+            nc.sync.dma_start(
+                out=w1_raw[a][:],
+                in_=w1[K_PASS * a : K_PASS * (a + 1), :].rearrange("(p j) c -> p j c", j=PACK),
+            )
+
+        nc.sync.dma_start(picked_list[:], offs)
+        nc.sync.dma_start(
+            out=table_scales[SCALE_ROW0:P, :].bitcast(I32),
+            in_=tab_scales.rearrange("a r c -> r a c").bitcast(I32),
+        )
+        load_table(0)
+        load_w1(0)
+        w4_codes = held([P, PASSES, 2 * H], U8, "w4_codes")
+        nc.sync.dma_start(
+            out=w4_codes[:].bitcast(I32), in_=w4_words.rearrange("a p c -> p a c").bitcast(I32)
+        )
+        load_w1(1)
+        load_table(1)
+        load_w1(2)
+        load_table(2)
+        w8_raw = held([P, N], I32, "w8_raw")
+        nc.sync.dma_start(
+            out=w8_raw[:], in_=w8_words[0].rearrange("p c i -> p (c i)").bitcast(I32)
+        )
+        nc.sync.dma_start(slot_list[:], offs2)
+        gains = held([P, S], F32, "gains", tag="late")
+        nc.sync.dma_start(out=gains[:], in_=wgs)
+        nc.sync.dma_start(pinned_list[:], offs3)
+        old_rows = [held([P, M], F32, "old%d" % b) for b in range(BLOCKS)]
+        for b in range(BLOCKS):
+            nc.sync.dma_start(out=old_rows[b][:], in_=old[P * b : P * (b + 1), :])
+        w3_raw = held([P, PACK, N], F32, "w3_raw")
+        nc.sync.dma_start(out=w3_raw[:], in_=w3.rearrange("(p j) c -> p j c", j=PACK))
+
+        load_scale_rows(nc.gpsimd, w4_plane, w4_scales)
+        load_scale_rows(nc.gpsimd, w8_plane_raw, w8_scales)
+        amp_cols = held([P, GROUPS, PACK], F32, "amp_cols")
+        nc.sync.dma_start(out=amp_cols[:], in_=amp.rearrange("(g p t) -> p g t", p=P, t=PACK))
+        ident = held([P, P], F32, "ident")
+        make_identity(nc, ident[:])
+
+        v_codes = [held([P, S], U32, "v_codes%d" % a) for a in range(PASSES)]
+        picked_scales = held([P, S], U8, "picked_scales")
+        w1_codes = [held([P, H], U32, "w1_codes%d" % a) for a in range(PASSES)]
+        w1_plane = [held([P, H], U8, "w1_plane%d" % a) for a in range(PASSES)]
+
+        def gather_words(a, first, count):
+            nc.vector.tensor_copy(
+                out=v_codes[a][:, first : first + count],
+                in_=table[a][:].indirect(entries(picked_list, first, count)),
+            )
+
+        def gather_scales():
+            nc.vector.tensor_copy(out=picked_scales[:], in_=table_scales[:].indirect(picked_list[:]))
+            for q in range(QUADS):
+                nc.gpsimd.dma_start(
+                    out=v_plane[32 * q : 32 * q + 4].bitcast(I32),
+                    in_=picked_scales[
+                        SCALE_ROW0 + 4 * PASSES * q : SCALE_ROW0 + 4 * PASSES * (q + 1), :
+                    ].bitcast(I32),
+                )
+
+        def quantise_w1(a):
+            rounded = held([P, H, PACK], BF16, "w1_rounded", tag="rounded", bufs=3)
+            nc.scalar.activation(
+                out=rounded[:].rearrange("p (c i) j -> p c j i", i=4),
+                in_=w1_raw[a][:].rearrange("p j (c i) -> p c j i", i=4),
+                func=ACT.Copy,
+                scale=-1.0,
+            )
+            nc.vector.quantize_mx(
+                out=w1_codes[a][:].bitcast(FP8X4),
+                scales=w1_plane[a][:],
+                in_=rounded[:].rearrange("p c j -> p (c j)"),
+            )
+
+        gather_scales()
+        gather_words(0, 0, S)
+        quantise_w1(0)
+        quantise_w1(1)
+        gather_words(1, 0, S)
+        quantise_w1(2)
+        for half in range(HALVES):
+            gather_words(2, BANK * half, BANK)
+
+        w8_codes = held([P, GROUPS, PACK, P], I32, "w8_codes")
+        w8_plane = held([P, GROUPS, PACK, P], U8, "w8_plane")
+        nc.vector.tensor_copy(
+            out=w8_codes[:].rearrange("p g t m -> p g m t"),
+            in_=w8_raw[:].rearrange("p (g m t) -> p g m t", g=GROUPS, t=PACK),
+        )
+        nc.vector.tensor_copy(
+            out=w8_plane[:].rearrange("p g t m -> p g m t"),
+            in_=w8_plane_raw[:, 0, :].rearrange("p (g m t) -> p g m t", g=GROUPS, t=PACK),
+        )
+
+        order = [(b, half) for pair in range(0, BLOCKS, 2) for half in range(HALVES) for b in (pair, pair + 1)]
+        sums = {key: next_bank([P, BANK]) for key in order}
+
+        def encode(a, b, half):
+            cols = slice(BANK * half, BANK * (half + 1))
+            rows = slice(P * b, P * (b + 1))
+            nc.tensor.matmul_mx(
+                out=sums[b, half][:],
+                lhsT=w1_codes[a][:, rows].bitcast(FP8X4), lhsT_scale=w1_plane[a][:, rows],
+                rhs=v_codes[a][:, cols].bitcast(FP8X4), rhs_scale=v_plane[:, a, cols],
+                start=(a == 0), stop=False,
+            )
+            nc.tensor.matmul_mx(
+                out=sums[b, half][:],
+                lhsT=w4_codes[:, a, 2 * P * b : 2 * P * (b + 1)].bitcast(FP4X4),
+                lhsT_scale=w4_plane[:, a, rows],
+                rhs=v_codes[a][:, cols].bitcast(FP8X4), rhs_scale=v_plane[:, a, cols],
+                start=False, stop=(a == PASSES - 1),
+            )
+
+        deltas = [held([P, S], F32, "deltas%d" % b) for b in range(BLOCKS)]
+        for b, half in order:
+            for a in range(PASSES):
+                encode(a, b, half)
+            nc.scalar.copy(out=deltas[b][:, BANK * half : BANK * (half + 1)], in_=sums[b, half][:])
+
+        w3_rounded = held([P, GROUPS, PACK, P, PACK], BF16, "w3_rounded")
+        for g in range(GROUPS):
+            nc.scalar.copy(
+                out=w3_rounded[:, g].rearrange("p t m j -> p m j t"),
+                in_=w3_raw[:, :, K_PASS * g : K_PASS * (g + 1)].rearrange("p j (m t) -> p m j t", t=PACK),
+            )
+
+        z_turned = [
+            held([P, width // P, 2, P, 2], BF16, "z_turned%d" % c) for c, (first, width) in enumerate(CHUNKS)
+        ]
+
+        def scatter(b, first, count):
+            cols = slice(first, first + count)
+            nc.vector.tensor_tensor(
+                out=pages[b % 2][:].indirect(entries(slot_list, first, count)),
+                in0=deltas[b][:, cols], in1=gains[:, cols], op=ALU.mult,
+            )
+
+        def turn(b, c, picked):
+            first, width = CHUNKS[c]
+            subs = width // P
+            turned = next_bank([P, subs, P])
+            for s in range(subs):
+                nc.tensor.matmul(
+                    out=turned[:, s, :], lhsT=old_rows[b][:, first + P * s : first + P * (s + 1)],
+                    rhs=ident[:], is_transpose=True, start=(s == 0), stop=False,
+                )
+            for s in range(subs):
+                nc.tensor.matmul(
+                    out=turned[:, s, :], lhsT=picked[:, first + P * s : first + P * (s + 1)],
+                    rhs=ident[:], is_transpose=True, start=False, stop=(s == subs - 1),
+                )
+            nc.scalar.copy(
+                out=z_turned[c][:, :, :, 32 * b : 32 * (b + 1), :],
+                in_=turned[:].rearrange("m s (q u e) -> m s u q e", u=2, e=2),
+            )
+
+        def fetch_all(b):
+            picked = held([P, M], F32, "picked", bufs=2)
+            for first, width in CHUNKS if b == BLOCKS - 1 else ((0, M),):
+                nc.vector.tensor_copy(
+                    out=picked[:, first : first + width],
+                    in_=pages[b % 2][:].indirect(entries(pinned_list, first, width)),
+                )
+            for c in range(len(CHUNKS)):
+                turn(b, c, picked)
+            return picked
+
+        for half in range(HALVES):
+            scatter(0, BANK * half, BANK)
+            scatter(1, BANK * half, BANK)
+        fetch_all(0)
+        scatter(2, 0, S)
+        fetch_all(1)
+        fetch_all(2)
+        scatter(3, 0, S)
+        fetch_all(3)
+
+        w3_codes = held([P, N], U32, "w3_codes", tag="late")
+        w3_plane = held([P, N], U8, "w3_plane")
+        nc.vector.quantize_mx(
+            out=w3_codes[:].bitcast(FP8X4), scales=w3_plane[:],
+            in_=w3_rounded[:].rearrange("p g t m j -> p (g t m j)"),
+        )
+
+        z_codes = [held([P, width], U32, "z_codes%d" % c) for c, (first, width) in enumerate(CHUNKS)]
+        z_plane = [held([P, width], U8, "z_plane%d" % c) for c, (first, width) in enumerate(CHUNKS)]
+
+        def quantise_z(c):
+            first, width = CHUNKS[c]
+            z_rounded = held([P, width, PACK], BF16, "z_rounded%d" % c)
+            z_words = z_rounded[:].rearrange("p m t -> p (m t)").bitcast(F32)
+            for s0 in range(0, width // P, 2):
+                back = next_bank([P, 2, 2, P])
+                for s in range(2):
+                    for u in range(2):
+                        nc.tensor.transpose(
+                            back[:, s, u, :],
+                            z_turned[c][:, s0 + s, u].rearrange("m p e -> m (p e)").bitcast(F32),
+                            ident[:],
+                        )
+                nc.scalar.copy(
+                    out=z_words[:, 2 * P * s0 : 2 * P * (s0 + 2)].rearrange("p (s m u) -> p s m u", s=2, u=2),
+                    in_=back[:].rearrange("p s u m -> p s m u"),
+                )
+            nc.vector.quantize_mx(
+                out=z_codes[c][:].bitcast(FP8X4), scales=z_plane[c][:],
+                in_=z_rounded[:].rearrange("p m t -> p (m t)"),
+            )
+
+        y_plane = held([P, GROUPS, M], U8, "y_plane")
+        w8_flat = w8_codes[:].rearrange("p g t m -> p (g t m)")
+        w8_plane_flat = w8_plane[:].rearrange("p g t m -> p (g t m)")
+        units = []
+
+        def score(c, g):
+            first, width = CHUNKS[c]
+            cols = slice(first, first + width)
+            y = held([P, PACK, width], F32, "y", tag="wide%d" % (len(units) % PASSES))
+            units.append((c, g))
+            y_rows = out_0[K_PASS * g : K_PASS * (g + 1), cols].rearrange("(p t) m -> p t m", t=PACK)
+            for t in range(PACK):
+                n_cols = slice(K_PASS * g + P * t, K_PASS * g + P * (t + 1))
+                gain = amp_cols[:, g, t : t + 1]
+                bounded_sum = next_bank([P, width])
+                direct_sum = next_bank([P, width])
+                nc.tensor.matmul_mx(
+                    out=bounded_sum[:],
+                    lhsT=w3_codes[:, n_cols].bitcast(FP8X4), lhsT_scale=w3_plane[:, n_cols],
+                    rhs=z_codes[c][:].bitcast(FP8X4), rhs_scale=z_plane[c][:],
+                    start=True, stop=True,
+                )
+                nc.tensor.matmul_mx(
+                    out=direct_sum[:],
+                    lhsT=w8_flat[:, n_cols].bitcast(FP8X4), lhsT_scale=w8_plane_flat[:, n_cols],
+                    rhs=z_codes[c][:].bitcast(FP8X4), rhs_scale=z_plane[c][:],
+                    start=True, stop=True,
+                )
+                bounded = held([P, width], F32, "bounded", bufs=4)
+                nc.scalar.activation(out=bounded[:], in_=bounded_sum[:], func=ACT.Tanh)
+                if t < ON_SCALAR:
+                    nc.scalar.activation(out=y[:, t, :], in_=direct_sum[:], func=ACT.Copy, scale=gain)
+                    nc.vector.scalar_tensor_tensor(
+                        out=y[:, t, :], in0=bounded[:], scalar=gain, in1=y[:, t, :],
+                        op0=ALU.mult, op1=ALU.add,
+                    )
+                else:
+                    both = held([P, width], F32, "both", bufs=2)
+                    nc.vector.tensor_tensor(out=both[:], in0=direct_sum[:], in1=bounded[:], op=ALU.add)
+                    nc.vector.tensor_scalar(
+                        out=y[:, t, :], in0=both[:], scalar1=gain, scalar2=None, op0=ALU.mult
+                    )
+                if t % 2 == 1:
+                    nc.sync.dma_start(out=y_rows[:, t - 1 : t + 1, :], in_=y[:, t - 1 : t + 1, :])
+            y_rounded = held([P, width, PACK], BF16, "y_rounded", tag="rounded", bufs=3)
+            nc.vector.tensor_copy(
+                out=y_rounded[:].rearrange("p (c i) t -> p c t i", i=4),
+                in_=y[:].rearrange("p t (c i) -> p c t i", i=4),
+            )
+            y_codes = held([P, width], U32, "y_codes", bufs=3)
+            nc.vector.quantize_mx(
+                out=y_codes[:].bitcast(FP8X4), scales=y_plane[:, g, cols],
+                in_=y_rounded[:].rearrange("p m t -> p (m t)"),
+            )
+            nc.sync.dma_start(
+                out=out_1[g].rearrange("p m t -> p (m t)").bitcast(I32)[:, cols],
+                in_=y_codes[:].bitcast(I32),
+            )
+
+        quantise_z(0)
+        quantise_z(1)
+        score(0, 0)
+        quantise_z(2)
+        score(0, 1)
+        for c in range(1, len(CHUNKS)):
+            for g in range(GROUPS):
+                score(c, g)
+        for q in range(QUADS):
+            queue = nc.sync if q % 2 == 0 else nc.scalar
+            queue.dma_start(
+                out=out_2[:, 4 * q : 4 * q + 4, :].rearrange("g r m -> r g m").bitcast(I32),
+                in_=y_plane[32 * q : 32 * q + 4].bitcast(I32),
+            )

@@ -46,12 +46,14 @@ def tile_list_schema_drift_scores_kernel(
         def held(shape, dtype, name, tag=None, bufs=1):
             return keep.tile(shape, dtype, name=name, tag=tag or name, bufs=bufs, align_bytes=64)
 
+        def bank(index, shape):
+            return psum.tile(shape, F32, name="bank%d" % index, tag="bank%d" % index)
+
         banks_used = []
 
         def next_bank(shape):
-            tag = "bank%d" % (len(banks_used) % BANKS)
-            banks_used.append(tag)
-            return psum.tile(shape, F32, name=tag, tag=tag)
+            banks_used.append(shape)
+            return bank((BANKS // 2 + len(banks_used) - 1) % BANKS, shape)
 
         def entries(list_tile, first, count):
             return list_tile[:, first // LIST : (first + count) // LIST]
@@ -70,15 +72,12 @@ def tile_list_schema_drift_scores_kernel(
         table_scales = held([P, T], U8, "table_scales")
         w4_plane = held([P, PASSES, H], U8, "w4_plane")
         w8_plane_raw = held([P, 1, N], U8, "w8_plane_raw")
-        pages = [held([P, T2], F32, "page%d" % i) for i in range(2)]
         nc.vector.memset(table_scales[0:64, :].bitcast(I32), 0)
         nc.vector.memset(table_scales[64:SCALE_ROW0, :].bitcast(I32), 0)
         nc.gpsimd.memset(w4_plane[:].bitcast(I32), 0)
         nc.gpsimd.memset(w8_plane_raw[:].bitcast(I32), 0)
         v_plane = held([P, PASSES, S], U8, "v_plane")
         nc.vector.memset(v_plane[:].bitcast(I32), 0)
-        for page in pages:
-            nc.vector.memset(page[:], 0.0)
 
         table = [held([P, T], U32, "table%d" % a) for a in range(PASSES)]
         w1_raw = [held([P, PACK, H], F32, "w1_raw%d" % a, tag="wide%d" % a) for a in range(PASSES)]
@@ -100,12 +99,22 @@ def tile_list_schema_drift_scores_kernel(
             out=table_scales[SCALE_ROW0:P, :].bitcast(I32),
             in_=tab_scales.rearrange("a r c -> r a c").bitcast(I32),
         )
+        load_scale_rows(nc.sync, w4_plane, w4_scales)
         load_table(0)
         load_w1(0)
         w4_codes = held([P, PASSES, 2 * H], U8, "w4_codes")
         nc.sync.dma_start(
             out=w4_codes[:].bitcast(I32), in_=w4_words.rearrange("a p c -> p a c").bitcast(I32)
         )
+        picked_scales = held([P, S], U8, "picked_scales")
+        nc.vector.tensor_copy(out=picked_scales[:], in_=table_scales[:].indirect(picked_list[:]))
+        for q in range(QUADS):
+            nc.sync.dma_start(
+                out=v_plane[32 * q : 32 * q + 4].bitcast(I32),
+                in_=picked_scales[
+                    SCALE_ROW0 + 4 * PASSES * q : SCALE_ROW0 + 4 * PASSES * (q + 1), :
+                ].bitcast(I32),
+            )
         load_w1(1)
         load_table(1)
         load_w1(2)
@@ -119,20 +128,18 @@ def tile_list_schema_drift_scores_kernel(
         nc.sync.dma_start(out=gains[:], in_=wgs)
         nc.sync.dma_start(pinned_list[:], offs3)
         old_rows = [held([P, M], F32, "old%d" % b) for b in range(BLOCKS)]
-        for b in range(BLOCKS):
-            nc.sync.dma_start(out=old_rows[b][:], in_=old[P * b : P * (b + 1), :])
         w3_raw = held([P, PACK, N], F32, "w3_raw")
-        nc.sync.dma_start(out=w3_raw[:], in_=w3.rearrange("(p j) c -> p j c", j=PACK))
-
-        load_scale_rows(nc.gpsimd, w4_plane, w4_scales)
+        for b in range(BLOCKS):
+            if b == 1:
+                nc.sync.dma_start(out=w3_raw[:], in_=w3.rearrange("(p j) c -> p j c", j=PACK))
+            nc.sync.dma_start(out=old_rows[b][:], in_=old[P * b : P * (b + 1), :])
         load_scale_rows(nc.gpsimd, w8_plane_raw, w8_scales)
-        amp_cols = held([P, GROUPS, PACK], F32, "amp_cols")
-        nc.sync.dma_start(out=amp_cols[:], in_=amp.rearrange("(g p t) -> p g t", p=P, t=PACK))
         ident = held([P, P], F32, "ident")
         make_identity(nc, ident[:])
+        amp_cols = held([P, GROUPS, PACK], F32, "amp_cols")
+        nc.gpsimd.dma_start(out=amp_cols[:], in_=amp.rearrange("(g p t) -> p g t", p=P, t=PACK))
 
         v_codes = [held([P, S], U32, "v_codes%d" % a) for a in range(PASSES)]
-        picked_scales = held([P, S], U8, "picked_scales")
         w1_codes = [held([P, H], U32, "w1_codes%d" % a) for a in range(PASSES)]
         w1_plane = [held([P, H], U8, "w1_plane%d" % a) for a in range(PASSES)]
 
@@ -141,16 +148,6 @@ def tile_list_schema_drift_scores_kernel(
                 out=v_codes[a][:, first : first + count],
                 in_=table[a][:].indirect(entries(picked_list, first, count)),
             )
-
-        def gather_scales():
-            nc.vector.tensor_copy(out=picked_scales[:], in_=table_scales[:].indirect(picked_list[:]))
-            for q in range(QUADS):
-                nc.gpsimd.dma_start(
-                    out=v_plane[32 * q : 32 * q + 4].bitcast(I32),
-                    in_=picked_scales[
-                        SCALE_ROW0 + 4 * PASSES * q : SCALE_ROW0 + 4 * PASSES * (q + 1), :
-                    ].bitcast(I32),
-                )
 
         def quantise_w1(a):
             rounded = held([P, H, PACK], BF16, "w1_rounded", tag="rounded", bufs=3)
@@ -166,9 +163,12 @@ def tile_list_schema_drift_scores_kernel(
                 in_=rounded[:].rearrange("p c j -> p (c j)"),
             )
 
-        gather_scales()
         gather_words(0, 0, S)
+        pages = [held([P, T2], F32, "page%d" % i, tag=tag) for i, tag in ((1, "table0"),)]
+        nc.vector.memset(pages[0][:], 0.0)
         quantise_w1(0)
+        pages = [held([P, T2], F32, "page0", tag="wide0")] + pages
+        nc.vector.memset(pages[0][:], 0.0)
         quantise_w1(1)
         gather_words(1, 0, S)
         quantise_w1(2)
@@ -187,7 +187,7 @@ def tile_list_schema_drift_scores_kernel(
         )
 
         order = [(b, half) for pair in range(0, BLOCKS, 2) for half in range(HALVES) for b in (pair, pair + 1)]
-        sums = {key: next_bank([P, BANK]) for key in order}
+        sums = {}
 
         def encode(a, b, half):
             cols = slice(BANK * half, BANK * (half + 1))
@@ -207,7 +207,8 @@ def tile_list_schema_drift_scores_kernel(
             )
 
         deltas = [held([P, S], F32, "deltas%d" % b) for b in range(BLOCKS)]
-        for b, half in order:
+        for i, (b, half) in enumerate(order):
+            sums[b, half] = bank(i % (BANKS // 2), [P, BANK])
             for a in range(PASSES):
                 encode(a, b, half)
             nc.scalar.copy(out=deltas[b][:, BANK * half : BANK * (half + 1)], in_=sums[b, half][:])

@@ -28,8 +28,8 @@ HALVES = S // BANK
 QUADS = 4
 LIST = 16
 BANKS = 8
-ON_SCALAR = 3
 SCALE_ROW0 = P - 16 * PASSES
+W1_SPANS = ((0, 128), (128, 128), (256, 256))
 CHUNKS = ((0, 256), (256, 512), (768, 256))
 
 
@@ -78,9 +78,11 @@ def tile_list_schema_drift_scores_kernel(
         nc.gpsimd.memset(w8_plane_raw[:].bitcast(I32), 0)
         v_plane = held([P, PASSES, S], U8, "v_plane")
         nc.vector.memset(v_plane[:].bitcast(I32), 0)
+        first_page = held([P, T2], F32, "first_page")
+        nc.vector.memset(first_page[:], 0.0)
 
         table = [held([P, T], U32, "table%d" % a) for a in range(PASSES)]
-        w1_raw = [held([P, PACK, H], F32, "w1_raw%d" % a, tag="wide%d" % a) for a in range(PASSES)]
+        w1_raw = {}
 
         def load_table(a):
             nc.sync.dma_start(
@@ -88,60 +90,57 @@ def tile_list_schema_drift_scores_kernel(
                 in_=tab_words[a].rearrange("p t i -> p (t i)").bitcast(I32),
             )
 
-        def load_w1(a):
-            nc.sync.dma_start(
-                out=w1_raw[a][:],
-                in_=w1[K_PASS * a : K_PASS * (a + 1), :].rearrange("(p j) c -> p j c", j=PACK),
-            )
+        def load_w1(span):
+            first, width = W1_SPANS[span]
+            for a in range(PASSES):
+                w1_raw[span, a] = held([P, PACK, width], F32, "w1_raw%d_%d" % (span, a))
+                nc.sync.dma_start(
+                    out=w1_raw[span, a][:],
+                    in_=w1[K_PASS * a : K_PASS * (a + 1), first : first + width].rearrange(
+                        "(p j) c -> p j c", j=PACK
+                    ),
+                )
 
         nc.sync.dma_start(picked_list[:], offs)
         nc.sync.dma_start(
             out=table_scales[SCALE_ROW0:P, :].bitcast(I32),
             in_=tab_scales.rearrange("a r c -> r a c").bitcast(I32),
         )
-        load_scale_rows(nc.sync, w4_plane, w4_scales)
-        load_table(0)
+        load_scale_rows(nc.gpsimd, w4_plane, w4_scales)
         load_w1(0)
+        load_table(0)
+        load_table(1)
         w4_codes = held([P, PASSES, 2 * H], U8, "w4_codes")
         nc.sync.dma_start(
             out=w4_codes[:].bitcast(I32), in_=w4_words.rearrange("a p c -> p a c").bitcast(I32)
         )
-        picked_scales = held([P, S], U8, "picked_scales")
-        nc.vector.tensor_copy(out=picked_scales[:], in_=table_scales[:].indirect(picked_list[:]))
-        for q in range(QUADS):
-            nc.sync.dma_start(
-                out=v_plane[32 * q : 32 * q + 4].bitcast(I32),
-                in_=picked_scales[
-                    SCALE_ROW0 + 4 * PASSES * q : SCALE_ROW0 + 4 * PASSES * (q + 1), :
-                ].bitcast(I32),
-            )
-        load_w1(1)
-        load_table(1)
-        load_w1(2)
         load_table(2)
+        load_w1(1)
+        nc.sync.dma_start(slot_list[:], offs2)
+        gains = held([P, S], F32, "gains", tag="late")
+        nc.sync.dma_start(out=gains[:, 0:BANK], in_=wgs[:, 0:BANK])
+        load_w1(2)
+        nc.sync.dma_start(out=gains[:, BANK:S], in_=wgs[:, BANK:S])
+        nc.sync.dma_start(pinned_list[:], offs3)
+        old_rows = [held([P, M], F32, "old%d" % b) for b in range(BLOCKS)]
+        nc.sync.dma_start(out=old_rows[0][:], in_=old[0:P, :])
+        load_scale_rows(nc.sync, w8_plane_raw, w8_scales)
         w8_raw = held([P, N], I32, "w8_raw")
         nc.sync.dma_start(
             out=w8_raw[:], in_=w8_words[0].rearrange("p c i -> p (c i)").bitcast(I32)
         )
-        nc.sync.dma_start(slot_list[:], offs2)
-        gains = held([P, S], F32, "gains", tag="late")
-        nc.sync.dma_start(out=gains[:], in_=wgs)
-        nc.sync.dma_start(pinned_list[:], offs3)
-        old_rows = [held([P, M], F32, "old%d" % b) for b in range(BLOCKS)]
         w3_raw = held([P, PACK, N], F32, "w3_raw")
-        for b in range(BLOCKS):
-            if b == 1:
-                nc.sync.dma_start(out=w3_raw[:], in_=w3.rearrange("(p j) c -> p j c", j=PACK))
+        nc.sync.dma_start(out=w3_raw[:], in_=w3.rearrange("(p j) c -> p j c", j=PACK))
+        for b in range(1, BLOCKS):
             nc.sync.dma_start(out=old_rows[b][:], in_=old[P * b : P * (b + 1), :])
-        load_scale_rows(nc.gpsimd, w8_plane_raw, w8_scales)
         ident = held([P, P], F32, "ident")
         make_identity(nc, ident[:])
         amp_cols = held([P, GROUPS, PACK], F32, "amp_cols")
         nc.gpsimd.dma_start(out=amp_cols[:], in_=amp.rearrange("(g p t) -> p g t", p=P, t=PACK))
 
         v_codes = [held([P, S], U32, "v_codes%d" % a) for a in range(PASSES)]
-        w1_codes = [held([P, H], U32, "w1_codes%d" % a) for a in range(PASSES)]
-        w1_plane = [held([P, H], U8, "w1_plane%d" % a) for a in range(PASSES)]
+        w1_codes = [held([P, PASSES, width], U32, "w1_codes%d" % first) for first, width in W1_SPANS]
+        w1_plane = [held([P, PASSES, width], U8, "w1_plane%d" % first) for first, width in W1_SPANS]
 
         def gather_words(a, first, count):
             nc.vector.tensor_copy(
@@ -149,52 +148,51 @@ def tile_list_schema_drift_scores_kernel(
                 in_=table[a][:].indirect(entries(picked_list, first, count)),
             )
 
-        def quantise_w1(a):
-            rounded = held([P, H, PACK], BF16, "w1_rounded", tag="rounded", bufs=3)
-            nc.scalar.activation(
-                out=rounded[:].rearrange("p (c i) j -> p c j i", i=4),
-                in_=w1_raw[a][:].rearrange("p j (c i) -> p c j i", i=4),
-                func=ACT.Copy,
-                scale=-1.0,
-            )
-            nc.vector.quantize_mx(
-                out=w1_codes[a][:].bitcast(FP8X4),
-                scales=w1_plane[a][:],
-                in_=rounded[:].rearrange("p c j -> p (c j)"),
-            )
+        def quantise_w1(span):
+            for a in range(PASSES):
+                rounded = held([P, W1_SPANS[span][1], PACK], BF16, "w1_rounded", tag="rounded", bufs=3)
+                nc.scalar.activation(
+                    out=rounded[:].rearrange("p (c i) j -> p c j i", i=4),
+                    in_=w1_raw[span, a][:].rearrange("p j (c i) -> p c j i", i=4),
+                    func=ACT.Copy,
+                    scale=-1.0,
+                )
+                nc.vector.quantize_mx(
+                    out=w1_codes[span][:, a, :].bitcast(FP8X4),
+                    scales=w1_plane[span][:, a, :],
+                    in_=rounded[:].rearrange("p c j -> p (c j)"),
+                )
 
-        gather_words(0, 0, S)
-        pages = [held([P, T2], F32, "page%d" % i, tag=tag) for i, tag in ((1, "table0"),)]
-        nc.vector.memset(pages[0][:], 0.0)
+        picked_scales = held([P, S], U8, "picked_scales")
+        nc.vector.tensor_copy(out=picked_scales[:], in_=table_scales[:].indirect(picked_list[:]))
         quantise_w1(0)
-        pages = [held([P, T2], F32, "page0", tag="wide0")] + pages
-        nc.vector.memset(pages[0][:], 0.0)
-        quantise_w1(1)
+        for q in range(QUADS):
+            nc.scalar.dma_start(
+                out=v_plane[32 * q : 32 * q + 4].bitcast(I32),
+                in_=picked_scales[
+                    SCALE_ROW0 + 4 * PASSES * q : SCALE_ROW0 + 4 * PASSES * (q + 1), :
+                ].bitcast(I32),
+            )
+        gather_words(0, 0, S)
         gather_words(1, 0, S)
-        quantise_w1(2)
         for half in range(HALVES):
             gather_words(2, BANK * half, BANK)
-
+        second_page = held([P, T2], F32, "second_page", tag="table2")
+        nc.vector.memset(second_page[:], 0.0)
+        pages = [first_page, second_page]
         w8_codes = held([P, GROUPS, PACK, P], I32, "w8_codes")
         w8_plane = held([P, GROUPS, PACK, P], U8, "w8_plane")
-        nc.vector.tensor_copy(
-            out=w8_codes[:].rearrange("p g t m -> p g m t"),
-            in_=w8_raw[:].rearrange("p (g m t) -> p g m t", g=GROUPS, t=PACK),
-        )
-        nc.vector.tensor_copy(
-            out=w8_plane[:].rearrange("p g t m -> p g m t"),
-            in_=w8_plane_raw[:, 0, :].rearrange("p (g m t) -> p g m t", g=GROUPS, t=PACK),
-        )
 
-        order = [(b, half) for pair in range(0, BLOCKS, 2) for half in range(HALVES) for b in (pair, pair + 1)]
         sums = {}
 
         def encode(a, b, half):
             cols = slice(BANK * half, BANK * (half + 1))
             rows = slice(P * b, P * (b + 1))
+            span = min(b, len(W1_SPANS) - 1)
+            own = slice(P * b - W1_SPANS[span][0], P * (b + 1) - W1_SPANS[span][0])
             nc.tensor.matmul_mx(
                 out=sums[b, half][:],
-                lhsT=w1_codes[a][:, rows].bitcast(FP8X4), lhsT_scale=w1_plane[a][:, rows],
+                lhsT=w1_codes[span][:, a, own].bitcast(FP8X4), lhsT_scale=w1_plane[span][:, a, own],
                 rhs=v_codes[a][:, cols].bitcast(FP8X4), rhs_scale=v_plane[:, a, cols],
                 start=(a == 0), stop=False,
             )
@@ -207,17 +205,20 @@ def tile_list_schema_drift_scores_kernel(
             )
 
         deltas = [held([P, S], F32, "deltas%d" % b) for b in range(BLOCKS)]
-        for i, (b, half) in enumerate(order):
-            sums[b, half] = bank(i % (BANKS // 2), [P, BANK])
-            for a in range(PASSES):
-                encode(a, b, half)
-            nc.scalar.copy(out=deltas[b][:, BANK * half : BANK * (half + 1)], in_=sums[b, half][:])
+        for b in range(BLOCKS):
+            if 0 < b < len(W1_SPANS):
+                quantise_w1(b)
+            for half in range(HALVES):
+                sums[b, half] = bank((HALVES * b + half) % (BANKS // 2), [P, BANK])
+                for a in range(PASSES):
+                    encode(a, b, half)
+                nc.scalar.copy(out=deltas[b][:, BANK * half : BANK * (half + 1)], in_=sums[b, half][:])
 
         w3_rounded = held([P, GROUPS, PACK, P, PACK], BF16, "w3_rounded")
         for g in range(GROUPS):
             nc.scalar.copy(
-                out=w3_rounded[:, g].rearrange("p t m j -> p m j t"),
-                in_=w3_raw[:, :, K_PASS * g : K_PASS * (g + 1)].rearrange("p j (m t) -> p m j t", t=PACK),
+                out=w3_rounded[:, g].rearrange("p t m j -> p m t j"),
+                in_=w3_raw[:, :, K_PASS * g : K_PASS * (g + 1)].rearrange("p j (m t) -> p m t j", t=PACK),
             )
 
         z_turned = [
@@ -263,8 +264,16 @@ def tile_list_schema_drift_scores_kernel(
 
         for half in range(HALVES):
             scatter(0, BANK * half, BANK)
-            scatter(1, BANK * half, BANK)
+        nc.vector.tensor_copy(
+            out=w8_plane[:].rearrange("p g t (c i) -> p g c t i", i=16),
+            in_=w8_plane_raw[:, 0, :].rearrange("p (g c i t) -> p g c t i", g=GROUPS, i=16, t=PACK),
+        )
+        scatter(1, 0, S)
         fetch_all(0)
+        nc.vector.tensor_copy(
+            out=w8_codes[:].rearrange("p g t (c i) -> p g c t i", i=4),
+            in_=w8_raw[:].rearrange("p (g c i t) -> p g c t i", g=GROUPS, i=4, t=PACK),
+        )
         scatter(2, 0, S)
         fetch_all(1)
         fetch_all(2)
@@ -308,10 +317,34 @@ def tile_list_schema_drift_scores_kernel(
         w8_plane_flat = w8_plane[:].rearrange("p g t m -> p (g t m)")
         units = []
 
-        def score(c, g):
+        def finish_steps(c, g, y):
             first, width = CHUNKS[c]
             cols = slice(first, first + width)
-            y = held([P, PACK, width], F32, "y", tag="wide%d" % (len(units) % PASSES))
+            y_rounded = held([P, width, PACK], BF16, "y_rounded", tag="rounded", bufs=3)
+            y_codes = held([P, width], U32, "y_codes", bufs=3)
+
+            def round_y():
+                nc.vector.tensor_copy(
+                    out=y_rounded[:].rearrange("p (c i) t -> p c t i", i=4),
+                    in_=y[:].rearrange("p t (c i) -> p c t i", i=4),
+                )
+
+            def quantise_y():
+                nc.vector.quantize_mx(
+                    out=y_codes[:].bitcast(FP8X4), scales=y_plane[:, g, cols],
+                    in_=y_rounded[:].rearrange("p m t -> p (m t)"),
+                )
+                nc.sync.dma_start(
+                    out=out_1[g].rearrange("p m t -> p (m t)").bitcast(I32)[:, cols],
+                    in_=y_codes[:].bitcast(I32),
+                )
+
+            return [round_y, quantise_y]
+
+        def score(c, g, pending):
+            first, width = CHUNKS[c]
+            cols = slice(first, first + width)
+            y = held([P, PACK, width], F32, "y", tag=("table0", "table1", "w3_raw")[len(units) % 3])
             units.append((c, g))
             y_rows = out_0[K_PASS * g : K_PASS * (g + 1), cols].rearrange("(p t) m -> p t m", t=PACK)
             for t in range(PACK):
@@ -333,43 +366,27 @@ def tile_list_schema_drift_scores_kernel(
                 )
                 bounded = held([P, width], F32, "bounded", bufs=4)
                 nc.scalar.activation(out=bounded[:], in_=bounded_sum[:], func=ACT.Tanh)
-                if t < ON_SCALAR:
-                    nc.scalar.activation(out=y[:, t, :], in_=direct_sum[:], func=ACT.Copy, scale=gain)
-                    nc.vector.scalar_tensor_tensor(
-                        out=y[:, t, :], in0=bounded[:], scalar=gain, in1=y[:, t, :],
-                        op0=ALU.mult, op1=ALU.add,
-                    )
-                else:
-                    both = held([P, width], F32, "both", bufs=2)
-                    nc.vector.tensor_tensor(out=both[:], in0=direct_sum[:], in1=bounded[:], op=ALU.add)
-                    nc.vector.tensor_scalar(
-                        out=y[:, t, :], in0=both[:], scalar1=gain, scalar2=None, op0=ALU.mult
-                    )
+                nc.scalar.activation(out=y[:, t, :], in_=direct_sum[:], func=ACT.Copy, scale=gain)
+                nc.vector.scalar_tensor_tensor(
+                    out=y[:, t, :], in0=bounded[:], scalar=gain, in1=y[:, t, :],
+                    op0=ALU.mult, op1=ALU.add,
+                )
                 if t % 2 == 1:
                     nc.sync.dma_start(out=y_rows[:, t - 1 : t + 1, :], in_=y[:, t - 1 : t + 1, :])
-            y_rounded = held([P, width, PACK], BF16, "y_rounded", tag="rounded", bufs=3)
-            nc.vector.tensor_copy(
-                out=y_rounded[:].rearrange("p (c i) t -> p c t i", i=4),
-                in_=y[:].rearrange("p t (c i) -> p c t i", i=4),
-            )
-            y_codes = held([P, width], U32, "y_codes", bufs=3)
-            nc.vector.quantize_mx(
-                out=y_codes[:].bitcast(FP8X4), scales=y_plane[:, g, cols],
-                in_=y_rounded[:].rearrange("p m t -> p (m t)"),
-            )
-            nc.sync.dma_start(
-                out=out_1[g].rearrange("p m t -> p (m t)").bitcast(I32)[:, cols],
-                in_=y_codes[:].bitcast(I32),
-            )
+                if t < len(pending):
+                    pending[t]()
+            return finish_steps(c, g, y)
 
         quantise_z(0)
         quantise_z(1)
-        score(0, 0)
+        pending = score(0, 0, [])
         quantise_z(2)
-        score(0, 1)
+        pending = score(0, 1, pending)
         for c in range(1, len(CHUNKS)):
             for g in range(GROUPS):
-                score(c, g)
+                pending = score(c, g, pending)
+        for step in pending:
+            step()
         for q in range(QUADS):
             queue = nc.sync if q % 2 == 0 else nc.scalar
             queue.dma_start(

@@ -72,14 +72,20 @@ def tile_list_schema_drift_scores_kernel(
         table_scales = held([P, T], U8, "table_scales")
         w4_plane = held([P, PASSES, H], U8, "w4_plane")
         w8_plane_raw = held([P, 1, N], U8, "w8_plane_raw")
+        nc.gpsimd.memset(w4_plane[:].bitcast(I32), 0)
         nc.vector.memset(table_scales[0:64, :].bitcast(I32), 0)
         nc.vector.memset(table_scales[64:SCALE_ROW0, :].bitcast(I32), 0)
-        nc.gpsimd.memset(w4_plane[:].bitcast(I32), 0)
         nc.gpsimd.memset(w8_plane_raw[:].bitcast(I32), 0)
+        ident = held([P, P], F32, "ident")
+        make_identity(nc, ident[:])
         v_plane = held([P, PASSES, S], U8, "v_plane")
         nc.vector.memset(v_plane[:].bitcast(I32), 0)
-        first_page = held([P, T2], F32, "first_page")
-        nc.vector.memset(first_page[:], 0.0)
+        pages = [held([P, T2], F32, "page0")]
+        nc.vector.memset(pages[0][:].bitcast(I32), 0)
+
+        def clear_page(tag):
+            pages.append(held([P, T2], F32, "page%d" % len(pages), tag=tag))
+            nc.vector.memset(pages[-1][:].bitcast(I32), 0)
 
         table = [held([P, T], U32, "table%d" % a) for a in range(PASSES)]
         w1_raw = {}
@@ -106,37 +112,45 @@ def tile_list_schema_drift_scores_kernel(
             out=table_scales[SCALE_ROW0:P, :].bitcast(I32),
             in_=tab_scales.rearrange("a r c -> r a c").bitcast(I32),
         )
-        load_scale_rows(nc.gpsimd, w4_plane, w4_scales)
+        load_scale_rows(nc.scalar, w4_plane, w4_scales)
         load_w1(0)
         load_table(0)
         load_table(1)
-        w4_codes = held([P, PASSES, 2 * H], U8, "w4_codes")
-        nc.sync.dma_start(
-            out=w4_codes[:].bitcast(I32), in_=w4_words.rearrange("a p c -> p a c").bitcast(I32)
-        )
+        w4_rows = w4_words.rearrange("a p c -> p a c")
+        w4_first = held([P, PASSES, 2 * P], U8, "w4_first")
+        w4_rest = held([P, PASSES, 2 * (H - P)], U8, "w4_rest")
+        nc.sync.dma_start(out=w4_first[:].bitcast(I32), in_=w4_rows[:, :, 0 : 2 * P].bitcast(I32))
         load_table(2)
-        load_w1(1)
+        picked_scales = held([P, S], U8, "picked_scales")
+        nc.vector.tensor_copy(out=picked_scales[:], in_=table_scales[:].indirect(picked_list[:]))
+        for q in range(QUADS):
+            nc.sync.dma_start(
+                out=v_plane[32 * q : 32 * q + 4].bitcast(I32),
+                in_=picked_scales[
+                    SCALE_ROW0 + 4 * PASSES * q : SCALE_ROW0 + 4 * PASSES * (q + 1), :
+                ].bitcast(I32),
+            )
         nc.sync.dma_start(slot_list[:], offs2)
-        gains = held([P, S], F32, "gains", tag="late")
+        gains = held([P, S], F32, "gains")
         nc.sync.dma_start(out=gains[:, 0:BANK], in_=wgs[:, 0:BANK])
-        load_w1(2)
+        load_w1(1)
+        nc.sync.dma_start(out=w4_rest[:].bitcast(I32), in_=w4_rows[:, :, 2 * P : 2 * H].bitcast(I32))
         nc.sync.dma_start(out=gains[:, BANK:S], in_=wgs[:, BANK:S])
+        load_w1(2)
         nc.sync.dma_start(pinned_list[:], offs3)
-        old_rows = [held([P, M], F32, "old%d" % b) for b in range(BLOCKS)]
-        nc.sync.dma_start(out=old_rows[0][:], in_=old[0:P, :])
         load_scale_rows(nc.sync, w8_plane_raw, w8_scales)
         w8_raw = held([P, N], I32, "w8_raw")
         nc.sync.dma_start(
             out=w8_raw[:], in_=w8_words[0].rearrange("p c i -> p (c i)").bitcast(I32)
         )
+        old_rows = [held([P, M], F32, "old%d" % b) for b in range(BLOCKS)]
+        nc.sync.dma_start(out=old_rows[0][:], in_=old[0:P, :])
         w3_raw = held([P, PACK, N], F32, "w3_raw")
         nc.sync.dma_start(out=w3_raw[:], in_=w3.rearrange("(p j) c -> p j c", j=PACK))
         for b in range(1, BLOCKS):
             nc.sync.dma_start(out=old_rows[b][:], in_=old[P * b : P * (b + 1), :])
-        ident = held([P, P], F32, "ident")
-        make_identity(nc, ident[:])
         amp_cols = held([P, GROUPS, PACK], F32, "amp_cols")
-        nc.gpsimd.dma_start(out=amp_cols[:], in_=amp.rearrange("(g p t) -> p g t", p=P, t=PACK))
+        nc.sync.dma_start(out=amp_cols[:], in_=amp.rearrange("(g p t) -> p g t", p=P, t=PACK))
 
         v_codes = [held([P, S], U32, "v_codes%d" % a) for a in range(PASSES)]
         w1_codes = [held([P, PASSES, width], U32, "w1_codes%d" % first) for first, width in W1_SPANS]
@@ -163,56 +177,63 @@ def tile_list_schema_drift_scores_kernel(
                     in_=rounded[:].rearrange("p c j -> p (c j)"),
                 )
 
-        picked_scales = held([P, S], U8, "picked_scales")
-        nc.vector.tensor_copy(out=picked_scales[:], in_=table_scales[:].indirect(picked_list[:]))
         quantise_w1(0)
-        for q in range(QUADS):
-            nc.scalar.dma_start(
-                out=v_plane[32 * q : 32 * q + 4].bitcast(I32),
-                in_=picked_scales[
-                    SCALE_ROW0 + 4 * PASSES * q : SCALE_ROW0 + 4 * PASSES * (q + 1), :
-                ].bitcast(I32),
-            )
         gather_words(0, 0, S)
         gather_words(1, 0, S)
         for half in range(HALVES):
             gather_words(2, BANK * half, BANK)
-        second_page = held([P, T2], F32, "second_page", tag="table2")
-        nc.vector.memset(second_page[:], 0.0)
-        pages = [first_page, second_page]
-        w8_codes = held([P, GROUPS, PACK, P], I32, "w8_codes")
-        w8_plane = held([P, GROUPS, PACK, P], U8, "w8_plane")
 
         sums = {}
 
-        def encode(a, b, half):
+        def encode_pass(a, b, half, old_schema, start, stop):
             cols = slice(BANK * half, BANK * (half + 1))
-            rows = slice(P * b, P * (b + 1))
-            span = min(b, len(W1_SPANS) - 1)
-            own = slice(P * b - W1_SPANS[span][0], P * (b + 1) - W1_SPANS[span][0])
+            if old_schema:
+                words = w4_first[:, a, :] if b == 0 else w4_rest[:, a, 2 * P * (b - 1) : 2 * P * b]
+                codes, plane = words.bitcast(FP4X4), w4_plane[:, a, P * b : P * (b + 1)]
+            else:
+                span = min(b, len(W1_SPANS) - 1)
+                own = slice(P * b - W1_SPANS[span][0], P * (b + 1) - W1_SPANS[span][0])
+                codes, plane = w1_codes[span][:, a, own].bitcast(FP8X4), w1_plane[span][:, a, own]
             nc.tensor.matmul_mx(
-                out=sums[b, half][:],
-                lhsT=w1_codes[span][:, a, own].bitcast(FP8X4), lhsT_scale=w1_plane[span][:, a, own],
+                out=sums[b, half][:], lhsT=codes, lhsT_scale=plane,
                 rhs=v_codes[a][:, cols].bitcast(FP8X4), rhs_scale=v_plane[:, a, cols],
-                start=(a == 0), stop=False,
-            )
-            nc.tensor.matmul_mx(
-                out=sums[b, half][:],
-                lhsT=w4_codes[:, a, 2 * P * b : 2 * P * (b + 1)].bitcast(FP4X4),
-                lhsT_scale=w4_plane[:, a, rows],
-                rhs=v_codes[a][:, cols].bitcast(FP8X4), rhs_scale=v_plane[:, a, cols],
-                start=False, stop=(a == PASSES - 1),
+                start=start, stop=stop,
             )
 
-        deltas = [held([P, S], F32, "deltas%d" % b) for b in range(BLOCKS)]
-        for b in range(BLOCKS):
-            if 0 < b < len(W1_SPANS):
-                quantise_w1(b)
+        deltas = {}
+
+        def encode_half(b, half, into):
+            sums[b, half] = bank(HALVES * b + half, [P, BANK])
+            if b == 0:
+                order = [(a, old_schema) for a in range(PASSES) for old_schema in (False, True)]
+            else:
+                order = [(a, old_schema) for old_schema in (True, False) for a in range(PASSES)]
+            for a, old_schema in order:
+                encode_pass(a, b, half, old_schema, (a, old_schema) == order[0], (a, old_schema) == order[-1])
+            nc.scalar.copy(out=into, in_=sums[b, half][:])
+
+        def scatter(b, first, count, values):
+            nc.vector.tensor_tensor(
+                out=pages[b % 2][:].indirect(entries(slot_list, first, count)),
+                in0=values, in1=gains[:, first : first + count], op=ALU.mult,
+            )
+
+        clear_page("table2")
+        for b in range(2):
+            early = held([P, BANK], F32, "early%d" % b)
+            encode_half(b, 0, early[:])
+            scatter(b, 0, BANK, early[:])
+            quantise_w1(b + 1)
+            late = held([P, BANK], F32, "late%d" % b, tag="w1_raw%d_%d" % (b + 1, PASSES - 1))
+            encode_half(b, 1, late[:])
+            scatter(b, BANK, BANK, late[:])
+
+        def encode_block(b, tag):
+            deltas[b] = held([P, S], F32, "deltas%d" % b, tag=tag)
             for half in range(HALVES):
-                sums[b, half] = bank((HALVES * b + half) % (BANKS // 2), [P, BANK])
-                for a in range(PASSES):
-                    encode(a, b, half)
-                nc.scalar.copy(out=deltas[b][:, BANK * half : BANK * (half + 1)], in_=sums[b, half][:])
+                encode_half(b, half, deltas[b][:, BANK * half : BANK * (half + 1)])
+
+        encode_block(2, "deltas2")
 
         w3_rounded = held([P, GROUPS, PACK, P, PACK], BF16, "w3_rounded")
         for g in range(GROUPS):
@@ -225,77 +246,72 @@ def tile_list_schema_drift_scores_kernel(
             held([P, width // P, 2, P, 2], BF16, "z_turned%d" % c) for c, (first, width) in enumerate(CHUNKS)
         ]
 
-        def scatter(b, first, count):
-            cols = slice(first, first + count)
-            nc.vector.tensor_tensor(
-                out=pages[b % 2][:].indirect(entries(slot_list, first, count)),
-                in0=deltas[b][:, cols], in1=gains[:, cols], op=ALU.mult,
-            )
-
-        def turn(b, c, picked):
+        def turn(c, blocks, picked, turned):
             first, width = CHUNKS[c]
             subs = width // P
-            turned = next_bank([P, subs, P])
-            for s in range(subs):
+            pieces = [(i, b, s) for i, b in enumerate(blocks) for s in range(subs)]
+            for i, b, s in pieces:
                 nc.tensor.matmul(
-                    out=turned[:, s, :], lhsT=old_rows[b][:, first + P * s : first + P * (s + 1)],
-                    rhs=ident[:], is_transpose=True, start=(s == 0), stop=False,
+                    out=turned[:, s, i, :], lhsT=old_rows[b][:, first + P * s : first + P * (s + 1)],
+                    rhs=ident[:], is_transpose=True, start=((i, s) == (0, 0)), stop=False,
                 )
-            for s in range(subs):
+            for i, b, s in pieces:
                 nc.tensor.matmul(
-                    out=turned[:, s, :], lhsT=picked[:, first + P * s : first + P * (s + 1)],
-                    rhs=ident[:], is_transpose=True, start=False, stop=(s == subs - 1),
+                    out=turned[:, s, i, :], lhsT=picked[i][:, P * s : P * (s + 1)],
+                    rhs=ident[:], is_transpose=True, start=False, stop=((i, b, s) == pieces[-1]),
                 )
             nc.scalar.copy(
-                out=z_turned[c][:, :, :, 32 * b : 32 * (b + 1), :],
-                in_=turned[:].rearrange("m s (q u e) -> m s u q e", u=2, e=2),
+                out=z_turned[c][:, :, :, 32 * blocks[0] : 32 * (blocks[-1] + 1), :],
+                in_=turned[:].rearrange("m s i (q u e) -> m s u (i q) e", u=2, e=2),
             )
 
-        def fetch_all(b):
-            picked = held([P, M], F32, "picked", bufs=2)
-            for first, width in CHUNKS if b == BLOCKS - 1 else ((0, M),):
-                nc.vector.tensor_copy(
-                    out=picked[:, first : first + width],
-                    in_=pages[b % 2][:].indirect(entries(pinned_list, first, width)),
-                )
-            for c in range(len(CHUNKS)):
-                turn(b, c, picked)
-            return picked
+        def fetch(b, first, into):
+            nc.vector.tensor_copy(
+                out=into, in_=pages[b % 2][:].indirect(entries(pinned_list, first, into.shape[1]))
+            )
 
-        for half in range(HALVES):
-            scatter(0, BANK * half, BANK)
-        nc.vector.tensor_copy(
-            out=w8_plane[:].rearrange("p g t (c i) -> p g c t i", i=16),
-            in_=w8_plane_raw[:, 0, :].rearrange("p (g c i t) -> p g c t i", g=GROUPS, i=16, t=PACK),
-        )
-        scatter(1, 0, S)
-        fetch_all(0)
+        w8_codes = held([P, GROUPS, PACK, P], I32, "w8_codes")
         nc.vector.tensor_copy(
             out=w8_codes[:].rearrange("p g t (c i) -> p g c t i", i=4),
             in_=w8_raw[:].rearrange("p (g c i t) -> p g c t i", g=GROUPS, i=4, t=PACK),
         )
-        scatter(2, 0, S)
-        fetch_all(1)
-        fetch_all(2)
-        scatter(3, 0, S)
-        fetch_all(3)
+        w8_plane = held([P, GROUPS, PACK, P], U8, "w8_plane")
+        nc.vector.tensor_copy(
+            out=w8_plane[:].rearrange("p g t (c i) -> p g c t i", i=16),
+            in_=w8_plane_raw[:, 0, :].rearrange("p (g c i t) -> p g c t i", g=GROUPS, i=16, t=PACK),
+        )
 
-        w3_codes = held([P, N], U32, "w3_codes", tag="late")
+        def fetch_block(b, tag):
+            picked = held([P, M], F32, "picked", tag=tag)
+            fetch(b, 0, picked[:])
+            for c, (first, width) in enumerate(CHUNKS):
+                turn(c, [b], [picked[:, first : first + width]], bank(c, [P, width // P, 1, P]))
+
+        encode_block(3, "w3_raw")
+        fetch_block(0, "picked0")
+        scatter(2, 0, S, deltas[2][:])
+        w3_codes = held([P, N], U32, "w3_codes", tag="w1_raw2_0")
         w3_plane = held([P, N], U8, "w3_plane")
         nc.vector.quantize_mx(
             out=w3_codes[:].bitcast(FP8X4), scales=w3_plane[:],
             in_=w3_rounded[:].rearrange("p g t m j -> p (g t m j)"),
         )
+        fetch_block(1, "picked1")
+        (first0, width0), (first1, width1), (first2, width2) = CHUNKS
+        ahead = held([P, 2, width0], F32, "ahead", tag="w1_raw2_1")
+        fetch(2, first0, ahead[:, 0, :])
+        turn(0, [2], [ahead[:, 0, :]], bank(3, [P, 2, 1, P]))
+        scatter(3, 0, S, deltas[3][:])
 
         z_codes = [held([P, width], U32, "z_codes%d" % c) for c, (first, width) in enumerate(CHUNKS)]
         z_plane = [held([P, width], U8, "z_plane%d" % c) for c, (first, width) in enumerate(CHUNKS)]
 
-        def quantise_z(c):
+        def quantise_z(c, back_banks):
             first, width = CHUNKS[c]
             z_rounded = held([P, width, PACK], BF16, "z_rounded%d" % c)
             z_words = z_rounded[:].rearrange("p m t -> p (m t)").bitcast(F32)
             for s0 in range(0, width // P, 2):
-                back = next_bank([P, 2, 2, P])
+                back = bank(back_banks[s0 // 2], [P, 2, 2, P])
                 for s in range(2):
                     for u in range(2):
                         nc.tensor.transpose(
@@ -324,7 +340,8 @@ def tile_list_schema_drift_scores_kernel(
             y_codes = held([P, width], U32, "y_codes", bufs=3)
 
             def round_y():
-                nc.vector.tensor_copy(
+                copy = nc.vector.tensor_copy
+                copy(
                     out=y_rounded[:].rearrange("p (c i) t -> p c t i", i=4),
                     in_=y[:].rearrange("p t (c i) -> p c t i", i=4),
                 )
@@ -341,47 +358,64 @@ def tile_list_schema_drift_scores_kernel(
 
             return [round_y, quantise_y]
 
+        score_banks = []
+
+        def score_bank(shape):
+            score_banks.append(shape)
+            n = len(score_banks) - 1
+            return bank(BANKS // 2 + n % (BANKS // 2), shape)
+
         def score(c, g, pending):
             first, width = CHUNKS[c]
             cols = slice(first, first + width)
-            y = held([P, PACK, width], F32, "y", tag=("table0", "table1", "w3_raw")[len(units) % 3])
+            y = held([P, PACK, width], F32, "y", tag=("table0", "table1", "v_codes2")[len(units) % 3])
             units.append((c, g))
             y_rows = out_0[K_PASS * g : K_PASS * (g + 1), cols].rearrange("(p t) m -> p t m", t=PACK)
-            for t in range(PACK):
-                n_cols = slice(K_PASS * g + P * t, K_PASS * g + P * (t + 1))
-                gain = amp_cols[:, g, t : t + 1]
-                bounded_sum = next_bank([P, width])
-                direct_sum = next_bank([P, width])
-                nc.tensor.matmul_mx(
-                    out=bounded_sum[:],
-                    lhsT=w3_codes[:, n_cols].bitcast(FP8X4), lhsT_scale=w3_plane[:, n_cols],
-                    rhs=z_codes[c][:].bitcast(FP8X4), rhs_scale=z_plane[c][:],
-                    start=True, stop=True,
-                )
-                nc.tensor.matmul_mx(
-                    out=direct_sum[:],
-                    lhsT=w8_flat[:, n_cols].bitcast(FP8X4), lhsT_scale=w8_plane_flat[:, n_cols],
-                    rhs=z_codes[c][:].bitcast(FP8X4), rhs_scale=z_plane[c][:],
-                    start=True, stop=True,
-                )
-                bounded = held([P, width], F32, "bounded", bufs=4)
+            per_bank = BANK // width
+            for t0 in range(0, PACK, per_bank):
+                bounded_sum = score_bank([P, per_bank, width])
+                direct_sum = score_bank([P, per_bank, width])
+                for sums_bank, codes, plane in (
+                    (bounded_sum, w3_codes[:], w3_plane[:]), (direct_sum, w8_flat, w8_plane_flat)
+                ):
+                    for i in range(per_bank):
+                        n_cols = slice(K_PASS * g + P * (t0 + i), K_PASS * g + P * (t0 + i + 1))
+                        nc.tensor.matmul_mx(
+                            out=sums_bank[:, i, :],
+                            lhsT=codes[:, n_cols].bitcast(FP8X4), lhsT_scale=plane[:, n_cols],
+                            rhs=z_codes[c][:].bitcast(FP8X4), rhs_scale=z_plane[c][:],
+                            start=True, stop=True,
+                        )
+                bounded = held([P, per_bank, width], F32, "bounded", bufs=4)
                 nc.scalar.activation(out=bounded[:], in_=bounded_sum[:], func=ACT.Tanh)
-                nc.scalar.activation(out=y[:, t, :], in_=direct_sum[:], func=ACT.Copy, scale=gain)
-                nc.vector.scalar_tensor_tensor(
-                    out=y[:, t, :], in0=bounded[:], scalar=gain, in1=y[:, t, :],
-                    op0=ALU.mult, op1=ALU.add,
-                )
-                if t % 2 == 1:
-                    nc.sync.dma_start(out=y_rows[:, t - 1 : t + 1, :], in_=y[:, t - 1 : t + 1, :])
-                if t < len(pending):
-                    pending[t]()
+                for t in range(t0, t0 + per_bank):
+                    gain = amp_cols[:, g, t : t + 1]
+                    nc.scalar.activation(out=y[:, t, :], in_=direct_sum[:, t - t0, :], func=ACT.Copy, scale=gain)
+                    nc.vector.scalar_tensor_tensor(
+                        out=y[:, t, :], in0=bounded[:, t - t0, :], scalar=gain, in1=y[:, t, :],
+                        op0=ALU.mult, op1=ALU.add,
+                    )
+                    if t % 2 == 1:
+                        nc.sync.dma_start(out=y_rows[:, t - 1 : t + 1, :], in_=y[:, t - 1 : t + 1, :])
+                    if t % 2 == 1:
+                        for step in pending[t // 2 : t // 2 + 1]:
+                            step()
             return finish_steps(c, g, y)
 
-        quantise_z(0)
-        quantise_z(1)
+        fetch(3, first0, ahead[:, 1, :])
+        turn(0, [3], [ahead[:, 1, :]], bank(0, [P, 2, 1, P]))
+        quantise_z(0, [1])
+        later = held([P, 2, width1 + width2], F32, "later", tag="w3_raw")
+        for i, index in enumerate((2, 0)):
+            fetch(2 + i, first1, later[:, i, 0:width1])
+            turn(1, [2 + i], [later[:, i, 0:width1]], bank(index, [P, 4, 1, P]))
+        for i in range(2):
+            fetch(2 + i, first2, later[:, i, width1:])
         pending = score(0, 0, [])
-        quantise_z(2)
+        quantise_z(1, [1, 2])
+        turn(2, [2, 3], [later[:, i, width1:] for i in range(2)], bank(0, [P, 2, 2, P]))
         pending = score(0, 1, pending)
+        quantise_z(2, [1])
         for c in range(1, len(CHUNKS)):
             for g in range(GROUPS):
                 pending = score(c, g, pending)

@@ -59,10 +59,10 @@ def tile_list_schema_drift_scores_kernel(
             return list_tile[:, first // LIST : (first + count) // LIST]
 
         def load_scale_rows(queue, plane, rows):
-            for q in range(QUADS):
+            for r in range(QUADS):
                 queue.dma_start(
-                    out=plane[32 * q : 32 * q + 4].bitcast(I32),
-                    in_=rows[:, 4 * q : 4 * q + 4, :].rearrange("a r c -> r a c").bitcast(I32),
+                    out=plane[r:P:32].bitcast(I32),
+                    in_=rows.rearrange("a (q r) c -> r q a c", r=QUADS)[r].bitcast(I32),
                 )
 
         picked_list = lists.tile([P, S // LIST], U16, name="picked_list")
@@ -108,13 +108,14 @@ def tile_list_schema_drift_scores_kernel(
                 )
 
         nc.sync.dma_start(picked_list[:], offs)
-        nc.sync.dma_start(
-            out=table_scales[SCALE_ROW0:P, :].bitcast(I32),
-            in_=tab_scales.rearrange("a r c -> r a c").bitcast(I32),
-        )
-        load_scale_rows(nc.scalar, w4_plane, w4_scales)
+        for a in range(PASSES):
+            nc.sync.dma_start(
+                out=table_scales[SCALE_ROW0 + a : P : PASSES, :].bitcast(I32),
+                in_=tab_scales[a].rearrange("(q r) c -> r q c", r=QUADS).bitcast(I32),
+            )
         load_w1(0)
         load_table(0)
+        load_scale_rows(nc.sync, w4_plane, w4_scales)
         load_table(1)
         w4_rows = w4_words.rearrange("a p c -> p a c")
         w4_first = held([P, PASSES, 2 * P], U8, "w4_first")
@@ -125,7 +126,7 @@ def tile_list_schema_drift_scores_kernel(
         nc.vector.tensor_copy(out=picked_scales[:], in_=table_scales[:].indirect(picked_list[:]))
         for q in range(QUADS):
             nc.sync.dma_start(
-                out=v_plane[32 * q : 32 * q + 4].bitcast(I32),
+                out=v_plane[q:P:32].bitcast(I32),
                 in_=picked_scales[
                     SCALE_ROW0 + 4 * PASSES * q : SCALE_ROW0 + 4 * PASSES * (q + 1), :
                 ].bitcast(I32),
@@ -179,7 +180,21 @@ def tile_list_schema_drift_scores_kernel(
 
         quantise_w1(0)
         gather_words(0, 0, S)
-        gather_words(1, 0, S)
+        gather_words(1, 0, BANK)
+        warm = bank(BANKS - 1, [P, 2 * P])
+
+        def warm_up(count, first):
+            for i in range(count):
+                nc.tensor.matmul_mx(
+                    out=warm[:], lhsT=w1_codes[0][:, 0, :].bitcast(FP8X4), lhsT_scale=w1_plane[0][:, 0, :],
+                    rhs=v_codes[1][:, first : first + 2 * P].bitcast(FP8X4),
+                    rhs_scale=w1_plane[0][:].rearrange("p a c -> p (a c)")[:, 0 : 2 * P],
+                    start=True, stop=True,
+                )
+
+        warm_up(5, 0)
+        gather_words(1, BANK, BANK)
+        warm_up(3, BANK)
         for half in range(HALVES):
             gather_words(2, BANK * half, BANK)
 
@@ -270,17 +285,6 @@ def tile_list_schema_drift_scores_kernel(
                 out=into, in_=pages[b % 2][:].indirect(entries(pinned_list, first, into.shape[1]))
             )
 
-        w8_codes = held([P, GROUPS, PACK, P], I32, "w8_codes")
-        nc.vector.tensor_copy(
-            out=w8_codes[:].rearrange("p g t (c i) -> p g c t i", i=4),
-            in_=w8_raw[:].rearrange("p (g c i t) -> p g c t i", g=GROUPS, i=4, t=PACK),
-        )
-        w8_plane = held([P, GROUPS, PACK, P], U8, "w8_plane")
-        nc.vector.tensor_copy(
-            out=w8_plane[:].rearrange("p g t (c i) -> p g c t i", i=16),
-            in_=w8_plane_raw[:, 0, :].rearrange("p (g c i t) -> p g c t i", g=GROUPS, i=16, t=PACK),
-        )
-
         def fetch_block(b, tag):
             picked = held([P, M], F32, "picked", tag=tag)
             fetch(b, 0, picked[:])
@@ -290,12 +294,6 @@ def tile_list_schema_drift_scores_kernel(
         encode_block(3, "w3_raw")
         fetch_block(0, "picked0")
         scatter(2, 0, S, deltas[2][:])
-        w3_codes = held([P, N], U32, "w3_codes", tag="w1_raw2_0")
-        w3_plane = held([P, N], U8, "w3_plane")
-        nc.vector.quantize_mx(
-            out=w3_codes[:].bitcast(FP8X4), scales=w3_plane[:],
-            in_=w3_rounded[:].rearrange("p g t m j -> p (g t m j)"),
-        )
         fetch_block(1, "picked1")
         (first0, width0), (first1, width1), (first2, width2) = CHUNKS
         ahead = held([P, 2, width0], F32, "ahead", tag="w1_raw2_1")
@@ -329,8 +327,6 @@ def tile_list_schema_drift_scores_kernel(
             )
 
         y_plane = held([P, GROUPS, M], U8, "y_plane")
-        w8_flat = w8_codes[:].rearrange("p g t m -> p (g t m)")
-        w8_plane_flat = w8_plane[:].rearrange("p g t m -> p (g t m)")
         units = []
 
         def finish_steps(c, g, y):
@@ -404,16 +400,37 @@ def tile_list_schema_drift_scores_kernel(
 
         fetch(3, first0, ahead[:, 1, :])
         turn(0, [3], [ahead[:, 1, :]], bank(0, [P, 2, 1, P]))
-        quantise_z(0, [1])
-        later = held([P, 2, width1 + width2], F32, "later", tag="w3_raw")
-        for i, index in enumerate((2, 0)):
-            fetch(2 + i, first1, later[:, i, 0:width1])
-            turn(1, [2 + i], [later[:, i, 0:width1]], bank(index, [P, 4, 1, P]))
+        later = held([P, 2, width1], F32, "later", tag="w3_raw")
         for i in range(2):
-            fetch(2 + i, first2, later[:, i, width1:])
+            fetch(2 + i, first1, later[:, i, :])
+        w3_codes = held([P, N], U32, "w3_codes", tag="gains")
+        w3_plane = held([P, N], U8, "w3_plane")
+        nc.vector.quantize_mx(
+            out=w3_codes[:].bitcast(FP8X4), scales=w3_plane[:],
+            in_=w3_rounded[:].rearrange("p g t m j -> p (g t m j)"),
+        )
+        w8_codes = held([P, GROUPS, PACK, P], I32, "w8_codes", tag="w3_rounded")
+        nc.vector.tensor_copy(
+            out=w8_codes[:].rearrange("p g t (c i) -> p g c t i", i=4),
+            in_=w8_raw[:].rearrange("p (g c i t) -> p g c t i", g=GROUPS, i=4, t=PACK),
+        )
+        w8_plane = held([P, GROUPS, PACK, P], U8, "w8_plane", tag="w8_raw")
+        nc.vector.tensor_copy(
+            out=w8_plane[:].rearrange("p g t (c i) -> p g c t i", i=16),
+            in_=w8_plane_raw[:, 0, :].rearrange("p (g c i t) -> p g c t i", g=GROUPS, i=16, t=PACK),
+        )
+
+        w8_flat = w8_codes[:].rearrange("p g t m -> p (g t m)")
+        w8_plane_flat = w8_plane[:].rearrange("p g t m -> p (g t m)")
+        quantise_z(0, [1])
+        for i, index in enumerate((2, 0)):
+            turn(1, [2 + i], [later[:, i, :]], bank(index, [P, 4, 1, P]))
+        last = held([P, 2, width2], F32, "last", tag="z_rounded0")
+        for i in range(2):
+            fetch(2 + i, first2, last[:, i, :])
         pending = score(0, 0, [])
         quantise_z(1, [1, 2])
-        turn(2, [2, 3], [later[:, i, width1:] for i in range(2)], bank(0, [P, 2, 2, P]))
+        turn(2, [2, 3], [last[:, i, :] for i in range(2)], bank(0, [P, 2, 2, P]))
         pending = score(0, 1, pending)
         quantise_z(2, [1])
         for c in range(1, len(CHUNKS)):
@@ -424,6 +441,6 @@ def tile_list_schema_drift_scores_kernel(
         for q in range(QUADS):
             queue = nc.sync if q % 2 == 0 else nc.scalar
             queue.dma_start(
-                out=out_2[:, 4 * q : 4 * q + 4, :].rearrange("g r m -> r g m").bitcast(I32),
-                in_=y_plane[32 * q : 32 * q + 4].bitcast(I32),
+                out=out_2.rearrange("g (q r) m -> r q g m", r=QUADS)[q].bitcast(I32),
+                in_=y_plane[q:P:32].bitcast(I32),
             )

@@ -80,14 +80,13 @@ def tile_list_schema_drift_scores_kernel(
         make_identity(nc, ident[:])
         v_plane = held([P, PASSES, S], U8, "v_plane")
         nc.vector.memset(v_plane[:].bitcast(I32), 0)
-        pages = [held([P, T2], F32, "page0")]
-        nc.vector.memset(pages[0][:].bitcast(I32), 0)
+        pages = []
 
         def clear_page(tag):
             pages.append(held([P, T2], F32, "page%d" % len(pages), tag=tag))
             nc.vector.memset(pages[-1][:].bitcast(I32), 0)
 
-        table = [held([P, T], U32, "table%d" % a) for a in range(PASSES)]
+        table = [held([P, T], U32, "table%d" % a) for a in range(PASSES - 1)]
         w1_raw = {}
 
         def load_table(a):
@@ -115,13 +114,12 @@ def tile_list_schema_drift_scores_kernel(
             )
         load_w1(0)
         load_table(0)
-        load_scale_rows(nc.sync, w4_plane, w4_scales)
-        load_table(1)
         w4_rows = w4_words.rearrange("a p c -> p a c")
         w4_first = held([P, PASSES, 2 * P], U8, "w4_first")
         w4_rest = held([P, PASSES, 2 * (H - P)], U8, "w4_rest")
+        load_scale_rows(nc.sync, w4_plane, w4_scales)
         nc.sync.dma_start(out=w4_first[:].bitcast(I32), in_=w4_rows[:, :, 0 : 2 * P].bitcast(I32))
-        load_table(2)
+        load_table(1)
         picked_scales = held([P, S], U8, "picked_scales")
         nc.vector.tensor_copy(out=picked_scales[:], in_=table_scales[:].indirect(picked_list[:]))
         for q in range(QUADS):
@@ -131,12 +129,14 @@ def tile_list_schema_drift_scores_kernel(
                     SCALE_ROW0 + 4 * PASSES * q : SCALE_ROW0 + 4 * PASSES * (q + 1), :
                 ].bitcast(I32),
             )
+        table.append(held([P, T], U32, "table2", tag="table_scales"))
+        load_table(2)
         nc.sync.dma_start(slot_list[:], offs2)
         gains = held([P, S], F32, "gains")
         nc.sync.dma_start(out=gains[:, 0:BANK], in_=wgs[:, 0:BANK])
         load_w1(1)
-        nc.sync.dma_start(out=w4_rest[:].bitcast(I32), in_=w4_rows[:, :, 2 * P : 2 * H].bitcast(I32))
         nc.sync.dma_start(out=gains[:, BANK:S], in_=wgs[:, BANK:S])
+        nc.sync.dma_start(out=w4_rest[:].bitcast(I32), in_=w4_rows[:, :, 2 * P : 2 * H].bitcast(I32))
         load_w1(2)
         nc.sync.dma_start(pinned_list[:], offs3)
         load_scale_rows(nc.sync, w8_plane_raw, w8_scales)
@@ -179,22 +179,10 @@ def tile_list_schema_drift_scores_kernel(
                 )
 
         quantise_w1(0)
+        clear_page("w1_raw0_0")
         gather_words(0, 0, S)
-        gather_words(1, 0, BANK)
-        warm = bank(BANKS - 1, [P, 2 * P])
-
-        def warm_up(count, first):
-            for i in range(count):
-                nc.tensor.matmul_mx(
-                    out=warm[:], lhsT=w1_codes[0][:, 0, :].bitcast(FP8X4), lhsT_scale=w1_plane[0][:, 0, :],
-                    rhs=v_codes[1][:, first : first + 2 * P].bitcast(FP8X4),
-                    rhs_scale=w1_plane[0][:].rearrange("p a c -> p (a c)")[:, 0 : 2 * P],
-                    start=True, stop=True,
-                )
-
-        warm_up(5, 0)
-        gather_words(1, BANK, BANK)
-        warm_up(3, BANK)
+        clear_page("table0")
+        gather_words(1, 0, S)
         for half in range(HALVES):
             gather_words(2, BANK * half, BANK)
 
@@ -233,7 +221,6 @@ def tile_list_schema_drift_scores_kernel(
                 in0=values, in1=gains[:, first : first + count], op=ALU.mult,
             )
 
-        clear_page("table2")
         for b in range(2):
             early = held([P, BANK], F32, "early%d" % b)
             encode_half(b, 0, early[:])
@@ -364,7 +351,7 @@ def tile_list_schema_drift_scores_kernel(
         def score(c, g, pending):
             first, width = CHUNKS[c]
             cols = slice(first, first + width)
-            y = held([P, PACK, width], F32, "y", tag=("table0", "table1", "v_codes2")[len(units) % 3])
+            y = held([P, PACK, width], F32, "y", tag=("table1", "table_scales", "v_codes2")[len(units) % 3])
             units.append((c, g))
             y_rows = out_0[K_PASS * g : K_PASS * (g + 1), cols].rearrange("(p t) m -> p t m", t=PACK)
             per_bank = BANK // width
@@ -401,19 +388,19 @@ def tile_list_schema_drift_scores_kernel(
         fetch(3, first0, ahead[:, 1, :])
         turn(0, [3], [ahead[:, 1, :]], bank(0, [P, 2, 1, P]))
         later = held([P, 2, width1], F32, "later", tag="w3_raw")
-        for i in range(2):
-            fetch(2 + i, first1, later[:, i, :])
         w3_codes = held([P, N], U32, "w3_codes", tag="gains")
         w3_plane = held([P, N], U8, "w3_plane")
         nc.vector.quantize_mx(
             out=w3_codes[:].bitcast(FP8X4), scales=w3_plane[:],
             in_=w3_rounded[:].rearrange("p g t m j -> p (g t m j)"),
         )
+        fetch(2, first1, later[:, 0, :])
         w8_codes = held([P, GROUPS, PACK, P], I32, "w8_codes", tag="w3_rounded")
         nc.vector.tensor_copy(
             out=w8_codes[:].rearrange("p g t (c i) -> p g c t i", i=4),
             in_=w8_raw[:].rearrange("p (g c i t) -> p g c t i", g=GROUPS, i=4, t=PACK),
         )
+        fetch(3, first1, later[:, 1, :])
         w8_plane = held([P, GROUPS, PACK, P], U8, "w8_plane", tag="w8_raw")
         nc.vector.tensor_copy(
             out=w8_plane[:].rearrange("p g t (c i) -> p g c t i", i=16),

@@ -323,7 +323,7 @@ def tile_list_schema_drift_scores_kernel(
             y_codes = held([P, width], U32, "y_codes", bufs=3)
 
             def round_y():
-                copy = nc.vector.tensor_copy
+                copy = nc.scalar.copy if (c, g) == (2, 0) else nc.vector.tensor_copy
                 copy(
                     out=y_rounded[:].rearrange("p (c i) t -> p c t i", i=4),
                     in_=y[:].rearrange("p t (c i) -> p c t i", i=4),
@@ -373,11 +373,18 @@ def tile_list_schema_drift_scores_kernel(
                 nc.scalar.activation(out=bounded[:], in_=bounded_sum[:], func=ACT.Tanh)
                 for t in range(t0, t0 + per_bank):
                     gain = amp_cols[:, g, t : t + 1]
-                    nc.scalar.activation(out=y[:, t, :], in_=direct_sum[:, t - t0, :], func=ACT.Copy, scale=gain)
-                    nc.vector.scalar_tensor_tensor(
-                        out=y[:, t, :], in0=bounded[:, t - t0, :], scalar=gain, in1=y[:, t, :],
-                        op0=ALU.mult, op1=ALU.add,
-                    )
+                    if t == 1 and c < 2:
+                        nc.vector.tensor_tensor(
+                            out=bounded[:, t - t0, :], in0=direct_sum[:, t - t0, :], in1=bounded[:, t - t0, :],
+                            op=ALU.add,
+                        )
+                        nc.vector.tensor_scalar_mul(y[:, t, :], bounded[:, t - t0, :], gain)
+                    else:
+                        nc.scalar.activation(out=y[:, t, :], in_=direct_sum[:, t - t0, :], func=ACT.Copy, scale=gain)
+                        nc.vector.scalar_tensor_tensor(
+                            out=y[:, t, :], in0=bounded[:, t - t0, :], scalar=gain, in1=y[:, t, :],
+                            op0=ALU.mult, op1=ALU.add,
+                        )
                     if t % 2 == 1:
                         nc.sync.dma_start(out=y_rows[:, t - 1 : t + 1, :], in_=y[:, t - 1 : t + 1, :])
                     if t % 2 == 1:
@@ -387,20 +394,19 @@ def tile_list_schema_drift_scores_kernel(
 
         fetch(3, first0, ahead[:, 1, :])
         turn(0, [3], [ahead[:, 1, :]], bank(0, [P, 2, 1, P]))
-        later = held([P, 2, width1], F32, "later", tag="w3_raw")
+        later = held([P, width1], F32, "later", tag="w3_raw")
         w3_codes = held([P, N], U32, "w3_codes", tag="gains")
         w3_plane = held([P, N], U8, "w3_plane")
         nc.vector.quantize_mx(
             out=w3_codes[:].bitcast(FP8X4), scales=w3_plane[:],
             in_=w3_rounded[:].rearrange("p g t m j -> p (g t m j)"),
         )
-        fetch(2, first1, later[:, 0, :])
+        fetch(2, first1, later[:])
         w8_codes = held([P, GROUPS, PACK, P], I32, "w8_codes", tag="w3_rounded")
         nc.vector.tensor_copy(
             out=w8_codes[:].rearrange("p g t (c i) -> p g c t i", i=4),
             in_=w8_raw[:].rearrange("p (g c i t) -> p g c t i", g=GROUPS, i=4, t=PACK),
         )
-        fetch(3, first1, later[:, 1, :])
         w8_plane = held([P, GROUPS, PACK, P], U8, "w8_plane", tag="w8_raw")
         nc.vector.tensor_copy(
             out=w8_plane[:].rearrange("p g t (c i) -> p g c t i", i=16),
@@ -410,21 +416,23 @@ def tile_list_schema_drift_scores_kernel(
         w8_flat = w8_codes[:].rearrange("p g t m -> p (g t m)")
         w8_plane_flat = w8_plane[:].rearrange("p g t m -> p (g t m)")
         quantise_z(0, [1])
-        for i, index in enumerate((2, 0)):
-            turn(1, [2 + i], [later[:, i, :]], bank(index, [P, 4, 1, P]))
-        last = held([P, 2, width2], F32, "last", tag="z_rounded0")
+        turn(1, [2], [later[:]], bank(2, [P, 4, 1, P]))
+        last = held([P, width1 + 2 * width2], F32, "last", tag="z_rounded0")
+        last_pair = [last[:, width1 + width2 * i : width1 + width2 * (i + 1)] for i in range(2)]
+        fetch(3, first1, last[:, 0:width1])
         for i in range(2):
-            fetch(2 + i, first2, last[:, i, :])
+            fetch(2 + i, first2, last_pair[i])
         pending = score(0, 0, [])
+        turn(1, [3], [last[:, 0:width1]], bank(3, [P, 4, 1, P]))
         quantise_z(1, [1, 2])
-        turn(2, [2, 3], [last[:, i, :] for i in range(2)], bank(0, [P, 2, 2, P]))
+        turn(2, [2, 3], last_pair, bank(0, [P, 2, 2, P]))
         pending = score(0, 1, pending)
         quantise_z(2, [1])
-        for c in range(1, len(CHUNKS)):
-            for g in range(GROUPS):
-                pending = score(c, g, pending)
-        for step in pending:
-            step()
+        for c, g in ((1, 0), (1, 1), (2, 0)):
+            pending = score(c, g, pending)
+        for pair in zip(score(2, 1, []), pending):
+            for step in pair:
+                step()
         for q in range(QUADS):
             queue = nc.sync if q % 2 == 0 else nc.scalar
             queue.dma_start(

@@ -30,7 +30,11 @@ LIST = 16
 BANKS = 8
 SCALE_ROW0 = P - 16 * PASSES
 W1_SPANS = ((0, 128), (128, 128), (256, 256))
-CHUNKS = ((0, 256), (256, 512), (768, 256))
+CHUNK = 256
+CHUNKS = M // CHUNK
+UNITS = ((0, 256), (256, 512), (768, 256))
+VECTOR_ROWS = {(0, 0): (1,), (0, 1): (1,), (1, 0): (1,), (1, 1): (1,), (2, 0): (), (2, 1): ()}
+SCALAR_ROUNDS = ((2, 0),)
 
 
 def tile_list_schema_drift_scores_kernel(
@@ -49,12 +53,6 @@ def tile_list_schema_drift_scores_kernel(
         def bank(index, shape):
             return psum.tile(shape, F32, name="bank%d" % index, tag="bank%d" % index)
 
-        banks_used = []
-
-        def next_bank(shape):
-            banks_used.append(shape)
-            return bank((BANKS // 2 + len(banks_used) - 1) % BANKS, shape)
-
         def entries(list_tile, first, count):
             return list_tile[:, first // LIST : (first + count) // LIST]
 
@@ -70,23 +68,21 @@ def tile_list_schema_drift_scores_kernel(
         pinned_list = lists.tile([P, M // LIST], U16, name="pinned_list")
 
         table_scales = held([P, T], U8, "table_scales")
+        v_plane = held([P, 2, S], U8, "v_plane")
+        v_plane_last = held([P, S], U8, "v_plane_last")
         w4_plane = held([P, PASSES, H], U8, "w4_plane")
         w8_plane_raw = held([P, 1, N], U8, "w8_plane_raw")
-        nc.gpsimd.memset(w4_plane[:].bitcast(I32), 0)
-        nc.vector.memset(table_scales[0:64, :].bitcast(I32), 0)
-        nc.vector.memset(table_scales[64:SCALE_ROW0, :].bitcast(I32), 0)
+        pages = [held([P, T2], F32, "page0")]
+        nc.vector.memset(table_scales[0:SCALE_ROW0, :].bitcast(I32), 0)
+        nc.vector.memset(v_plane[:].bitcast(I32), 0)
+        nc.vector.memset(pages[0][:].bitcast(I32), 0)
+        nc.vector.memset(v_plane_last[:].bitcast(I32), 0)
+        nc.vector.memset(w4_plane[:].bitcast(I32), 0)
         nc.gpsimd.memset(w8_plane_raw[:].bitcast(I32), 0)
         ident = held([P, P], F32, "ident")
         make_identity(nc, ident[:])
-        v_plane = held([P, PASSES, S], U8, "v_plane")
-        nc.vector.memset(v_plane[:].bitcast(I32), 0)
-        pages = []
 
-        def clear_page(tag):
-            pages.append(held([P, T2], F32, "page%d" % len(pages), tag=tag))
-            nc.vector.memset(pages[-1][:].bitcast(I32), 0)
-
-        table = [held([P, T], U32, "table%d" % a) for a in range(PASSES - 1)]
+        table = [held([P, T], U32, "table%d" % a) for a in range(PASSES)]
         w1_raw = {}
 
         def load_table(a):
@@ -95,235 +91,260 @@ def tile_list_schema_drift_scores_kernel(
                 in_=tab_words[a].rearrange("p t i -> p (t i)").bitcast(I32),
             )
 
-        def load_w1(span):
+        def load_w1(span, a):
             first, width = W1_SPANS[span]
-            for a in range(PASSES):
-                w1_raw[span, a] = held([P, PACK, width], F32, "w1_raw%d_%d" % (span, a))
-                nc.sync.dma_start(
-                    out=w1_raw[span, a][:],
-                    in_=w1[K_PASS * a : K_PASS * (a + 1), first : first + width].rearrange(
-                        "(p j) c -> p j c", j=PACK
-                    ),
-                )
+            w1_raw[span, a] = held([P, PACK, width], F32, "w1_raw%d_%d" % (span, a))
+            nc.sync.dma_start(
+                out=w1_raw[span, a][:],
+                in_=w1[K_PASS * a : K_PASS * (a + 1), first : first + width].rearrange("(p j) c -> p j c", j=PACK),
+            )
+
+        def round_w1(span, a, tag, bufs):
+            rounded = held([P, W1_SPANS[span][1], PACK], BF16, "w1_rounded", tag=tag, bufs=bufs)
+            nc.scalar.activation(
+                out=rounded[:].rearrange("p (c i) j -> p c j i", i=4),
+                in_=w1_raw[span, a][:].rearrange("p j (c i) -> p c j i", i=4),
+                func=ACT.Copy,
+                scale=-1.0,
+            )
+            return rounded
 
         nc.sync.dma_start(picked_list[:], offs)
+        scale_rows = [slice(P - 32 + a, P, 2) for a in range(2)] + [slice(SCALE_ROW0, P - 32)]
         for a in range(PASSES):
             nc.sync.dma_start(
-                out=table_scales[SCALE_ROW0 + a : P : PASSES, :].bitcast(I32),
+                out=table_scales[scale_rows[a], :].bitcast(I32),
                 in_=tab_scales[a].rearrange("(q r) c -> r q c", r=QUADS).bitcast(I32),
             )
-        load_w1(0)
+        load_w1(0, 0)
+        first_rounded = round_w1(0, 0, "rounded", 3)
         load_table(0)
-        w4_rows = w4_words.rearrange("a p c -> p a c")
-        w4_first = held([P, PASSES, 2 * P], U8, "w4_first")
-        w4_rest = held([P, PASSES, 2 * (H - P)], U8, "w4_rest")
-        load_scale_rows(nc.sync, w4_plane, w4_scales)
-        nc.sync.dma_start(out=w4_first[:].bitcast(I32), in_=w4_rows[:, :, 0 : 2 * P].bitcast(I32))
         load_table(1)
         picked_scales = held([P, S], U8, "picked_scales")
         nc.vector.tensor_copy(out=picked_scales[:], in_=table_scales[:].indirect(picked_list[:]))
-        for q in range(QUADS):
-            nc.sync.dma_start(
-                out=v_plane[q:P:32].bitcast(I32),
-                in_=picked_scales[
-                    SCALE_ROW0 + 4 * PASSES * q : SCALE_ROW0 + 4 * PASSES * (q + 1), :
-                ].bitcast(I32),
+        for r in range(QUADS):
+            nc.scalar.dma_start(
+                out=v_plane[r:P:32].bitcast(I32),
+                in_=picked_scales[P - 32 + 8 * r : P - 32 + 8 * (r + 1), :].bitcast(I32),
             )
-        table.append(held([P, T], U32, "table2", tag="table_scales"))
+        for r in range(QUADS):
+            nc.scalar.dma_start(
+                out=v_plane_last[r:P:32].bitcast(I32),
+                in_=picked_scales[SCALE_ROW0 + 4 * r : SCALE_ROW0 + 4 * (r + 1), :].bitcast(I32),
+            )
+        load_scale_rows(nc.scalar, w4_plane, w4_scales)
+        load_w1(0, 1)
         load_table(2)
+        load_w1(0, 2)
+        w4_rows = w4_words.rearrange("a p c -> p a c")
+        w4_first = held([P, PASSES, 2 * P], U8, "w4_first")
+        w4_rest = held([P, PASSES, 2 * (H - P)], U8, "w4_rest")
+        nc.sync.dma_start(out=w4_first[:].bitcast(I32), in_=w4_rows[:, :, 0 : 2 * P].bitcast(I32))
         nc.sync.dma_start(slot_list[:], offs2)
-        gains = held([P, S], F32, "gains")
-        nc.sync.dma_start(out=gains[:, 0:BANK], in_=wgs[:, 0:BANK])
-        load_w1(1)
-        nc.sync.dma_start(out=gains[:, BANK:S], in_=wgs[:, BANK:S])
+        gains = [held([P, BANK], F32, "gains%d" % half) for half in range(HALVES)]
+        nc.sync.dma_start(out=gains[0][:], in_=wgs[:, 0:BANK])
+        for a in range(PASSES):
+            load_w1(1, a)
         nc.sync.dma_start(out=w4_rest[:].bitcast(I32), in_=w4_rows[:, :, 2 * P : 2 * H].bitcast(I32))
-        load_w1(2)
+        nc.sync.dma_start(out=gains[1][:], in_=wgs[:, BANK:S])
         nc.sync.dma_start(pinned_list[:], offs3)
         load_scale_rows(nc.sync, w8_plane_raw, w8_scales)
         w8_raw = held([P, N], I32, "w8_raw")
-        nc.sync.dma_start(
-            out=w8_raw[:], in_=w8_words[0].rearrange("p c i -> p (c i)").bitcast(I32)
-        )
+        nc.sync.dma_start(out=w8_raw[:], in_=w8_words[0].rearrange("p c i -> p (c i)").bitcast(I32))
+        for a in range(PASSES):
+            load_w1(2, a)
+        w3_raw = [held([P, PACK, K_PASS], F32, "w3_raw%d" % g) for g in range(GROUPS)]
+        for g in range(GROUPS):
+            nc.sync.dma_start(
+                out=w3_raw[g][:],
+                in_=w3[:, K_PASS * g : K_PASS * (g + 1)].rearrange("(p j) c -> p j c", j=PACK),
+            )
         old_rows = [held([P, M], F32, "old%d" % b) for b in range(BLOCKS)]
-        nc.sync.dma_start(out=old_rows[0][:], in_=old[0:P, :])
-        w3_raw = held([P, PACK, N], F32, "w3_raw")
-        nc.sync.dma_start(out=w3_raw[:], in_=w3.rearrange("(p j) c -> p j c", j=PACK))
-        for b in range(1, BLOCKS):
+        for b in range(BLOCKS):
             nc.sync.dma_start(out=old_rows[b][:], in_=old[P * b : P * (b + 1), :])
         amp_cols = held([P, GROUPS, PACK], F32, "amp_cols")
         nc.sync.dma_start(out=amp_cols[:], in_=amp.rearrange("(g p t) -> p g t", p=P, t=PACK))
 
-        v_codes = [held([P, S], U32, "v_codes%d" % a) for a in range(PASSES)]
         w1_codes = [held([P, PASSES, width], U32, "w1_codes%d" % first) for first, width in W1_SPANS]
         w1_plane = [held([P, PASSES, width], U8, "w1_plane%d" % first) for first, width in W1_SPANS]
+        v_codes = {}
 
-        def gather_words(a, first, count):
-            nc.vector.tensor_copy(
-                out=v_codes[a][:, first : first + count],
-                in_=table[a][:].indirect(entries(picked_list, first, count)),
+        def gather_words(a, first, count, tag):
+            codes = held([P, count], U32, "v_codes", tag=tag)
+            nc.vector.tensor_copy(out=codes[:], in_=table[a][:].indirect(entries(picked_list, first, count)))
+            for half in range(first // BANK, (first + count) // BANK):
+                v_codes[a, half] = codes[:, BANK * half - first : BANK * (half + 1) - first]
+
+        def quantise_w1(span, a, rounded):
+            nc.vector.quantize_mx(
+                out=w1_codes[span][:, a, :].bitcast(FP8X4),
+                scales=w1_plane[span][:, a, :],
+                in_=rounded[:].rearrange("p c j -> p (c j)"),
             )
 
-        def quantise_w1(span):
-            for a in range(PASSES):
-                rounded = held([P, W1_SPANS[span][1], PACK], BF16, "w1_rounded", tag="rounded", bufs=3)
-                nc.scalar.activation(
-                    out=rounded[:].rearrange("p (c i) j -> p c j i", i=4),
-                    in_=w1_raw[span, a][:].rearrange("p j (c i) -> p c j i", i=4),
-                    func=ACT.Copy,
-                    scale=-1.0,
-                )
-                nc.vector.quantize_mx(
-                    out=w1_codes[span][:, a, :].bitcast(FP8X4),
-                    scales=w1_plane[span][:, a, :],
-                    in_=rounded[:].rearrange("p c j -> p (c j)"),
-                )
-
-        quantise_w1(0)
-        clear_page("w1_raw0_0")
-        gather_words(0, 0, S)
-        clear_page("table0")
-        gather_words(1, 0, S)
-        for half in range(HALVES):
-            gather_words(2, BANK * half, BANK)
-
-        sums = {}
-
-        def encode_pass(a, b, half, old_schema, start, stop):
-            cols = slice(BANK * half, BANK * (half + 1))
-            if old_schema:
-                words = w4_first[:, a, :] if b == 0 else w4_rest[:, a, 2 * P * (b - 1) : 2 * P * b]
-                codes, plane = words.bitcast(FP4X4), w4_plane[:, a, P * b : P * (b + 1)]
-            else:
-                span = min(b, len(W1_SPANS) - 1)
-                own = slice(P * b - W1_SPANS[span][0], P * (b + 1) - W1_SPANS[span][0])
-                codes, plane = w1_codes[span][:, a, own].bitcast(FP8X4), w1_plane[span][:, a, own]
-            nc.tensor.matmul_mx(
-                out=sums[b, half][:], lhsT=codes, lhsT_scale=plane,
-                rhs=v_codes[a][:, cols].bitcast(FP8X4), rhs_scale=v_plane[:, a, cols],
-                start=start, stop=stop,
-            )
+        gather_words(0, 0, S, "v_codes0")
+        quantise_w1(0, 0, first_rounded)
+        gather_words(1, 0, S, "v_codes1")
+        quantise_w1(0, 1, round_w1(0, 1, "page1", 1))
+        pages.append(held([P, T2], F32, "page1"))
+        nc.vector.memset(pages[1][:].bitcast(I32), 0)
+        gather_words(2, 0, BANK, "v_codes2_0")
+        quantise_w1(0, 2, round_w1(0, 2, "v_codes2_1", 1))
+        gather_words(2, BANK, BANK, "v_codes2_1")
 
         deltas = {}
 
-        def encode_half(b, half, into):
-            sums[b, half] = bank(HALVES * b + half, [P, BANK])
-            if b == 0:
-                order = [(a, old_schema) for a in range(PASSES) for old_schema in (False, True)]
-            else:
-                order = [(a, old_schema) for old_schema in (True, False) for a in range(PASSES)]
+        def encode(b, half, order, tag):
+            sums = bank(2 if b == 1 else half, [P, BANK])
+            cols = slice(BANK * half, BANK * (half + 1))
             for a, old_schema in order:
-                encode_pass(a, b, half, old_schema, (a, old_schema) == order[0], (a, old_schema) == order[-1])
-            nc.scalar.copy(out=into, in_=sums[b, half][:])
+                if old_schema:
+                    words = w4_first[:, a, :] if b == 0 else w4_rest[:, a, 2 * P * (b - 1) : 2 * P * b]
+                    codes, plane = words.bitcast(FP4X4), w4_plane[:, a, P * b : P * (b + 1)]
+                else:
+                    span = min(b, len(W1_SPANS) - 1)
+                    own = slice(P * b - W1_SPANS[span][0], P * (b + 1) - W1_SPANS[span][0])
+                    codes, plane = w1_codes[span][:, a, own].bitcast(FP8X4), w1_plane[span][:, a, own]
+                nc.tensor.matmul_mx(
+                    out=sums[:], lhsT=codes, lhsT_scale=plane,
+                    rhs=v_codes[a, half].bitcast(FP8X4), rhs_scale=(v_plane[:, a, cols] if a < 2 else v_plane_last[:, cols]),
+                    start=((a, old_schema) == order[0]), stop=((a, old_schema) == order[-1]),
+                )
+            deltas[b, half] = held([P, BANK], F32, "deltas", tag=tag)
+            nc.scalar.copy(out=deltas[b, half][:], in_=sums[:])
 
-        def scatter(b, first, count, values):
+        def scatter(b, half):
             nc.vector.tensor_tensor(
-                out=pages[b % 2][:].indirect(entries(slot_list, first, count)),
-                in0=values, in1=gains[:, first : first + count], op=ALU.mult,
+                out=pages[b % 2][:].indirect(entries(slot_list, BANK * half, BANK)),
+                in0=deltas[b, half][:], in1=gains[half][:], op=ALU.mult,
             )
 
-        for b in range(2):
-            early = held([P, BANK], F32, "early%d" % b)
-            encode_half(b, 0, early[:])
-            scatter(b, 0, BANK, early[:])
-            quantise_w1(b + 1)
-            late = held([P, BANK], F32, "late%d" % b, tag="w1_raw%d_%d" % (b + 1, PASSES - 1))
-            encode_half(b, 1, late[:])
-            scatter(b, BANK, BANK, late[:])
+        new_passes = [(a, False) for a in range(PASSES)]
+        old_passes = [(a, True) for a in range(PASSES)]
 
-        def encode_block(b, tag):
-            deltas[b] = held([P, S], F32, "deltas%d" % b, tag=tag)
-            for half in range(HALVES):
-                encode_half(b, half, deltas[b][:, BANK * half : BANK * (half + 1)])
+        z_turned = [held([P, CHUNK // P, 2, P, 2], BF16, "z_turned%d" % c) for c in range(CHUNKS)]
 
-        encode_block(2, "deltas2")
+        def fetch(b, first, count, tag):
+            picked = held([P, count], F32, "picked", tag=tag)
+            nc.vector.tensor_copy(out=picked[:], in_=pages[b % 2][:].indirect(entries(pinned_list, first, count)))
+            return picked
 
-        w3_rounded = held([P, GROUPS, PACK, P, PACK], BF16, "w3_rounded")
-        for g in range(GROUPS):
-            nc.scalar.copy(
-                out=w3_rounded[:, g].rearrange("p t m j -> p m t j"),
-                in_=w3_raw[:, :, K_PASS * g : K_PASS * (g + 1)].rearrange("p j (m t) -> p m t j", t=PACK),
-            )
-
-        z_turned = [
-            held([P, width // P, 2, P, 2], BF16, "z_turned%d" % c) for c, (first, width) in enumerate(CHUNKS)
-        ]
-
-        def turn(c, blocks, picked, turned):
-            first, width = CHUNKS[c]
-            subs = width // P
-            pieces = [(i, b, s) for i, b in enumerate(blocks) for s in range(subs)]
-            for i, b, s in pieces:
+        def turn_old(b, first, count, index):
+            turned = bank(index, [P, count // P, P])
+            for s in range(count // P):
                 nc.tensor.matmul(
-                    out=turned[:, s, i, :], lhsT=old_rows[b][:, first + P * s : first + P * (s + 1)],
-                    rhs=ident[:], is_transpose=True, start=((i, s) == (0, 0)), stop=False,
+                    out=turned[:, s, :], lhsT=old_rows[b][:, first + P * s : first + P * (s + 1)],
+                    rhs=ident[:], is_transpose=True, start=(s == 0), stop=False,
                 )
-            for i, b, s in pieces:
+            return turned
+
+        def turn_picked(b, first, picked, turned):
+            subs = picked.shape[1] // P
+            for s in range(subs):
                 nc.tensor.matmul(
-                    out=turned[:, s, i, :], lhsT=picked[i][:, P * s : P * (s + 1)],
-                    rhs=ident[:], is_transpose=True, start=False, stop=((i, b, s) == pieces[-1]),
+                    out=turned[:, s, :], lhsT=picked[:, P * s : P * (s + 1)],
+                    rhs=ident[:], is_transpose=True, start=False, stop=(s == subs - 1),
                 )
-            nc.scalar.copy(
-                out=z_turned[c][:, :, :, 32 * blocks[0] : 32 * (blocks[-1] + 1), :],
-                in_=turned[:].rearrange("m s i (q u e) -> m s u (i q) e", u=2, e=2),
-            )
-
-        def fetch(b, first, into):
-            nc.vector.tensor_copy(
-                out=into, in_=pages[b % 2][:].indirect(entries(pinned_list, first, into.shape[1]))
-            )
-
-        def fetch_block(b, tag):
-            picked = held([P, M], F32, "picked", tag=tag)
-            fetch(b, 0, picked[:])
-            for c, (first, width) in enumerate(CHUNKS):
-                turn(c, [b], [picked[:, first : first + width]], bank(c, [P, width // P, 1, P]))
-
-        encode_block(3, "w3_raw")
-        fetch_block(0, "picked0")
-        scatter(2, 0, S, deltas[2][:])
-        fetch_block(1, "picked1")
-        (first0, width0), (first1, width1), (first2, width2) = CHUNKS
-        ahead = held([P, 2, width0], F32, "ahead", tag="w1_raw2_1")
-        fetch(2, first0, ahead[:, 0, :])
-        turn(0, [2], [ahead[:, 0, :]], bank(3, [P, 2, 1, P]))
-        scatter(3, 0, S, deltas[3][:])
-
-        z_codes = [held([P, width], U32, "z_codes%d" % c) for c, (first, width) in enumerate(CHUNKS)]
-        z_plane = [held([P, width], U8, "z_plane%d" % c) for c, (first, width) in enumerate(CHUNKS)]
-
-        def quantise_z(c, back_banks):
-            first, width = CHUNKS[c]
-            z_rounded = held([P, width, PACK], BF16, "z_rounded%d" % c)
-            z_words = z_rounded[:].rearrange("p m t -> p (m t)").bitcast(F32)
-            for s0 in range(0, width // P, 2):
-                back = bank(back_banks[s0 // 2], [P, 2, 2, P])
-                for s in range(2):
-                    for u in range(2):
-                        nc.tensor.transpose(
-                            back[:, s, u, :],
-                            z_turned[c][:, s0 + s, u].rearrange("m p e -> m (p e)").bitcast(F32),
-                            ident[:],
-                        )
+            for s0 in range(0, subs, CHUNK // P):
                 nc.scalar.copy(
-                    out=z_words[:, 2 * P * s0 : 2 * P * (s0 + 2)].rearrange("p (s m u) -> p s m u", s=2, u=2),
-                    in_=back[:].rearrange("p s u m -> p s m u"),
+                    out=z_turned[(first + P * s0) // CHUNK][:, :, :, 32 * b : 32 * (b + 1), :],
+                    in_=turned[:, s0 : s0 + CHUNK // P, :].rearrange("m s (q u e) -> m s u q e", u=2, e=2),
                 )
+
+        def turn(b, picked):
+            for half in range(M // BANK):
+                turned = turn_old(b, BANK * half, BANK, 2 * b + half)
+                turn_picked(b, BANK * half, picked[:, BANK * half : BANK * (half + 1)], turned)
+
+        w3_rounded = [held([P, PACK, P, PACK], BF16, "w3_rounded%d" % g) for g in range(GROUPS)]
+
+        def round_w3(g):
+            nc.scalar.copy(
+                out=w3_rounded[g][:].rearrange("p t m j -> p m t j"),
+                in_=w3_raw[g][:].rearrange("p j (m t) -> p m t j", t=PACK),
+            )
+
+        encode(0, 0, new_passes[:2] + old_passes + new_passes[2:], "deltas0_0")
+        scatter(0, 0)
+        for a in range(PASSES):
+            quantise_w1(1, a, round_w1(1, a, "rounded", 3))
+        encode(0, 1, new_passes + old_passes, "w1_raw1_2")
+        scatter(0, 1)
+        encode(1, 0, old_passes + new_passes, "deltas1_0")
+        scatter(1, 0)
+        for a in range(PASSES - 1):
+            quantise_w1(2, a, round_w1(2, a, "rounded", 3))
+        quantise_w1(2, PASSES - 1, round_w1(2, PASSES - 1, "picked0", 1))
+        picked0 = fetch(0, 0, M, "picked0")
+        encode(1, 1, old_passes + new_passes, "w1_raw2_2")
+        scatter(1, 1)
+        encode(2, 0, old_passes + new_passes, "deltas2_0")
+        scatter(2, 0)
+        picked1 = fetch(1, 0, M, "deltas2_0")
+        encode(2, 1, old_passes + new_passes, "deltas0_0")
+        scatter(2, 1)
+        encode(3, 0, old_passes + new_passes, "deltas3_0")
+        scatter(3, 0)
+        picked2 = fetch(2, 0, M, "deltas3_0")
+        round_w3(0)
+        encode(3, 1, old_passes + new_passes, "w3_raw0")
+        turn(0, picked0)
+        turn(1, picked1)
+        round_w3(1)
+        last = BLOCKS - 1
+        last_turned = [turn_old(last, CHUNK * c, CHUNK, c) for c in range(CHUNKS)]
+        turn(2, picked2)
+        scatter(3, 1)
+
+        z_codes = held([P, M], U32, "z_codes")
+        z_plane = held([P, M], U8, "z_plane")
+        z_rounded = {}
+
+        def turn_back(c, index):
+            z_rounded[c] = held([P, CHUNK, PACK], BF16, "z_rounded%d" % c)
+            back = bank(index, [P, 2, 2, P])
+            for s in range(2):
+                for u in range(2):
+                    nc.tensor.transpose(
+                        back[:, s, u, :],
+                        z_turned[c][:, s, u].rearrange("m p e -> m (p e)").bitcast(F32),
+                        ident[:],
+                    )
+            nc.scalar.copy(
+                out=z_rounded[c][:].rearrange("p m t -> p (m t)").bitcast(F32).rearrange(
+                    "p (s m u) -> p s m u", s=2, u=2
+                ),
+                in_=back[:].rearrange("p s u m -> p s m u"),
+            )
+
+        def quantise_z(c):
+            cols = slice(CHUNK * c, CHUNK * (c + 1))
             nc.vector.quantize_mx(
-                out=z_codes[c][:].bitcast(FP8X4), scales=z_plane[c][:],
-                in_=z_rounded[:].rearrange("p m t -> p (m t)"),
+                out=z_codes[:, cols].bitcast(FP8X4), scales=z_plane[:, cols],
+                in_=z_rounded[c][:].rearrange("p m t -> p (m t)"),
+            )
+
+        w3_codes, w3_plane = {}, {}
+
+        def quantise_w3(g, tag):
+            w3_codes[g] = held([P, K_PASS], U32, "w3_codes", tag=tag)
+            w3_plane[g] = held([P, K_PASS], U8, "w3_plane%d" % g)
+            nc.vector.quantize_mx(
+                out=w3_codes[g][:].bitcast(FP8X4), scales=w3_plane[g][:],
+                in_=w3_rounded[g][:].rearrange("p t m j -> p (t m j)"),
             )
 
         y_plane = held([P, GROUPS, M], U8, "y_plane")
-        units = []
+        pairs_used = []
 
-        def finish_steps(c, g, y):
-            first, width = CHUNKS[c]
+        def finish_steps(unit, g, y):
+            first, width = UNITS[unit]
             cols = slice(first, first + width)
-            y_rounded = held([P, width, PACK], BF16, "y_rounded", tag="rounded", bufs=3)
+            y_rounded = held([P, width, PACK], BF16, "y_rounded", bufs=3)
             y_codes = held([P, width], U32, "y_codes", bufs=3)
 
             def round_y():
-                copy = nc.scalar.copy if (c, g) == (2, 0) else nc.vector.tensor_copy
+                copy = nc.scalar.copy if (unit, g) in SCALAR_ROUNDS else nc.vector.tensor_copy
                 copy(
                     out=y_rounded[:].rearrange("p (c i) t -> p c t i", i=4),
                     in_=y[:].rearrange("p t (c i) -> p c t i", i=4),
@@ -341,39 +362,35 @@ def tile_list_schema_drift_scores_kernel(
 
             return [round_y, quantise_y]
 
-        score_banks = []
-
-        def score_bank(shape):
-            score_banks.append(shape)
-            n = len(score_banks) - 1
-            return bank(BANKS // 2 + n % (BANKS // 2), shape)
-
-        def score(c, g, pending):
-            first, width = CHUNKS[c]
+        def score(unit, g, between):
+            first, width = UNITS[unit]
             cols = slice(first, first + width)
-            y = held([P, PACK, width], F32, "y", tag=("table1", "table_scales", "v_codes2")[len(units) % 3])
-            units.append((c, g))
+            y = held([P, PACK, width], F32, "y", tag="table%d" % ((GROUPS * unit + g) % PASSES))
             y_rows = out_0[K_PASS * g : K_PASS * (g + 1), cols].rearrange("(p t) m -> p t m", t=PACK)
             per_bank = BANK // width
             for t0 in range(0, PACK, per_bank):
-                bounded_sum = score_bank([P, per_bank, width])
-                direct_sum = score_bank([P, per_bank, width])
+                n = len(pairs_used)
+                pairs_used.append(n)
+                pair = 2 + n % 2 if n < 4 else n % 4
+                bounded_sum = bank(2 * pair, [P, per_bank, width])
+                direct_sum = bank(2 * pair + 1, [P, per_bank, width])
                 for sums_bank, codes, plane in (
-                    (bounded_sum, w3_codes[:], w3_plane[:]), (direct_sum, w8_flat, w8_plane_flat)
+                    (bounded_sum, w3_codes[g][:], w3_plane[g][:]),
+                    (direct_sum, w8_codes[:, g].rearrange("p t m -> p (t m)"), w8_plane[:, g].rearrange("p t m -> p (t m)")),
                 ):
                     for i in range(per_bank):
-                        n_cols = slice(K_PASS * g + P * (t0 + i), K_PASS * g + P * (t0 + i + 1))
+                        n_cols = slice(P * (t0 + i), P * (t0 + i + 1))
                         nc.tensor.matmul_mx(
                             out=sums_bank[:, i, :],
                             lhsT=codes[:, n_cols].bitcast(FP8X4), lhsT_scale=plane[:, n_cols],
-                            rhs=z_codes[c][:].bitcast(FP8X4), rhs_scale=z_plane[c][:],
+                            rhs=z_codes[:, cols].bitcast(FP8X4), rhs_scale=z_plane[:, cols],
                             start=True, stop=True,
                         )
                 bounded = held([P, per_bank, width], F32, "bounded", bufs=4)
                 nc.scalar.activation(out=bounded[:], in_=bounded_sum[:], func=ACT.Tanh)
                 for t in range(t0, t0 + per_bank):
                     gain = amp_cols[:, g, t : t + 1]
-                    if t == 1 and c < 2:
+                    if t in VECTOR_ROWS[unit, g]:
                         nc.vector.tensor_tensor(
                             out=bounded[:, t - t0, :], in0=direct_sum[:, t - t0, :], in1=bounded[:, t - t0, :],
                             op=ALU.add,
@@ -387,55 +404,44 @@ def tile_list_schema_drift_scores_kernel(
                         )
                     if t % 2 == 1:
                         nc.sync.dma_start(out=y_rows[:, t - 1 : t + 1, :], in_=y[:, t - 1 : t + 1, :])
-                    if t % 2 == 1:
-                        for step in pending[t // 2 : t // 2 + 1]:
+                        for step in between[t // 2]:
                             step()
-            return finish_steps(c, g, y)
+            return finish_steps(unit, g, y)
 
-        fetch(3, first0, ahead[:, 1, :])
-        turn(0, [3], [ahead[:, 1, :]], bank(0, [P, 2, 1, P]))
-        later = held([P, width1], F32, "later", tag="w3_raw")
-        w3_codes = held([P, N], U32, "w3_codes", tag="gains")
-        w3_plane = held([P, N], U8, "w3_plane")
-        nc.vector.quantize_mx(
-            out=w3_codes[:].bitcast(FP8X4), scales=w3_plane[:],
-            in_=w3_rounded[:].rearrange("p g t m j -> p (g t m j)"),
-        )
-        fetch(2, first1, later[:])
-        w8_codes = held([P, GROUPS, PACK, P], I32, "w8_codes", tag="w3_rounded")
+        turn_picked(last, 0, fetch(last, 0, CHUNK, "picked3_0")[:], last_turned[0])
+        turn_picked(last, CHUNK, fetch(last, CHUNK, CHUNK, "picked3_1")[:], last_turned[1])
+        quantise_w3(0, "gains1")
+        w8_codes = held([P, GROUPS, PACK, P], I32, "w8_codes", tag="w3_raw0")
         nc.vector.tensor_copy(
             out=w8_codes[:].rearrange("p g t (c i) -> p g c t i", i=4),
             in_=w8_raw[:].rearrange("p (g c i t) -> p g c t i", g=GROUPS, i=4, t=PACK),
         )
-        w8_plane = held([P, GROUPS, PACK, P], U8, "w8_plane", tag="w8_raw")
+        w8_plane = held([P, GROUPS, PACK, P], U8, "w8_plane", tag="gains0")
         nc.vector.tensor_copy(
             out=w8_plane[:].rearrange("p g t (c i) -> p g c t i", i=16),
             in_=w8_plane_raw[:, 0, :].rearrange("p (g c i t) -> p g c t i", g=GROUPS, i=16, t=PACK),
         )
+        turn_back(0, 0)
+        turn_back(1, 1)
+        turn_picked(last, 2 * CHUNK, fetch(last, 2 * CHUNK, CHUNK, "z_turned0")[:], last_turned[2])
+        quantise_z(0)
+        rest = fetch(last, 3 * CHUNK, CHUNK, "z_rounded0")
+        quantise_z(1)
+        quantise_w3(1, "z_rounded1")
 
-        w8_flat = w8_codes[:].rearrange("p g t m -> p (g t m)")
-        w8_plane_flat = w8_plane[:].rearrange("p g t m -> p (g t m)")
-        quantise_z(0, [1])
-        turn(1, [2], [later[:]], bank(2, [P, 4, 1, P]))
-        last = held([P, width1 + 2 * width2], F32, "last", tag="z_rounded0")
-        last_pair = [last[:, width1 + width2 * i : width1 + width2 * (i + 1)] for i in range(2)]
-        fetch(3, first1, last[:, 0:width1])
-        for i in range(2):
-            fetch(2 + i, first2, last_pair[i])
-        pending = score(0, 0, [])
-        turn(1, [3], [last[:, 0:width1]], bank(3, [P, 4, 1, P]))
-        quantise_z(1, [1, 2])
-        turn(2, [2, 3], last_pair, bank(0, [P, 2, 2, P]))
-        pending = score(0, 1, pending)
-        quantise_z(2, [1])
-        for c, g in ((1, 0), (1, 1), (2, 0)):
-            pending = score(c, g, pending)
-        for pair in zip(score(2, 1, []), pending):
+        def chunk_steps(c):
+            return [lambda: turn_back(c, c), lambda: quantise_z(c)]
+
+        round_y, quantise_y = score(0, 0, [[lambda: turn_picked(last, 3 * CHUNK, rest[:], last_turned[3])], chunk_steps(2)])
+        round_y, quantise_y = score(0, 1, [[round_y] + chunk_steps(3), [quantise_y]])
+        for unit, g in ((1, 0), (1, 1), (2, 0)):
+            round_y, quantise_y = score(unit, g, [[round_y], [quantise_y]])
+        for pair in zip(score(2, 1, [[], []]), [round_y, quantise_y]):
             for step in pair:
                 step()
-        for q in range(QUADS):
-            queue = nc.sync if q % 2 == 0 else nc.scalar
+        for r in range(QUADS):
+            queue = nc.sync if r % 2 == 0 else nc.scalar
             queue.dma_start(
-                out=out_2.rearrange("g (q r) m -> r q g m", r=QUADS)[q].bitcast(I32),
-                in_=y_plane[q:P:32].bitcast(I32),
+                out=out_2.rearrange("g (q r) m -> r q g m", r=QUADS)[r].bitcast(I32),
+                in_=y_plane[r:P:32].bitcast(I32),
             )

@@ -110,31 +110,29 @@ def tile_list_schema_drift_scores_kernel(
             return rounded
 
         nc.sync.dma_start(picked_list[:], offs)
-        scale_rows = [slice(P - 32 + a, P, 2) for a in range(2)] + [slice(SCALE_ROW0, P - 32)]
-        for a in range(PASSES):
-            nc.sync.dma_start(
-                out=table_scales[scale_rows[a], :].bitcast(I32),
-                in_=tab_scales[a].rearrange("(q r) c -> r q c", r=QUADS).bitcast(I32),
-            )
-        load_w1(0, 0)
-        first_rounded = round_w1(0, 0, "rounded", 3)
+        nc.sync.dma_start(
+            out=table_scales[P - 32 : P, :].bitcast(I32),
+            in_=tab_scales[0:2].rearrange("a k c -> k a c").bitcast(I32),
+        )
+        nc.sync.dma_start(out=table_scales[SCALE_ROW0 : P - 32, :].bitcast(I32), in_=tab_scales[2].bitcast(I32))
         load_table(0)
+        load_scale_rows(nc.scalar, w4_plane, w4_scales)
+        load_w1(0, 0)
         load_table(1)
+        load_w1(0, 1)
         picked_scales = held([P, S], U8, "picked_scales")
         nc.vector.tensor_copy(out=picked_scales[:], in_=table_scales[:].indirect(picked_list[:]))
         for r in range(QUADS):
-            nc.scalar.dma_start(
-                out=v_plane[r:P:32].bitcast(I32),
+            nc.sync.dma_start(
+                out=v_plane[32 * r : 32 * r + 4].bitcast(I32),
                 in_=picked_scales[P - 32 + 8 * r : P - 32 + 8 * (r + 1), :].bitcast(I32),
             )
+        load_table(2)
         for r in range(QUADS):
-            nc.scalar.dma_start(
-                out=v_plane_last[r:P:32].bitcast(I32),
+            nc.sync.dma_start(
+                out=v_plane_last[32 * r : 32 * r + 4].bitcast(I32),
                 in_=picked_scales[SCALE_ROW0 + 4 * r : SCALE_ROW0 + 4 * (r + 1), :].bitcast(I32),
             )
-        load_scale_rows(nc.scalar, w4_plane, w4_scales)
-        load_w1(0, 1)
-        load_table(2)
         load_w1(0, 2)
         w4_rows = w4_words.rearrange("a p c -> p a c")
         w4_first = held([P, PASSES, 2 * P], U8, "w4_first")
@@ -148,11 +146,11 @@ def tile_list_schema_drift_scores_kernel(
         nc.sync.dma_start(out=w4_rest[:].bitcast(I32), in_=w4_rows[:, :, 2 * P : 2 * H].bitcast(I32))
         nc.sync.dma_start(out=gains[1][:], in_=wgs[:, BANK:S])
         nc.sync.dma_start(pinned_list[:], offs3)
+        for a in range(PASSES):
+            load_w1(2, a)
         load_scale_rows(nc.sync, w8_plane_raw, w8_scales)
         w8_raw = held([P, N], I32, "w8_raw")
         nc.sync.dma_start(out=w8_raw[:], in_=w8_words[0].rearrange("p c i -> p (c i)").bitcast(I32))
-        for a in range(PASSES):
-            load_w1(2, a)
         w3_raw = [held([P, PACK, K_PASS], F32, "w3_raw%d" % g) for g in range(GROUPS)]
         for g in range(GROUPS):
             nc.sync.dma_start(
@@ -183,7 +181,7 @@ def tile_list_schema_drift_scores_kernel(
             )
 
         gather_words(0, 0, S, "v_codes0")
-        quantise_w1(0, 0, first_rounded)
+        quantise_w1(0, 0, round_w1(0, 0, "rounded", 3))
         gather_words(1, 0, S, "v_codes1")
         quantise_w1(0, 1, round_w1(0, 1, "page1", 1))
         pages.append(held([P, T2], F32, "page1"))
@@ -272,10 +270,10 @@ def tile_list_schema_drift_scores_kernel(
         scatter(0, 1)
         encode(1, 0, old_passes + new_passes, "deltas1_0")
         scatter(1, 0)
-        for a in range(PASSES - 1):
-            quantise_w1(2, a, round_w1(2, a, "rounded", 3))
-        quantise_w1(2, PASSES - 1, round_w1(2, PASSES - 1, "picked0", 1))
+        quantise_w1(2, 0, round_w1(2, 0, "rounded", 3))
+        quantise_w1(2, 1, round_w1(2, 1, "picked0", 1))
         picked0 = fetch(0, 0, M, "picked0")
+        quantise_w1(2, 2, round_w1(2, 2, "rounded", 3))
         encode(1, 1, old_passes + new_passes, "w1_raw2_2")
         scatter(1, 1)
         encode(2, 0, old_passes + new_passes, "deltas2_0")
@@ -434,14 +432,16 @@ def tile_list_schema_drift_scores_kernel(
 
         round_y, quantise_y = score(0, 0, [[lambda: turn_picked(last, 3 * CHUNK, rest[:], last_turned[3])], chunk_steps(2)])
         round_y, quantise_y = score(0, 1, [[round_y] + chunk_steps(3), [quantise_y]])
+        def store_scale_rows(cols, queues):
+            for r in range(QUADS):
+                queues[r % len(queues)].dma_start(
+                    out=out_2.rearrange("g (q r) m -> r q g m", r=QUADS)[r, :, :, cols].bitcast(I32),
+                    in_=y_plane[r:P:32, :, cols].bitcast(I32),
+                )
+
         for unit, g in ((1, 0), (1, 1), (2, 0)):
             round_y, quantise_y = score(unit, g, [[round_y], [quantise_y]])
         for pair in zip(score(2, 1, [[], []]), [round_y, quantise_y]):
             for step in pair:
                 step()
-        for r in range(QUADS):
-            queue = nc.sync if r % 2 == 0 else nc.scalar
-            queue.dma_start(
-                out=out_2.rearrange("g (q r) m -> r q g m", r=QUADS)[r].bitcast(I32),
-                in_=y_plane[r:P:32].bitcast(I32),
-            )
+        store_scale_rows(slice(0, M), [nc.sync, nc.scalar])

@@ -35,6 +35,7 @@ CHUNKS = M // CHUNK
 UNITS = ((0, 256), (256, 512), (768, 256))
 VECTOR_ROWS = {(0, 0): (1,), (0, 1): (1,), (1, 0): (1,), (1, 1): (1,), (2, 0): (), (2, 1): ()}
 SCALAR_ROUNDS = ((2, 0),)
+SUM_FIRST = ()
 
 
 def tile_list_schema_drift_scores_kernel(
@@ -70,15 +71,17 @@ def tile_list_schema_drift_scores_kernel(
         table_scales = held([P, T], U8, "table_scales")
         v_plane = held([P, 2, S], U8, "v_plane")
         v_plane_last = held([P, S], U8, "v_plane_last")
-        w4_plane = held([P, PASSES, H], U8, "w4_plane")
+        w4_plane_first = held([P, PASSES, P], U8, "w4_plane_first")
+        w4_plane_rest = held([P, PASSES, H - P], U8, "w4_plane_rest")
         w8_plane_raw = held([P, 1, N], U8, "w8_plane_raw")
         pages = [held([P, T2], F32, "page0")]
+        nc.vector.memset(w4_plane_first[:].bitcast(I32), 0)
         nc.vector.memset(table_scales[0:SCALE_ROW0, :].bitcast(I32), 0)
         nc.vector.memset(v_plane[:].bitcast(I32), 0)
         nc.vector.memset(pages[0][:].bitcast(I32), 0)
         nc.vector.memset(v_plane_last[:].bitcast(I32), 0)
-        nc.vector.memset(w4_plane[:].bitcast(I32), 0)
-        nc.gpsimd.memset(w8_plane_raw[:].bitcast(I32), 0)
+        nc.vector.memset(w4_plane_rest[:].bitcast(I32), 0)
+        nc.vector.memset(w8_plane_raw[:].bitcast(I32), 0)
         ident = held([P, P], F32, "ident")
         make_identity(nc, ident[:])
 
@@ -116,35 +119,36 @@ def tile_list_schema_drift_scores_kernel(
         )
         nc.sync.dma_start(out=table_scales[SCALE_ROW0 : P - 32, :].bitcast(I32), in_=tab_scales[2].bitcast(I32))
         load_table(0)
-        load_scale_rows(nc.scalar, w4_plane, w4_scales)
+        load_scale_rows(nc.scalar, w4_plane_first, w4_scales[:, :, 0:P])
         load_w1(0, 0)
         load_table(1)
         load_w1(0, 1)
         picked_scales = held([P, S], U8, "picked_scales")
         nc.vector.tensor_copy(out=picked_scales[:], in_=table_scales[:].indirect(picked_list[:]))
-        for r in range(QUADS):
+        for r in (0, 2, 1, 3):
             nc.sync.dma_start(
                 out=v_plane[32 * r : 32 * r + 4].bitcast(I32),
                 in_=picked_scales[P - 32 + 8 * r : P - 32 + 8 * (r + 1), :].bitcast(I32),
             )
         load_table(2)
-        for r in range(QUADS):
-            nc.sync.dma_start(
-                out=v_plane_last[32 * r : 32 * r + 4].bitcast(I32),
-                in_=picked_scales[SCALE_ROW0 + 4 * r : SCALE_ROW0 + 4 * (r + 1), :].bitcast(I32),
-            )
         load_w1(0, 2)
         w4_rows = w4_words.rearrange("a p c -> p a c")
         w4_first = held([P, PASSES, 2 * P], U8, "w4_first")
         w4_rest = held([P, PASSES, 2 * (H - P)], U8, "w4_rest")
         nc.sync.dma_start(out=w4_first[:].bitcast(I32), in_=w4_rows[:, :, 0 : 2 * P].bitcast(I32))
+        for r in (0, 2, 1, 3):
+            nc.sync.dma_start(
+                out=v_plane_last[32 * r : 32 * r + 4].bitcast(I32),
+                in_=picked_scales[SCALE_ROW0 + 4 * r : SCALE_ROW0 + 4 * (r + 1), :].bitcast(I32),
+            )
         nc.sync.dma_start(slot_list[:], offs2)
-        gains = [held([P, BANK], F32, "gains%d" % half) for half in range(HALVES)]
-        nc.sync.dma_start(out=gains[0][:], in_=wgs[:, 0:BANK])
+        gains = held([P, S], F32, "gains")
+        nc.sync.dma_start(out=gains[:, 0:BANK], in_=wgs[:, 0:BANK])
         for a in range(PASSES):
             load_w1(1, a)
+        nc.sync.dma_start(out=gains[:, BANK:S], in_=wgs[:, BANK:S])
         nc.sync.dma_start(out=w4_rest[:].bitcast(I32), in_=w4_rows[:, :, 2 * P : 2 * H].bitcast(I32))
-        nc.sync.dma_start(out=gains[1][:], in_=wgs[:, BANK:S])
+        load_scale_rows(nc.sync, w4_plane_rest, w4_scales[:, :, P:H])
         nc.sync.dma_start(pinned_list[:], offs3)
         for a in range(PASSES):
             load_w1(2, a)
@@ -183,22 +187,21 @@ def tile_list_schema_drift_scores_kernel(
         gather_words(0, 0, S, "v_codes0")
         quantise_w1(0, 0, round_w1(0, 0, "rounded", 3))
         gather_words(1, 0, S, "v_codes1")
-        quantise_w1(0, 1, round_w1(0, 1, "page1", 1))
-        pages.append(held([P, T2], F32, "page1"))
+        quantise_w1(0, 1, round_w1(0, 1, "rounded", 3))
+        pages.append(held([P, T2], F32, "page1", tag="w1_raw0_1"))
         nc.vector.memset(pages[1][:].bitcast(I32), 0)
         gather_words(2, 0, BANK, "v_codes2_0")
-        quantise_w1(0, 2, round_w1(0, 2, "v_codes2_1", 1))
-        gather_words(2, BANK, BANK, "v_codes2_1")
+        quantise_w1(0, 2, round_w1(0, 2, "rounded", 3))
+        gather_words(2, BANK, BANK, "w1_raw0_2")
 
-        deltas = {}
-
-        def encode(b, half, order, tag):
+        def encode(b, half, order, into):
             sums = bank(2 if b == 1 else half, [P, BANK])
             cols = slice(BANK * half, BANK * (half + 1))
             for a, old_schema in order:
                 if old_schema:
                     words = w4_first[:, a, :] if b == 0 else w4_rest[:, a, 2 * P * (b - 1) : 2 * P * b]
-                    codes, plane = words.bitcast(FP4X4), w4_plane[:, a, P * b : P * (b + 1)]
+                    plane = w4_plane_first[:, a, :] if b == 0 else w4_plane_rest[:, a, P * (b - 1) : P * b]
+                    codes = words.bitcast(FP4X4)
                 else:
                     span = min(b, len(W1_SPANS) - 1)
                     own = slice(P * b - W1_SPANS[span][0], P * (b + 1) - W1_SPANS[span][0])
@@ -208,14 +211,25 @@ def tile_list_schema_drift_scores_kernel(
                     rhs=v_codes[a, half].bitcast(FP8X4), rhs_scale=(v_plane[:, a, cols] if a < 2 else v_plane_last[:, cols]),
                     start=((a, old_schema) == order[0]), stop=((a, old_schema) == order[-1]),
                 )
-            deltas[b, half] = held([P, BANK], F32, "deltas", tag=tag)
-            nc.scalar.copy(out=deltas[b, half][:], in_=sums[:])
+            nc.scalar.copy(out=into, in_=sums[:])
 
-        def scatter(b, half):
+        def scatter(b, first, deltas):
+            count = deltas.shape[1]
             nc.vector.tensor_tensor(
-                out=pages[b % 2][:].indirect(entries(slot_list, BANK * half, BANK)),
-                in0=deltas[b, half][:], in1=gains[half][:], op=ALU.mult,
+                out=pages[b % 2][:].indirect(entries(slot_list, first, count)),
+                in0=deltas, in1=gains[:, first : first + count], op=ALU.mult,
             )
+
+        def put_half(b, half, order, tag):
+            deltas = held([P, BANK], F32, "deltas", tag=tag)
+            encode(b, half, order, deltas[:])
+            scatter(b, BANK * half, deltas[:])
+
+        def encode_block(b, tag):
+            deltas = held([P, S], F32, "deltas", tag=tag)
+            for half in range(HALVES):
+                encode(b, half, old_passes + new_passes, deltas[:, BANK * half : BANK * (half + 1)])
+            return deltas
 
         new_passes = [(a, False) for a in range(PASSES)]
         old_passes = [(a, True) for a in range(PASSES)]
@@ -262,37 +276,30 @@ def tile_list_schema_drift_scores_kernel(
                 in_=w3_raw[g][:].rearrange("p j (m t) -> p m t j", t=PACK),
             )
 
-        encode(0, 0, new_passes[:2] + old_passes + new_passes[2:], "deltas0_0")
-        scatter(0, 0)
+        put_half(0, 0, new_passes[:2] + old_passes + new_passes[2:], "deltas0_0")
         for a in range(PASSES):
             quantise_w1(1, a, round_w1(1, a, "rounded", 3))
-        encode(0, 1, new_passes + old_passes, "w1_raw1_2")
-        scatter(0, 1)
-        encode(1, 0, old_passes + new_passes, "deltas1_0")
-        scatter(1, 0)
+        put_half(0, 1, new_passes + old_passes, "w1_raw1_2")
+        put_half(1, 0, old_passes + new_passes, "deltas1_0")
         quantise_w1(2, 0, round_w1(2, 0, "rounded", 3))
-        quantise_w1(2, 1, round_w1(2, 1, "picked0", 1))
-        picked0 = fetch(0, 0, M, "picked0")
+        put_half(1, 1, old_passes + new_passes, "w1_raw2_0")
+        quantise_w1(2, 1, round_w1(2, 1, "rounded", 3))
+        picked0 = fetch(0, 0, M, "w1_raw2_1")
         quantise_w1(2, 2, round_w1(2, 2, "rounded", 3))
-        encode(1, 1, old_passes + new_passes, "w1_raw2_2")
-        scatter(1, 1)
-        encode(2, 0, old_passes + new_passes, "deltas2_0")
-        scatter(2, 0)
-        picked1 = fetch(1, 0, M, "deltas2_0")
-        encode(2, 1, old_passes + new_passes, "deltas0_0")
-        scatter(2, 1)
-        encode(3, 0, old_passes + new_passes, "deltas3_0")
-        scatter(3, 0)
-        picked2 = fetch(2, 0, M, "deltas3_0")
+        picked1 = fetch(1, 0, M, "w1_raw2_2")
+        scatter(2, 0, encode_block(2, "deltas2")[:])
+        put_half(3, 0, old_passes + new_passes, "deltas0_0")
+        picked2 = fetch(2, 0, M, "picked2")
         round_w3(0)
-        encode(3, 1, old_passes + new_passes, "w3_raw0")
+        last_deltas = held([P, BANK], F32, "deltas", tag="w3_raw0")
+        encode(3, 1, old_passes + new_passes, last_deltas[:])
         turn(0, picked0)
         turn(1, picked1)
         round_w3(1)
         last = BLOCKS - 1
         last_turned = [turn_old(last, CHUNK * c, CHUNK, c) for c in range(CHUNKS)]
         turn(2, picked2)
-        scatter(3, 1)
+        scatter(3, BANK, last_deltas[:])
 
         z_codes = held([P, M], U32, "z_codes")
         z_plane = held([P, M], U8, "z_plane")
@@ -386,35 +393,48 @@ def tile_list_schema_drift_scores_kernel(
                         )
                 bounded = held([P, per_bank, width], F32, "bounded", bufs=4)
                 nc.scalar.activation(out=bounded[:], in_=bounded_sum[:], func=ACT.Tanh)
-                for t in range(t0, t0 + per_bank):
-                    gain = amp_cols[:, g, t : t + 1]
+                rows = range(t0, t0 + per_bank)
+                if (unit, g) in SUM_FIRST:
+                    nc.vector.tensor_tensor(out=bounded[:], in0=direct_sum[:], in1=bounded[:], op=ALU.add)
+                    for t in rows:
+                        if t not in VECTOR_ROWS[unit, g]:
+                            nc.scalar.activation(
+                                out=y[:, t, :], in_=bounded[:, t - t0, :], func=ACT.Copy, scale=amp_cols[:, g, t : t + 1]
+                            )
+                else:
+                    for t in rows:
+                        if t in VECTOR_ROWS[unit, g]:
+                            nc.vector.tensor_tensor(
+                                out=bounded[:, t - t0, :], in0=direct_sum[:, t - t0, :], in1=bounded[:, t - t0, :],
+                                op=ALU.add,
+                            )
+                    for t in rows:
+                        gain = amp_cols[:, g, t : t + 1]
+                        if t not in VECTOR_ROWS[unit, g]:
+                            nc.scalar.activation(out=y[:, t, :], in_=direct_sum[:, t - t0, :], func=ACT.Copy, scale=gain)
+                            nc.vector.scalar_tensor_tensor(
+                                out=y[:, t, :], in0=bounded[:, t - t0, :], scalar=gain, in1=y[:, t, :],
+                                op0=ALU.mult, op1=ALU.add,
+                            )
+                if rows[-1] % 2 == 1:
+                    for step in between[rows[-1] // 2]:
+                        step()
+                for t in rows:
                     if t in VECTOR_ROWS[unit, g]:
-                        nc.vector.tensor_tensor(
-                            out=bounded[:, t - t0, :], in0=direct_sum[:, t - t0, :], in1=bounded[:, t - t0, :],
-                            op=ALU.add,
-                        )
-                        nc.vector.tensor_scalar_mul(y[:, t, :], bounded[:, t - t0, :], gain)
-                    else:
-                        nc.scalar.activation(out=y[:, t, :], in_=direct_sum[:, t - t0, :], func=ACT.Copy, scale=gain)
-                        nc.vector.scalar_tensor_tensor(
-                            out=y[:, t, :], in0=bounded[:, t - t0, :], scalar=gain, in1=y[:, t, :],
-                            op0=ALU.mult, op1=ALU.add,
-                        )
-                    if t % 2 == 1:
-                        nc.sync.dma_start(out=y_rows[:, t - 1 : t + 1, :], in_=y[:, t - 1 : t + 1, :])
-                        for step in between[t // 2]:
-                            step()
+                        nc.vector.tensor_scalar_mul(y[:, t, :], bounded[:, t - t0, :], amp_cols[:, g, t : t + 1])
+                if rows[-1] % 2 == 1:
+                    nc.sync.dma_start(out=y_rows[:, rows[-1] - 1 : rows[-1] + 1, :], in_=y[:, rows[-1] - 1 : rows[-1] + 1, :])
             return finish_steps(unit, g, y)
 
         turn_picked(last, 0, fetch(last, 0, CHUNK, "picked3_0")[:], last_turned[0])
         turn_picked(last, CHUNK, fetch(last, CHUNK, CHUNK, "picked3_1")[:], last_turned[1])
-        quantise_w3(0, "gains1")
+        quantise_w3(0, "gains")
         w8_codes = held([P, GROUPS, PACK, P], I32, "w8_codes", tag="w3_raw0")
         nc.vector.tensor_copy(
             out=w8_codes[:].rearrange("p g t (c i) -> p g c t i", i=4),
             in_=w8_raw[:].rearrange("p (g c i t) -> p g c t i", g=GROUPS, i=4, t=PACK),
         )
-        w8_plane = held([P, GROUPS, PACK, P], U8, "w8_plane", tag="gains0")
+        w8_plane = held([P, GROUPS, PACK, P], U8, "w8_plane", tag="w8_raw")
         nc.vector.tensor_copy(
             out=w8_plane[:].rearrange("p g t (c i) -> p g c t i", i=16),
             in_=w8_plane_raw[:, 0, :].rearrange("p (g c i t) -> p g c t i", g=GROUPS, i=16, t=PACK),

@@ -72,16 +72,12 @@ def tile_list_schema_drift_scores_kernel(
         v_plane = held([P, 2, S], U8, "v_plane")
         v_plane_last = held([P, S], U8, "v_plane_last")
         w4_plane_first = held([P, PASSES, P], U8, "w4_plane_first")
-        w4_plane_rest = held([P, PASSES, H - P], U8, "w4_plane_rest")
-        w8_plane_raw = held([P, 1, N], U8, "w8_plane_raw")
         pages = [held([P, T2], F32, "page0")]
         nc.vector.memset(w4_plane_first[:].bitcast(I32), 0)
         nc.vector.memset(table_scales[0:SCALE_ROW0, :].bitcast(I32), 0)
         nc.vector.memset(v_plane[:].bitcast(I32), 0)
         nc.vector.memset(pages[0][:].bitcast(I32), 0)
         nc.vector.memset(v_plane_last[:].bitcast(I32), 0)
-        nc.vector.memset(w4_plane_rest[:].bitcast(I32), 0)
-        nc.vector.memset(w8_plane_raw[:].bitcast(I32), 0)
         ident = held([P, P], F32, "ident")
         make_identity(nc, ident[:])
 
@@ -146,26 +142,6 @@ def tile_list_schema_drift_scores_kernel(
         nc.sync.dma_start(out=gains[:, 0:BANK], in_=wgs[:, 0:BANK])
         for a in range(PASSES):
             load_w1(1, a)
-        nc.sync.dma_start(out=gains[:, BANK:S], in_=wgs[:, BANK:S])
-        nc.sync.dma_start(out=w4_rest[:].bitcast(I32), in_=w4_rows[:, :, 2 * P : 2 * H].bitcast(I32))
-        load_scale_rows(nc.sync, w4_plane_rest, w4_scales[:, :, P:H])
-        nc.sync.dma_start(pinned_list[:], offs3)
-        for a in range(PASSES):
-            load_w1(2, a)
-        load_scale_rows(nc.sync, w8_plane_raw, w8_scales)
-        w8_raw = held([P, N], I32, "w8_raw")
-        nc.sync.dma_start(out=w8_raw[:], in_=w8_words[0].rearrange("p c i -> p (c i)").bitcast(I32))
-        w3_raw = [held([P, PACK, K_PASS], F32, "w3_raw%d" % g) for g in range(GROUPS)]
-        for g in range(GROUPS):
-            nc.sync.dma_start(
-                out=w3_raw[g][:],
-                in_=w3[:, K_PASS * g : K_PASS * (g + 1)].rearrange("(p j) c -> p j c", j=PACK),
-            )
-        old_rows = [held([P, M], F32, "old%d" % b) for b in range(BLOCKS)]
-        for b in range(BLOCKS):
-            nc.sync.dma_start(out=old_rows[b][:], in_=old[P * b : P * (b + 1), :])
-        amp_cols = held([P, GROUPS, PACK], F32, "amp_cols")
-        nc.sync.dma_start(out=amp_cols[:], in_=amp.rearrange("(g p t) -> p g t", p=P, t=PACK))
 
         w1_codes = [held([P, PASSES, width], U32, "w1_codes%d" % first) for first, width in W1_SPANS]
         w1_plane = [held([P, PASSES, width], U8, "w1_plane%d" % first) for first, width in W1_SPANS]
@@ -193,6 +169,31 @@ def tile_list_schema_drift_scores_kernel(
         gather_words(2, 0, BANK, "v_codes2_0")
         quantise_w1(0, 2, round_w1(0, 2, "rounded", 3))
         gather_words(2, BANK, BANK, "w1_raw0_2")
+        late_planes = held([P, PASSES * (H - P) + N], U8, "late_planes", tag="table2")
+        nc.vector.memset(late_planes[:].bitcast(I32), 0)
+        w4_plane_rest = late_planes[:, 0 : PASSES * (H - P)].rearrange("p (a c) -> p a c", a=PASSES)
+        w8_plane_raw = late_planes[:, PASSES * (H - P) :].rearrange("p (a c) -> p a c", a=1)
+        nc.sync.dma_start(out=w4_rest[:].bitcast(I32), in_=w4_rows[:, :, 2 * P : 2 * H].bitcast(I32))
+        load_scale_rows(nc.sync, w4_plane_rest, w4_scales[:, :, P:H])
+        nc.sync.dma_start(out=gains[:, BANK:S], in_=wgs[:, BANK:S])
+        nc.sync.dma_start(pinned_list[:], offs3)
+        for a in range(PASSES):
+            load_w1(2, a)
+        load_scale_rows(nc.sync, w8_plane_raw, w8_scales)
+        w8_raw = held([P, N], I32, "w8_raw")
+        nc.sync.dma_start(out=w8_raw[:], in_=w8_words[0].rearrange("p c i -> p (c i)").bitcast(I32))
+        w3_raw = [held([P, PACK, K_PASS], F32, "w3_raw%d" % g) for g in range(GROUPS)]
+        for g in range(GROUPS):
+            nc.sync.dma_start(
+                out=w3_raw[g][:],
+                in_=w3[:, K_PASS * g : K_PASS * (g + 1)].rearrange("(p j) c -> p j c", j=PACK),
+            )
+        old_rows = [held([P, M], F32, "old%d" % b) for b in range(BLOCKS)]
+        for b in range(BLOCKS):
+            nc.sync.dma_start(out=old_rows[b][:], in_=old[P * b : P * (b + 1), :])
+        amp_cols = held([P, GROUPS, PACK], F32, "amp_cols")
+        nc.sync.dma_start(out=amp_cols[:], in_=amp.rearrange("(g p t) -> p g t", p=P, t=PACK))
+
 
         def encode(b, half, order, into):
             sums = bank(2 if b == 1 else half, [P, BANK])
@@ -452,11 +453,11 @@ def tile_list_schema_drift_scores_kernel(
 
         round_y, quantise_y = score(0, 0, [[lambda: turn_picked(last, 3 * CHUNK, rest[:], last_turned[3])], chunk_steps(2)])
         round_y, quantise_y = score(0, 1, [[round_y] + chunk_steps(3), [quantise_y]])
-        def store_scale_rows(cols, queues):
+        def store_scale_rows(plane, cols, queues):
             for r in range(QUADS):
                 queues[r % len(queues)].dma_start(
                     out=out_2.rearrange("g (q r) m -> r q g m", r=QUADS)[r, :, :, cols].bitcast(I32),
-                    in_=y_plane[r:P:32, :, cols].bitcast(I32),
+                    in_=plane[r:P:32].bitcast(I32),
                 )
 
         for unit, g in ((1, 0), (1, 1), (2, 0)):
@@ -464,4 +465,4 @@ def tile_list_schema_drift_scores_kernel(
         for pair in zip(score(2, 1, [[], []]), [round_y, quantise_y]):
             for step in pair:
                 step()
-        store_scale_rows(slice(0, M), [nc.sync, nc.scalar])
+        store_scale_rows(y_plane, slice(0, M), [nc.sync, nc.scalar])

@@ -27,15 +27,11 @@ BANK = 512
 HALVES = S // BANK
 QUADS = 4
 LIST = 16
-BANKS = 8
 SCALE_ROW0 = P - 16 * PASSES
 W1_SPANS = ((0, 128), (128, 128), (256, 256))
 CHUNK = 256
 CHUNKS = M // CHUNK
-UNITS = ((0, 256), (256, 512), (768, 256))
-VECTOR_ROWS = {(0, 0): (1,), (0, 1): (1,), (1, 0): (1,), (1, 1): (1,), (2, 0): (), (2, 1): ()}
-SCALAR_ROUNDS = ((2, 0),)
-SUM_FIRST = ()
+GPSIMD_ROWS = 10
 
 
 def tile_list_schema_drift_scores_kernel(
@@ -180,8 +176,8 @@ def tile_list_schema_drift_scores_kernel(
         for a in range(PASSES):
             load_w1(2, a)
         load_scale_rows(nc.sync, w8_plane_raw, w8_scales)
-        w8_raw = held([P, N], I32, "w8_raw")
-        nc.sync.dma_start(out=w8_raw[:], in_=w8_words[0].rearrange("p c i -> p (c i)").bitcast(I32))
+        w8_raw = held([P, N], U32, "w8_raw")
+        nc.sync.dma_start(out=w8_raw[:].bitcast(I32), in_=w8_words[0].rearrange("p c i -> p (c i)").bitcast(I32))
         w3_raw = [held([P, PACK, K_PASS], F32, "w3_raw%d" % g) for g in range(GROUPS)]
         for g in range(GROUPS):
             nc.sync.dma_start(
@@ -294,6 +290,11 @@ def tile_list_schema_drift_scores_kernel(
         round_w3(0)
         last_deltas = held([P, BANK], F32, "deltas", tag="w3_raw0")
         encode(3, 1, old_passes + new_passes, last_deltas[:])
+        w8_codes = held([P, GROUPS, PACK, P], U32, "w8_codes", tag="w1_raw0_2")
+        nc.scalar.copy(
+            out=w8_codes[:].rearrange("p g t (c i) -> p g c t i", i=4),
+            in_=w8_raw[:].rearrange("p (g c i t) -> p g c t i", g=GROUPS, i=4, t=PACK),
+        )
         turn(0, picked0)
         turn(1, picked1)
         round_w3(1)
@@ -304,11 +305,10 @@ def tile_list_schema_drift_scores_kernel(
 
         z_codes = held([P, M], U32, "z_codes")
         z_plane = held([P, M], U8, "z_plane")
-        z_rounded = {}
+        z_rounded = [held([P, BANK, PACK], BF16, "z_rounded%d" % half) for half in range(M // BANK)]
 
-        def turn_back(c, index):
-            z_rounded[c] = held([P, CHUNK, PACK], BF16, "z_rounded%d" % c)
-            back = bank(index, [P, 2, 2, P])
+        def turn_back(c):
+            back = bank(c, [P, 2, 2, P])
             for s in range(2):
                 for u in range(2):
                     nc.tensor.transpose(
@@ -316,18 +316,17 @@ def tile_list_schema_drift_scores_kernel(
                         z_turned[c][:, s, u].rearrange("m p e -> m (p e)").bitcast(F32),
                         ident[:],
                     )
+            words = z_rounded[c // 2][:].rearrange("p m t -> p (m t)").bitcast(F32)
             nc.scalar.copy(
-                out=z_rounded[c][:].rearrange("p m t -> p (m t)").bitcast(F32).rearrange(
-                    "p (s m u) -> p s m u", s=2, u=2
-                ),
+                out=words[:, 2 * CHUNK * (c % 2) : 2 * CHUNK * (c % 2 + 1)].rearrange("p (s m u) -> p s m u", s=2, u=2),
                 in_=back[:].rearrange("p s u m -> p s m u"),
             )
 
-        def quantise_z(c):
-            cols = slice(CHUNK * c, CHUNK * (c + 1))
+        def quantise_z(half):
+            cols = slice(BANK * half, BANK * (half + 1))
             nc.vector.quantize_mx(
                 out=z_codes[:, cols].bitcast(FP8X4), scales=z_plane[:, cols],
-                in_=z_rounded[c][:].rearrange("p m t -> p (m t)"),
+                in_=z_rounded[half][:].rearrange("p m t -> p (m t)"),
             )
 
         w3_codes, w3_plane = {}, {}
@@ -340,129 +339,98 @@ def tile_list_schema_drift_scores_kernel(
                 in_=w3_rounded[g][:].rearrange("p t m j -> p (t m j)"),
             )
 
-        y_plane = held([P, GROUPS, M], U8, "y_plane")
-        pairs_used = []
-
-        def finish_steps(unit, g, y):
-            first, width = UNITS[unit]
-            cols = slice(first, first + width)
-            y_rounded = held([P, width, PACK], BF16, "y_rounded", bufs=3)
-            y_codes = held([P, width], U32, "y_codes", bufs=3)
-
-            def round_y():
-                copy = nc.scalar.copy if (unit, g) in SCALAR_ROUNDS else nc.vector.tensor_copy
-                copy(
-                    out=y_rounded[:].rearrange("p (c i) t -> p c t i", i=4),
-                    in_=y[:].rearrange("p t (c i) -> p c t i", i=4),
-                )
-
-            def quantise_y():
-                nc.vector.quantize_mx(
-                    out=y_codes[:].bitcast(FP8X4), scales=y_plane[:, g, cols],
-                    in_=y_rounded[:].rearrange("p m t -> p (m t)"),
-                )
-                nc.sync.dma_start(
-                    out=out_1[g].rearrange("p m t -> p (m t)").bitcast(I32)[:, cols],
-                    in_=y_codes[:].bitcast(I32),
-                )
-
-            return [round_y, quantise_y]
-
-        def score(unit, g, between):
-            first, width = UNITS[unit]
-            cols = slice(first, first + width)
-            y = held([P, PACK, width], F32, "y", tag="table%d" % ((GROUPS * unit + g) % PASSES))
-            y_rows = out_0[K_PASS * g : K_PASS * (g + 1), cols].rearrange("(p t) m -> p t m", t=PACK)
-            per_bank = BANK // width
-            for t0 in range(0, PACK, per_bank):
-                n = len(pairs_used)
-                pairs_used.append(n)
-                pair = 2 + n % 2 if n < 4 else n % 4
-                bounded_sum = bank(2 * pair, [P, per_bank, width])
-                direct_sum = bank(2 * pair + 1, [P, per_bank, width])
-                for sums_bank, codes, plane in (
-                    (bounded_sum, w3_codes[g][:], w3_plane[g][:]),
-                    (direct_sum, w8_codes[:, g].rearrange("p t m -> p (t m)"), w8_plane[:, g].rearrange("p t m -> p (t m)")),
-                ):
-                    for i in range(per_bank):
-                        n_cols = slice(P * (t0 + i), P * (t0 + i + 1))
-                        nc.tensor.matmul_mx(
-                            out=sums_bank[:, i, :],
-                            lhsT=codes[:, n_cols].bitcast(FP8X4), lhsT_scale=plane[:, n_cols],
-                            rhs=z_codes[:, cols].bitcast(FP8X4), rhs_scale=z_plane[:, cols],
-                            start=True, stop=True,
-                        )
-                bounded = held([P, per_bank, width], F32, "bounded", bufs=4)
-                nc.scalar.activation(out=bounded[:], in_=bounded_sum[:], func=ACT.Tanh)
-                rows = range(t0, t0 + per_bank)
-                if (unit, g) in SUM_FIRST:
-                    nc.vector.tensor_tensor(out=bounded[:], in0=direct_sum[:], in1=bounded[:], op=ALU.add)
-                    for t in rows:
-                        if t not in VECTOR_ROWS[unit, g]:
-                            nc.scalar.activation(
-                                out=y[:, t, :], in_=bounded[:, t - t0, :], func=ACT.Copy, scale=amp_cols[:, g, t : t + 1]
-                            )
-                else:
-                    for t in rows:
-                        if t in VECTOR_ROWS[unit, g]:
-                            nc.vector.tensor_tensor(
-                                out=bounded[:, t - t0, :], in0=direct_sum[:, t - t0, :], in1=bounded[:, t - t0, :],
-                                op=ALU.add,
-                            )
-                    for t in rows:
-                        gain = amp_cols[:, g, t : t + 1]
-                        if t not in VECTOR_ROWS[unit, g]:
-                            nc.scalar.activation(out=y[:, t, :], in_=direct_sum[:, t - t0, :], func=ACT.Copy, scale=gain)
-                            nc.vector.scalar_tensor_tensor(
-                                out=y[:, t, :], in0=bounded[:, t - t0, :], scalar=gain, in1=y[:, t, :],
-                                op0=ALU.mult, op1=ALU.add,
-                            )
-                if rows[-1] % 2 == 1:
-                    for step in between[rows[-1] // 2]:
-                        step()
-                for t in rows:
-                    if t in VECTOR_ROWS[unit, g]:
-                        nc.vector.tensor_scalar_mul(y[:, t, :], bounded[:, t - t0, :], amp_cols[:, g, t : t + 1])
-                if rows[-1] % 2 == 1:
-                    nc.sync.dma_start(out=y_rows[:, rows[-1] - 1 : rows[-1] + 1, :], in_=y[:, rows[-1] - 1 : rows[-1] + 1, :])
-            return finish_steps(unit, g, y)
-
-        turn_picked(last, 0, fetch(last, 0, CHUNK, "picked3_0")[:], last_turned[0])
-        turn_picked(last, CHUNK, fetch(last, CHUNK, CHUNK, "picked3_1")[:], last_turned[1])
+        for c in range(CHUNKS):
+            turn_picked(last, CHUNK * c, fetch(last, CHUNK * c, CHUNK, "picked3_%d" % c)[:], last_turned[c])
+            if c > 0:
+                turn_back(c - 1)
         quantise_w3(0, "gains")
-        w8_codes = held([P, GROUPS, PACK, P], I32, "w8_codes", tag="w3_raw0")
-        nc.vector.tensor_copy(
-            out=w8_codes[:].rearrange("p g t (c i) -> p g c t i", i=4),
-            in_=w8_raw[:].rearrange("p (g c i t) -> p g c t i", g=GROUPS, i=4, t=PACK),
-        )
         w8_plane = held([P, GROUPS, PACK, P], U8, "w8_plane", tag="w8_raw")
         nc.vector.tensor_copy(
             out=w8_plane[:].rearrange("p g t (c i) -> p g c t i", i=16),
             in_=w8_plane_raw[:, 0, :].rearrange("p (g c i t) -> p g c t i", g=GROUPS, i=16, t=PACK),
         )
-        turn_back(0, 0)
-        turn_back(1, 1)
-        turn_picked(last, 2 * CHUNK, fetch(last, 2 * CHUNK, CHUNK, "z_turned0")[:], last_turned[2])
         quantise_z(0)
-        rest = fetch(last, 3 * CHUNK, CHUNK, "z_rounded0")
+        turn_back(CHUNKS - 1)
+        quantise_w3(1, "z_rounded0")
         quantise_z(1)
-        quantise_w3(1, "z_rounded1")
 
-        def chunk_steps(c):
-            return [lambda: turn_back(c, c), lambda: quantise_z(c)]
+        units = [(half, g) for half in range(M // BANK) for g in range(GROUPS)]
+        y_tags = ["table0", "table1", "table2", "page0"]
+        y = [held([P, PACK, BANK], F32, "y", tag=tag) for tag in y_tags]
+        last_bounded = held([P, BANK], F32, "last_bounded")
+        rows = [(unit, t) for unit in range(len(units)) for t in range(PACK)]
 
-        round_y, quantise_y = score(0, 0, [[lambda: turn_picked(last, 3 * CHUNK, rest[:], last_turned[3])], chunk_steps(2)])
-        round_y, quantise_y = score(0, 1, [[round_y] + chunk_steps(3), [quantise_y]])
-        def store_scale_rows(plane, cols, queues):
-            for r in range(QUADS):
-                queues[r % len(queues)].dma_start(
-                    out=out_2.rearrange("g (q r) m -> r q g m", r=QUADS)[r, :, :, cols].bitcast(I32),
-                    in_=plane[r:P:32].bitcast(I32),
+        def store_rows(unit, t):
+            half, g = units[unit]
+            y_rows = out_0[K_PASS * g : K_PASS * (g + 1), BANK * half : BANK * (half + 1)]
+            nc.sync.dma_start(
+                out=y_rows.rearrange("(p t) m -> p t m", t=PACK)[:, t - 1 : t + 1, :], in_=y[unit][:, t - 1 : t + 1, :]
+            )
+
+        for n, (unit, t) in enumerate(rows):
+            half, g = units[unit]
+            cols = slice(BANK * half, BANK * (half + 1))
+            n_cols = slice(P * t, P * (t + 1))
+            pair = (n + 2) % 4
+            bounded_sum = bank(2 * pair, [P, BANK])
+            direct_sum = bank(2 * pair + 1, [P, BANK])
+            for sums, codes, plane in (
+                (bounded_sum, w3_codes[g][:, n_cols], w3_plane[g][:, n_cols]),
+                (direct_sum, w8_codes[:, g, t, :], w8_plane[:, g, t, :]),
+            ):
+                nc.tensor.matmul_mx(
+                    out=sums[:], lhsT=codes.bitcast(FP8X4), lhsT_scale=plane,
+                    rhs=z_codes[:, cols].bitcast(FP8X4), rhs_scale=z_plane[:, cols],
+                    start=True, stop=True,
                 )
+            bounded = last_bounded[:] if n == len(rows) - 1 else y[unit][:, t, :]
+            nc.scalar.activation(out=bounded, in_=bounded_sum[:], func=ACT.Tanh)
+            nc.vector.tensor_tensor(out=y[unit][:, t, :], in0=bounded, in1=direct_sum[:], op=ALU.add)
+            if n < GPSIMD_ROWS:
+                nc.gpsimd.tensor_scalar(
+                    out=y[unit][:, t, :], in0=y[unit][:, t, :], scalar1=amp_cols[:, g, t : t + 1], scalar2=0.0,
+                    op0=ALU.mult, op1=ALU.add,
+                )
+                if t % 2 == 1:
+                    store_rows(unit, t)
+        for unit, t in rows[GPSIMD_ROWS:]:
+            nc.scalar.activation(
+                out=y[unit][:, t, :], in_=y[unit][:, t, :], func=ACT.Copy, scale=amp_cols[:, units[unit][1], t : t + 1]
+            )
+            if t % 2 == 1:
+                store_rows(unit, t)
 
-        for unit, g in ((1, 0), (1, 1), (2, 0)):
-            round_y, quantise_y = score(unit, g, [[round_y], [quantise_y]])
-        for pair in zip(score(2, 1, [[], []]), [round_y, quantise_y]):
-            for step in pair:
-                step()
-        store_scale_rows(y_plane, slice(0, M), [nc.sync, nc.scalar])
+        y_plane = held([P, GROUPS, M], U8, "y_plane")
+        by_vector = held([P, len(units) - 1, BANK, PACK], BF16, "by_vector", tag="last_bounded")
+        by_scalar = held([P, BANK, PACK], BF16, "by_scalar")
+        y_rounded = [by_vector[:, unit] for unit in range(len(units) - 1)] + [by_scalar[:]]
+
+        def round_y(unit):
+            copy = nc.scalar.copy if unit == len(units) - 1 else nc.vector.tensor_copy
+            copy(
+                out=y_rounded[unit].rearrange("p (c i) t -> p c t i", i=4),
+                in_=y[unit][:].rearrange("p t (c i) -> p c t i", i=4),
+            )
+
+        def quantise_y(unit):
+            half, g = units[unit]
+            cols = slice(BANK * half, BANK * (half + 1))
+            y_codes = held([P, BANK], U32, "y_codes%d" % unit)
+            nc.vector.quantize_mx(
+                out=y_codes[:].bitcast(FP8X4), scales=y_plane[:, g, cols],
+                in_=y_rounded[unit].rearrange("p m t -> p (m t)"),
+            )
+            nc.sync.dma_start(
+                out=out_1[g].rearrange("p m t -> p (m t)").bitcast(I32)[:, cols], in_=y_codes[:].bitcast(I32)
+            )
+
+        round_y(0)
+        for unit in range(1, len(units)):
+            round_y(unit)
+            quantise_y(unit - 1)
+        quantise_y(len(units) - 1)
+        for r in range(QUADS):
+            [nc.sync, nc.scalar][r % 2].dma_start(
+                out=out_2.rearrange("g (q r) m -> r q g m", r=QUADS)[r].bitcast(I32),
+                in_=y_plane[r:P:32].bitcast(I32),
+            )

@@ -31,7 +31,11 @@ SCALE_ROW0 = P - 16 * PASSES
 W1_SPANS = ((0, 128), (128, 128), (256, 256))
 CHUNK = 256
 CHUNKS = M // CHUNK
-GPSIMD_ROWS = 10
+GPSIMD_STEPS = 11
+SCALAR_COLUMNS = 704
+FIRST_ROWS = 3
+BACK_BANKS = (6, 7, 0, 1)
+STEP_BANKS = (4, 2, 6, 0)
 
 
 def tile_list_schema_drift_scores_kernel(
@@ -308,7 +312,7 @@ def tile_list_schema_drift_scores_kernel(
         z_rounded = [held([P, BANK, PACK], BF16, "z_rounded%d" % half) for half in range(M // BANK)]
 
         def turn_back(c):
-            back = bank(c, [P, 2, 2, P])
+            back = bank(BACK_BANKS[c], [P, 2, 2, P])
             for s in range(2):
                 for u in range(2):
                     nc.tensor.transpose(
@@ -354,28 +358,33 @@ def tile_list_schema_drift_scores_kernel(
         quantise_w3(1, "z_rounded0")
         quantise_z(1)
 
-        units = [(half, g) for half in range(M // BANK) for g in range(GROUPS)]
-        y_tags = ["table0", "table1", "table2", "page0"]
-        y = [held([P, PACK, BANK], F32, "y", tag=tag) for tag in y_tags]
+        y = [held([P, PACK, M], F32, "y", tag="table%d" % g) for g in range(GROUPS)]
         last_bounded = held([P, BANK], F32, "last_bounded")
-        rows = [(unit, t) for unit in range(len(units)) for t in range(PACK)]
+        rows = [(g, t) for g in range(GROUPS) for t in range(PACK)]
+        steps = [(0, t, half) for half in range(HALVES) for t in range(FIRST_ROWS)]
+        steps.extend((g, t, half) for g, t in rows[FIRST_ROWS:] for half in range(HALVES))
 
-        def store_rows(unit, t):
-            half, g = units[unit]
-            y_rows = out_0[K_PASS * g : K_PASS * (g + 1), BANK * half : BANK * (half + 1)]
+        def runs(some_steps):
+            joined = []
+            for g, t, half in some_steps:
+                if joined and joined[-1][:2] == (g, t):
+                    joined[-1] = (g, t, 0, M)
+                else:
+                    joined.append((g, t, BANK * half, BANK * (half + 1)))
+            return joined
+
+        def store_row(g, t):
             nc.sync.dma_start(
-                out=y_rows.rearrange("(p t) m -> p t m", t=PACK)[:, t - 1 : t + 1, :], in_=y[unit][:, t - 1 : t + 1, :]
+                out=out_0[K_PASS * g : K_PASS * (g + 1), :].rearrange("(p t) m -> p t m", t=PACK)[:, t, :],
+                in_=y[g][:, t, :],
             )
 
-        for n, (unit, t) in enumerate(rows):
-            half, g = units[unit]
+        for n, (g, t, half) in enumerate(steps):
             cols = slice(BANK * half, BANK * (half + 1))
-            n_cols = slice(P * t, P * (t + 1))
-            pair = (n + 2) % 4
-            bounded_sum = bank(2 * pair, [P, BANK])
-            direct_sum = bank(2 * pair + 1, [P, BANK])
+            bounded_sum = bank(STEP_BANKS[n % 4], [P, BANK])
+            direct_sum = bank(STEP_BANKS[n % 4] + 1, [P, BANK])
             for sums, codes, plane in (
-                (bounded_sum, w3_codes[g][:, n_cols], w3_plane[g][:, n_cols]),
+                (bounded_sum, w3_codes[g][:, P * t : P * (t + 1)], w3_plane[g][:, P * t : P * (t + 1)]),
                 (direct_sum, w8_codes[:, g, t, :], w8_plane[:, g, t, :]),
             ):
                 nc.tensor.matmul_mx(
@@ -383,54 +392,53 @@ def tile_list_schema_drift_scores_kernel(
                     rhs=z_codes[:, cols].bitcast(FP8X4), rhs_scale=z_plane[:, cols],
                     start=True, stop=True,
                 )
-            bounded = last_bounded[:] if n == len(rows) - 1 else y[unit][:, t, :]
+            bounded = last_bounded[:] if n == len(steps) - 1 else y[g][:, t, cols]
             nc.scalar.activation(out=bounded, in_=bounded_sum[:], func=ACT.Tanh)
-            nc.vector.tensor_tensor(out=y[unit][:, t, :], in0=bounded, in1=direct_sum[:], op=ALU.add)
-            if n < GPSIMD_ROWS:
-                nc.gpsimd.tensor_scalar(
-                    out=y[unit][:, t, :], in0=y[unit][:, t, :], scalar1=amp_cols[:, g, t : t + 1], scalar2=0.0,
-                    op0=ALU.mult, op1=ALU.add,
-                )
-                if t % 2 == 1:
-                    store_rows(unit, t)
-        for unit, t in rows[GPSIMD_ROWS:]:
+            nc.vector.tensor_tensor(out=y[g][:, t, cols], in0=bounded, in1=direct_sum[:], op=ALU.add)
+        for g, t, first, end in runs(steps[:GPSIMD_STEPS]):
+            nc.gpsimd.tensor_scalar(
+                out=y[g][:, t, first:end], in0=y[g][:, t, first:end], scalar1=amp_cols[:, g, t : t + 1], scalar2=0.0,
+                op0=ALU.mult, op1=ALU.add,
+            )
+            if end == M:
+                store_row(g, t)
+        for g, t, first, end in runs(steps[GPSIMD_STEPS:]):
             nc.scalar.activation(
-                out=y[unit][:, t, :], in_=y[unit][:, t, :], func=ACT.Copy, scale=amp_cols[:, units[unit][1], t : t + 1]
+                out=y[g][:, t, first:end], in_=y[g][:, t, first:end], func=ACT.Copy, scale=amp_cols[:, g, t : t + 1]
             )
-            if t % 2 == 1:
-                store_rows(unit, t)
+            store_row(g, t)
 
-        y_plane = held([P, GROUPS, M], U8, "y_plane")
-        by_vector = held([P, len(units) - 1, BANK, PACK], BF16, "by_vector", tag="last_bounded")
-        by_scalar = held([P, BANK, PACK], BF16, "by_scalar")
-        y_rounded = [by_vector[:, unit] for unit in range(len(units) - 1)] + [by_scalar[:]]
+        y_plane = held([P, M], U8, "y_plane")
+        y_rounded = held([P, GROUPS, M, PACK], BF16, "y_rounded", tag="last_bounded")
 
-        def round_y(unit):
-            copy = nc.scalar.copy if unit == len(units) - 1 else nc.vector.tensor_copy
+        def round_y(copy, g, first, end):
             copy(
-                out=y_rounded[unit].rearrange("p (c i) t -> p c t i", i=4),
-                in_=y[unit][:].rearrange("p t (c i) -> p c t i", i=4),
+                out=y_rounded[:, g, first:end, :].rearrange("p (c i) t -> p c t i", i=4),
+                in_=y[g][:, :, first:end].rearrange("p t (c i) -> p c t i", i=4),
             )
 
-        def quantise_y(unit):
-            half, g = units[unit]
+        def quantise_y(g, half):
             cols = slice(BANK * half, BANK * (half + 1))
-            y_codes = held([P, BANK], U32, "y_codes%d" % unit)
+            y_codes = held([P, BANK], U32, "y_codes", tag="old%d" % (HALVES * g + half))
             nc.vector.quantize_mx(
-                out=y_codes[:].bitcast(FP8X4), scales=y_plane[:, g, cols],
-                in_=y_rounded[unit].rearrange("p m t -> p (m t)"),
+                out=y_codes[:].bitcast(FP8X4), scales=y_plane[QUADS * g : P, cols],
+                in_=y_rounded[:, g, cols, :].rearrange("p m t -> p (m t)"),
             )
             nc.sync.dma_start(
                 out=out_1[g].rearrange("p m t -> p (m t)").bitcast(I32)[:, cols], in_=y_codes[:].bitcast(I32)
             )
 
-        round_y(0)
-        for unit in range(1, len(units)):
-            round_y(unit)
-            quantise_y(unit - 1)
-        quantise_y(len(units) - 1)
-        for r in range(QUADS):
-            [nc.sync, nc.scalar][r % 2].dma_start(
-                out=out_2.rearrange("g (q r) m -> r q g m", r=QUADS)[r].bitcast(I32),
-                in_=y_plane[r:P:32].bitcast(I32),
+        round_y(nc.vector.tensor_copy, 0, 0, BANK)
+        round_y(nc.vector.tensor_copy, 0, BANK, M)
+        quantise_y(0, 0)
+        round_y(nc.vector.tensor_copy, 1, 0, M - SCALAR_COLUMNS)
+        round_y(nc.scalar.copy, 1, M - SCALAR_COLUMNS, BANK)
+        round_y(nc.scalar.copy, 1, BANK, M)
+        quantise_y(0, 1)
+        quantise_y(1, 0)
+        quantise_y(1, 1)
+        for q in (0, 2, 1, 3):
+            [nc.sync, nc.scalar][q % 2].dma_start(
+                out=out_2[:, QUADS * q : QUADS * (q + 1), :].bitcast(I32),
+                in_=y_plane[32 * q : 32 * q + QUADS * GROUPS, :].bitcast(I32),
             )

@@ -46,6 +46,7 @@ def tile_list_schema_drift_scores_kernel(
     with ExitStack() as ctx:
         lists = ctx.enter_context(tc.tile_pool(name="lists", bufs=1))
         keep = ctx.enter_context(tc.tile_pool(name="keep", bufs=1))
+        shared = ctx.enter_context(tc.tile_pool(name="shared", bufs=1))
         psum = ctx.enter_context(tc.psum_pool(name="psum", bufs=1))
 
         def held(shape, dtype, name, tag=None, bufs=1):
@@ -81,7 +82,9 @@ def tile_list_schema_drift_scores_kernel(
         ident = held([P, P], F32, "ident")
         make_identity(nc, ident[:])
 
-        table = [held([P, T], U32, "table%d" % a) for a in range(PASSES)]
+        late_bytes = PASSES * (H - P) + N
+        table = [held([P, T], U32, "table%d" % a) for a in range(PASSES - 1)]
+        table.append(shared.tile([P, T], U32, name="table_last", align_bytes=64, offset=late_bytes))
         w1_raw = {}
 
         def load_table(a):
@@ -164,13 +167,13 @@ def tile_list_schema_drift_scores_kernel(
         quantise_w1(0, 0, round_w1(0, 0, "rounded", 3))
         gather_words(1, 0, S, "v_codes1")
         quantise_w1(0, 1, round_w1(0, 1, "rounded", 3))
-        pages.append(held([P, T2], F32, "page1", tag="w1_raw0_1"))
-        nc.vector.memset(pages[1][:].bitcast(I32), 0)
         gather_words(2, 0, BANK, "v_codes2_0")
         quantise_w1(0, 2, round_w1(0, 2, "rounded", 3))
         gather_words(2, BANK, BANK, "w1_raw0_2")
-        late_planes = held([P, PASSES * (H - P) + N], U8, "late_planes", tag="table2")
+        late_planes = shared.tile([P, late_bytes], U8, name="late_planes", align_bytes=64, offset=4 * T2)
         nc.vector.memset(late_planes[:].bitcast(I32), 0)
+        pages.append(shared.tile([P, T2], F32, name="page1", align_bytes=64, offset=0))
+        nc.gpsimd.memset(pages[1][:].bitcast(I32), 0)
         w4_plane_rest = late_planes[:, 0 : PASSES * (H - P)].rearrange("p (a c) -> p a c", a=PASSES)
         w8_plane_raw = late_planes[:, PASSES * (H - P) :].rearrange("p (a c) -> p a c", a=1)
         nc.sync.dma_start(out=w4_rest[:].bitcast(I32), in_=w4_rows[:, :, 2 * P : 2 * H].bitcast(I32))

@@ -31,9 +31,8 @@ SCALE_ROW0 = P - 16 * PASSES
 W1_SPANS = ((0, 128), (128, 128), (256, 256))
 CHUNK = 256
 CHUNKS = M // CHUNK
-GPSIMD_STEPS = 11
-SCALAR_COLUMNS = 704
-FIRST_ROWS = 3
+SCALAR_COLUMNS = 768
+Z_PARTS = ((0, 256), (256, 256), (512, 512))
 BACK_BANKS = (6, 7, 0, 1)
 STEP_BANKS = (4, 2, 6, 0)
 
@@ -312,7 +311,7 @@ def tile_list_schema_drift_scores_kernel(
 
         z_codes = held([P, M], U32, "z_codes")
         z_plane = held([P, M], U8, "z_plane")
-        z_rounded = [held([P, BANK, PACK], BF16, "z_rounded%d" % half) for half in range(M // BANK)]
+        z_rounded = [held([P, width, PACK], BF16, "z_rounded%d" % first) for first, width in Z_PARTS]
 
         def turn_back(c):
             back = bank(BACK_BANKS[c], [P, 2, 2, P])
@@ -323,17 +322,18 @@ def tile_list_schema_drift_scores_kernel(
                         z_turned[c][:, s, u].rearrange("m p e -> m (p e)").bitcast(F32),
                         ident[:],
                     )
-            words = z_rounded[c // 2][:].rearrange("p m t -> p (m t)").bitcast(F32)
+            part = min(c, len(Z_PARTS) - 1)
+            words = z_rounded[part][:].rearrange("p m t -> p (m t)").bitcast(F32)
             nc.scalar.copy(
-                out=words[:, 2 * CHUNK * (c % 2) : 2 * CHUNK * (c % 2 + 1)].rearrange("p (s m u) -> p s m u", s=2, u=2),
+                out=words[:, 2 * CHUNK * (c - part) : 2 * CHUNK * (c - part + 1)].rearrange("p (s m u) -> p s m u", s=2, u=2),
                 in_=back[:].rearrange("p s u m -> p s m u"),
             )
 
-        def quantise_z(half):
-            cols = slice(BANK * half, BANK * (half + 1))
+        def quantise_z(part):
+            cols = slice(Z_PARTS[part][0], sum(Z_PARTS[part]))
             nc.vector.quantize_mx(
                 out=z_codes[:, cols].bitcast(FP8X4), scales=z_plane[:, cols],
-                in_=z_rounded[half][:].rearrange("p m t -> p (m t)"),
+                in_=z_rounded[part][:].rearrange("p m t -> p (m t)"),
             )
 
         w3_codes, w3_plane = {}, {}
@@ -360,21 +360,16 @@ def tile_list_schema_drift_scores_kernel(
         turn_back(CHUNKS - 1)
         quantise_w3(1, "z_rounded0")
         quantise_z(1)
+        quantise_z(2)
 
         y = [held([P, PACK, M], F32, "y", tag="table%d" % g) for g in range(GROUPS)]
-        last_bounded = held([P, BANK], F32, "last_bounded")
-        rows = [(g, t) for g in range(GROUPS) for t in range(PACK)]
-        steps = [(0, t, half) for half in range(HALVES) for t in range(FIRST_ROWS)]
-        steps.extend((g, t, half) for g, t in rows[FIRST_ROWS:] for half in range(HALVES))
-
-        def runs(some_steps):
-            joined = []
-            for g, t, half in some_steps:
-                if joined and joined[-1][:2] == (g, t):
-                    joined[-1] = (g, t, 0, M)
-                else:
-                    joined.append((g, t, BANK * half, BANK * (half + 1)))
-            return joined
+        last_bounded = held([P, 1, BANK], F32, "last_bounded")
+        steps = [(0, t, first, CHUNK) for first in (0, CHUNK) for t in (0, 2)]
+        steps.extend((0, t, BANK, BANK) for t in range(PACK))
+        steps.extend((1, t, first, BANK) for t in range(PACK) for first in (0, BANK))
+        by_gpsimd = [(0, t, first, end) for first, end in ((0, CHUNK), (CHUNK, M)) for t in range(PACK)]
+        by_gpsimd.extend([(1, 0, 0, M), (1, 1, 0, BANK)])
+        by_scalar = [(1, 1, BANK, M), (1, 2, 0, M), (1, 3, 0, M)]
 
         def store_row(g, t):
             nc.sync.dma_start(
@@ -382,30 +377,34 @@ def tile_list_schema_drift_scores_kernel(
                 in_=y[g][:, t, :],
             )
 
-        for n, (g, t, half) in enumerate(steps):
-            cols = slice(BANK * half, BANK * (half + 1))
-            bounded_sum = bank(STEP_BANKS[n % 4], [P, BANK])
-            direct_sum = bank(STEP_BANKS[n % 4] + 1, [P, BANK])
+        for n, (g, t0, first, width) in enumerate(steps):
+            cols = slice(first, first + width)
+            count = BANK // width
+            bounded_sum = bank(STEP_BANKS[n % 4], [P, count, width])
+            direct_sum = bank(STEP_BANKS[n % 4] + 1, [P, count, width])
             for sums, codes, plane in (
-                (bounded_sum, w3_codes[g][:, P * t : P * (t + 1)], w3_plane[g][:, P * t : P * (t + 1)]),
-                (direct_sum, w8_codes[:, g, t, :], w8_plane[:, g, t, :]),
+                (bounded_sum, w3_codes[g][:], w3_plane[g][:]),
+                (direct_sum, w8_codes[:, g].rearrange("p t m -> p (t m)"), w8_plane[:, g].rearrange("p t m -> p (t m)")),
             ):
-                nc.tensor.matmul_mx(
-                    out=sums[:], lhsT=codes.bitcast(FP8X4), lhsT_scale=plane,
-                    rhs=z_codes[:, cols].bitcast(FP8X4), rhs_scale=z_plane[:, cols],
-                    start=True, stop=True,
-                )
-            bounded = last_bounded[:] if n == len(steps) - 1 else y[g][:, t, cols]
+                for i in range(count):
+                    n_cols = slice(P * (t0 + i), P * (t0 + i + 1))
+                    nc.tensor.matmul_mx(
+                        out=sums[:, i, :], lhsT=codes[:, n_cols].bitcast(FP8X4), lhsT_scale=plane[:, n_cols],
+                        rhs=z_codes[:, cols].bitcast(FP8X4), rhs_scale=z_plane[:, cols],
+                        start=True, stop=True,
+                    )
+            own = y[g][:, t0 : t0 + count, cols]
+            bounded = last_bounded[:] if n == len(steps) - 1 else own
             nc.scalar.activation(out=bounded, in_=bounded_sum[:], func=ACT.Tanh)
-            nc.vector.tensor_tensor(out=y[g][:, t, cols], in0=bounded, in1=direct_sum[:], op=ALU.add)
-        for g, t, first, end in runs(steps[:GPSIMD_STEPS]):
+            nc.vector.tensor_tensor(out=own, in0=bounded, in1=direct_sum[:], op=ALU.add)
+        for g, t, first, end in by_gpsimd:
             nc.gpsimd.tensor_scalar(
                 out=y[g][:, t, first:end], in0=y[g][:, t, first:end], scalar1=amp_cols[:, g, t : t + 1], scalar2=0.0,
                 op0=ALU.mult, op1=ALU.add,
             )
             if end == M:
                 store_row(g, t)
-        for g, t, first, end in runs(steps[GPSIMD_STEPS:]):
+        for g, t, first, end in by_scalar:
             nc.scalar.activation(
                 out=y[g][:, t, first:end], in_=y[g][:, t, first:end], func=ACT.Copy, scale=amp_cols[:, g, t : t + 1]
             )
@@ -420,9 +419,9 @@ def tile_list_schema_drift_scores_kernel(
                 in_=y[g][:, :, first:end].rearrange("p t (c i) -> p c t i", i=4),
             )
 
-        def quantise_y(g, half):
-            cols = slice(BANK * half, BANK * (half + 1))
-            y_codes = held([P, BANK], U32, "y_codes", tag="old%d" % (HALVES * g + half))
+        def quantise_y(g, first, end):
+            cols = slice(first, end)
+            y_codes = held([P, end - first], U32, "y_codes%d_%d" % (g, first))
             nc.vector.quantize_mx(
                 out=y_codes[:].bitcast(FP8X4), scales=y_plane[QUADS * g : P, cols],
                 in_=y_rounded[:, g, cols, :].rearrange("p m t -> p (m t)"),
@@ -433,13 +432,15 @@ def tile_list_schema_drift_scores_kernel(
 
         round_y(nc.vector.tensor_copy, 0, 0, BANK)
         round_y(nc.vector.tensor_copy, 0, BANK, M)
-        quantise_y(0, 0)
+        quantise_y(0, 0, BANK)
         round_y(nc.vector.tensor_copy, 1, 0, M - SCALAR_COLUMNS)
         round_y(nc.scalar.copy, 1, M - SCALAR_COLUMNS, BANK)
-        round_y(nc.scalar.copy, 1, BANK, M)
-        quantise_y(0, 1)
-        quantise_y(1, 0)
-        quantise_y(1, 1)
+        round_y(nc.scalar.copy, 1, BANK, M - CHUNK)
+        round_y(nc.scalar.copy, 1, M - CHUNK, M)
+        quantise_y(0, BANK, M)
+        quantise_y(1, 0, BANK)
+        quantise_y(1, BANK, M - CHUNK)
+        quantise_y(1, M - CHUNK, M)
         for q in (0, 2, 1, 3):
             [nc.sync, nc.scalar][q % 2].dma_start(
                 out=out_2[:, QUADS * q : QUADS * (q + 1), :].bitcast(I32),

@@ -31,10 +31,10 @@ SCALE_ROW0 = P - 16 * PASSES
 W1_SPANS = ((0, 128), (128, 128), (256, 256))
 CHUNK = 256
 CHUNKS = M // CHUNK
-SCALAR_COLUMNS = 768
+SCALAR_COLUMNS = 832
 Z_PARTS = ((0, 256), (256, 256), (512, 512))
-BACK_BANKS = (6, 7, 0, 1)
-STEP_BANKS = (4, 2, 6, 0)
+BACK_BANKS = (6, 7, 2, 3)
+STEP_BANKS = (4, 6, 0, 2)
 
 
 def tile_list_schema_drift_scores_kernel(
@@ -253,12 +253,12 @@ def tile_list_schema_drift_scores_kernel(
                 )
             return turned
 
-        def turn_picked(b, first, picked, turned):
+        def turn_picked(b, first, picked, turned, opens=False):
             subs = picked.shape[1] // P
             for s in range(subs):
                 nc.tensor.matmul(
                     out=turned[:, s, :], lhsT=picked[:, P * s : P * (s + 1)],
-                    rhs=ident[:], is_transpose=True, start=False, stop=(s == subs - 1),
+                    rhs=ident[:], is_transpose=True, start=(opens and s == 0), stop=(s == subs - 1),
                 )
             for s0 in range(0, subs, CHUNK // P):
                 nc.scalar.copy(
@@ -305,7 +305,7 @@ def tile_list_schema_drift_scores_kernel(
         turn(1, picked1)
         round_w3(1)
         last = BLOCKS - 1
-        last_turned = [turn_old(last, CHUNK * c, CHUNK, c) for c in range(CHUNKS)]
+        last_turned = [turn_old(last, CHUNK * c, CHUNK, c) for c in range(2)]
         turn(2, picked2)
         scatter(3, BANK, last_deltas[:])
 
@@ -346,20 +346,27 @@ def tile_list_schema_drift_scores_kernel(
                 in_=w3_rounded[g][:].rearrange("p t m j -> p (t m j)"),
             )
 
-        for c in range(CHUNKS):
+        for c in range(2):
             turn_picked(last, CHUNK * c, fetch(last, CHUNK * c, CHUNK, "picked3_%d" % c)[:], last_turned[c])
-            if c > 0:
-                turn_back(c - 1)
+        for c in range(2, CHUNKS):
+            summed = held([P, CHUNK], F32, "summed%d" % c)
+            nc.vector.tensor_tensor(
+                out=summed[:], in0=pages[last % 2][:].indirect(entries(pinned_list, CHUNK * c, CHUNK)),
+                in1=old_rows[last][:, CHUNK * c : CHUNK * (c + 1)], op=ALU.add,
+            )
+            turn_back(c - 2)
+            turn_picked(last, CHUNK * c, summed[:], bank(c - 2, [P, CHUNK // P, P]), opens=True)
         quantise_w3(0, "gains")
-        w8_plane = held([P, GROUPS, PACK, P], U8, "w8_plane", tag="w8_raw")
+        quantise_z(0)
+        w8_plane = held([P, GROUPS, PACK, P], U8, "w8_plane", tag="z_rounded0")
         nc.vector.tensor_copy(
             out=w8_plane[:].rearrange("p g t (c i) -> p g c t i", i=16),
             in_=w8_plane_raw[:, 0, :].rearrange("p (g c i t) -> p g c t i", g=GROUPS, i=16, t=PACK),
         )
-        quantise_z(0)
-        turn_back(CHUNKS - 1)
-        quantise_w3(1, "z_rounded0")
+        for c in range(2, CHUNKS):
+            turn_back(c)
         quantise_z(1)
+        quantise_w3(1, "z_rounded256")
         quantise_z(2)
 
         y = [held([P, PACK, M], F32, "y", tag="table%d" % g) for g in range(GROUPS)]
@@ -368,11 +375,11 @@ def tile_list_schema_drift_scores_kernel(
         steps.extend((0, t, BANK, BANK) for t in range(PACK))
         steps.extend((1, t, first, BANK) for t in range(PACK) for first in (0, BANK))
         by_gpsimd = [(0, t, first, end) for first, end in ((0, CHUNK), (CHUNK, M)) for t in range(PACK)]
-        by_gpsimd.extend([(1, 0, 0, M), (1, 1, 0, BANK)])
-        by_scalar = [(1, 1, BANK, M), (1, 2, 0, M), (1, 3, 0, M)]
+        by_gpsimd.extend((1, t, 0, M) for t in range(2))
+        by_scalar = [(1, t, 0, M) for t in range(2, PACK)]
 
-        def store_row(g, t):
-            nc.sync.dma_start(
+        def store_row(g, t, queue=nc.sync):
+            queue.dma_start(
                 out=out_0[K_PASS * g : K_PASS * (g + 1), :].rearrange("(p t) m -> p t m", t=PACK)[:, t, :],
                 in_=y[g][:, t, :],
             )
@@ -408,10 +415,12 @@ def tile_list_schema_drift_scores_kernel(
             nc.scalar.activation(
                 out=y[g][:, t, first:end], in_=y[g][:, t, first:end], func=ACT.Copy, scale=amp_cols[:, g, t : t + 1]
             )
-            store_row(g, t)
+            store_row(g, t, nc.scalar if t < PACK - 1 else nc.sync)
 
         y_plane = held([P, M], U8, "y_plane")
         y_rounded = held([P, GROUPS, M, PACK], BF16, "y_rounded", tag="last_bounded")
+
+        y_codes = [held([P, M], U32, "y_codes%d" % g) for g in range(GROUPS)]
 
         def round_y(copy, g, first, end):
             copy(
@@ -421,13 +430,15 @@ def tile_list_schema_drift_scores_kernel(
 
         def quantise_y(g, first, end):
             cols = slice(first, end)
-            y_codes = held([P, end - first], U32, "y_codes%d_%d" % (g, first))
             nc.vector.quantize_mx(
-                out=y_codes[:].bitcast(FP8X4), scales=y_plane[QUADS * g : P, cols],
+                out=y_codes[g][:, cols].bitcast(FP8X4), scales=y_plane[QUADS * g : P, cols],
                 in_=y_rounded[:, g, cols, :].rearrange("p m t -> p (m t)"),
             )
+
+        def store_codes(g, first, end):
             nc.sync.dma_start(
-                out=out_1[g].rearrange("p m t -> p (m t)").bitcast(I32)[:, cols], in_=y_codes[:].bitcast(I32)
+                out=out_1[g].rearrange("p m t -> p (m t)").bitcast(I32)[:, first:end],
+                in_=y_codes[g][:, first:end].bitcast(I32),
             )
 
         round_y(nc.vector.tensor_copy, 0, 0, BANK)
@@ -438,9 +449,12 @@ def tile_list_schema_drift_scores_kernel(
         round_y(nc.scalar.copy, 1, BANK, M - CHUNK)
         round_y(nc.scalar.copy, 1, M - CHUNK, M)
         quantise_y(0, BANK, M)
+        store_codes(0, 0, M)
         quantise_y(1, 0, BANK)
+        store_codes(1, 0, BANK)
         quantise_y(1, BANK, M - CHUNK)
         quantise_y(1, M - CHUNK, M)
+        store_codes(1, BANK, M)
         for q in (0, 2, 1, 3):
             [nc.sync, nc.scalar][q % 2].dma_start(
                 out=out_2[:, QUADS * q : QUADS * (q + 1), :].bitcast(I32),

@@ -292,9 +292,10 @@ def tile_list_schema_drift_scores_kernel(
         picked1 = fetch(1, 0, M, "w1_raw2_2")
         scatter(2, 0, encode_block(2, "deltas2")[:])
         put_half(3, 0, old_passes + new_passes, "deltas0_0")
-        picked2 = fetch(2, 0, M, "picked2")
         round_w3(0)
-        last_deltas = held([P, BANK], F32, "deltas", tag="w3_raw0")
+        picked2 = fetch(2, 0, M, "w3_raw0")
+        round_w3(1)
+        last_deltas = held([P, BANK], F32, "deltas", tag="w3_raw1")
         encode(3, 1, old_passes + new_passes, last_deltas[:])
         w8_codes = held([P, GROUPS, PACK, P], U32, "w8_codes", tag="w1_raw0_2")
         nc.scalar.copy(
@@ -303,10 +304,11 @@ def tile_list_schema_drift_scores_kernel(
         )
         turn(0, picked0)
         turn(1, picked1)
-        round_w3(1)
         last = BLOCKS - 1
+        for c, index in enumerate((4, 5, 0, 1)):
+            turned = turn_old(2, CHUNK * c, CHUNK, index)
+            turn_picked(2, CHUNK * c, picked2[:, CHUNK * c : CHUNK * (c + 1)], turned)
         last_turned = [turn_old(last, CHUNK * c, CHUNK, c) for c in range(2)]
-        turn(2, picked2)
         scatter(3, BANK, last_deltas[:])
 
         z_codes = held([P, M], U32, "z_codes")

@@ -308,6 +308,13 @@ def tile_list_schema_drift_scores_kernel(
         for c, index in enumerate((4, 5, 0, 1)):
             turned = turn_old(2, CHUNK * c, CHUNK, index)
             turn_picked(2, CHUNK * c, picked2[:, CHUNK * c : CHUNK * (c + 1)], turned)
+        warm = bank(4, [P, BANK])
+        for a in range(PASSES):
+            nc.tensor.matmul_mx(
+                out=warm[:], lhsT=w1_codes[0][:, a, :].bitcast(FP8X4), lhsT_scale=w1_plane[0][:, a, :],
+                rhs=v_codes[0, 0].bitcast(FP8X4), rhs_scale=v_plane[:, 0, 0:BANK],
+                start=True, stop=True,
+            )
         last_turned = [turn_old(last, CHUNK * c, CHUNK, c) for c in range(2)]
         scatter(3, BANK, last_deltas[:])
 

@@ -253,12 +253,12 @@ def tile_list_schema_drift_scores_kernel(
                 )
             return turned
 
-        def turn_picked(b, first, picked, turned, opens=False):
+        def turn_picked(b, first, picked, turned):
             subs = picked.shape[1] // P
             for s in range(subs):
                 nc.tensor.matmul(
                     out=turned[:, s, :], lhsT=picked[:, P * s : P * (s + 1)],
-                    rhs=ident[:], is_transpose=True, start=(opens and s == 0), stop=(s == subs - 1),
+                    rhs=ident[:], is_transpose=True, start=False, stop=(s == subs - 1),
                 )
             for s0 in range(0, subs, CHUNK // P):
                 nc.scalar.copy(
@@ -358,13 +358,9 @@ def tile_list_schema_drift_scores_kernel(
         for c in range(2):
             turn_picked(last, CHUNK * c, fetch(last, CHUNK * c, CHUNK, "picked3_%d" % c)[:], last_turned[c])
         for c in range(2, CHUNKS):
-            summed = held([P, CHUNK], F32, "summed%d" % c)
-            nc.vector.tensor_tensor(
-                out=summed[:], in0=pages[last % 2][:].indirect(entries(pinned_list, CHUNK * c, CHUNK)),
-                in1=old_rows[last][:, CHUNK * c : CHUNK * (c + 1)], op=ALU.add,
-            )
+            picked = fetch(last, CHUNK * c, CHUNK, "picked3_%d" % c)
             turn_back(c - 2)
-            turn_picked(last, CHUNK * c, summed[:], bank(c - 2, [P, CHUNK // P, P]), opens=True)
+            turn_picked(last, CHUNK * c, picked[:], turn_old(last, CHUNK * c, CHUNK, c - 2))
         quantise_w3(0, "gains")
         quantise_z(0)
         w8_plane = held([P, GROUPS, PACK, P], U8, "w8_plane", tag="z_rounded0")

@@ -279,10 +279,20 @@ def tile_list_schema_drift_scores_kernel(
                 in_=w3_raw[g][:].rearrange("p j (m t) -> p m t j", t=PACK),
             )
 
+        def warm_up(index, a, count):
+            warm = bank(index, [P, BANK])
+            for n in range(count):
+                nc.tensor.matmul_mx(
+                    out=warm[:], lhsT=w1_codes[0][:, a, :].bitcast(FP8X4), lhsT_scale=w1_plane[0][:, a, :],
+                    rhs=v_codes[a, 0].bitcast(FP8X4), rhs_scale=v_plane[:, a, 0:BANK],
+                    start=True, stop=True,
+                )
+
         put_half(0, 0, new_passes[:2] + old_passes + new_passes[2:], "deltas0_0")
         for a in range(PASSES):
             quantise_w1(1, a, round_w1(1, a, "rounded", 3))
         put_half(0, 1, new_passes + old_passes, "w1_raw1_2")
+        warm_up(3, 1, 2)
         put_half(1, 0, old_passes + new_passes, "deltas1_0")
         quantise_w1(2, 0, round_w1(2, 0, "rounded", 3))
         put_half(1, 1, old_passes + new_passes, "w1_raw2_0")
@@ -308,13 +318,7 @@ def tile_list_schema_drift_scores_kernel(
         for c, index in enumerate((4, 5, 0, 1)):
             turned = turn_old(2, CHUNK * c, CHUNK, index)
             turn_picked(2, CHUNK * c, picked2[:, CHUNK * c : CHUNK * (c + 1)], turned)
-        warm = bank(4, [P, BANK])
-        for a in range(PASSES):
-            nc.tensor.matmul_mx(
-                out=warm[:], lhsT=w1_codes[0][:, a, :].bitcast(FP8X4), lhsT_scale=w1_plane[0][:, a, :],
-                rhs=v_codes[0, 0].bitcast(FP8X4), rhs_scale=v_plane[:, 0, 0:BANK],
-                start=True, stop=True,
-            )
+        warm_up(4, 0, 3)
         last_turned = [turn_old(last, CHUNK * c, CHUNK, c) for c in range(2)]
         scatter(3, BANK, last_deltas[:])
 

@@ -32,8 +32,9 @@ W1_SPANS = ((0, 128), (128, 128), (256, 256))
 CHUNK = 256
 CHUNKS = M // CHUNK
 SCALAR_COLUMNS = 832
-Z_PARTS = ((0, 256), (256, 256), (512, 512))
-BACK_BANKS = (6, 7, 2, 3)
+PIECES = ((0, 128), (128, 128), (256, 256), (512, 256), (768, 256))
+Z_PARTS = ((0, 128), (128, 128), (256, 256), (512, 512))
+BACK_BANKS = (6, 7, 3, 2, 3)
 STEP_BANKS = (4, 6, 0, 2)
 
 
@@ -237,7 +238,7 @@ def tile_list_schema_drift_scores_kernel(
         new_passes = [(a, False) for a in range(PASSES)]
         old_passes = [(a, True) for a in range(PASSES)]
 
-        z_turned = [held([P, CHUNK // P, 2, P, 2], BF16, "z_turned%d" % c) for c in range(CHUNKS)]
+        z_turned = [held([P, width // P, 2, P, 2], BF16, "z_turned%d" % first) for first, width in PIECES]
 
         def fetch(b, first, count, tag):
             picked = held([P, count], F32, "picked", tag=tag)
@@ -260,11 +261,13 @@ def tile_list_schema_drift_scores_kernel(
                     out=turned[:, s, :], lhsT=picked[:, P * s : P * (s + 1)],
                     rhs=ident[:], is_transpose=True, start=False, stop=(s == subs - 1),
                 )
-            for s0 in range(0, subs, CHUNK // P):
-                nc.scalar.copy(
-                    out=z_turned[(first + P * s0) // CHUNK][:, :, :, 32 * b : 32 * (b + 1), :],
-                    in_=turned[:, s0 : s0 + CHUNK // P, :].rearrange("m s (q u e) -> m s u q e", u=2, e=2),
-                )
+            for c, (start, width) in enumerate(PIECES):
+                if first <= start < first + P * subs:
+                    own = slice((start - first) // P, (start + width - first) // P)
+                    nc.scalar.copy(
+                        out=z_turned[c][:, :, :, 32 * b : 32 * (b + 1), :],
+                        in_=turned[:, own, :].rearrange("m s (q u e) -> m s u q e", u=2, e=2),
+                    )
 
         def turn(b, picked):
             for half in range(M // BANK):
@@ -319,7 +322,7 @@ def tile_list_schema_drift_scores_kernel(
             turned = turn_old(2, CHUNK * c, CHUNK, index)
             turn_picked(2, CHUNK * c, picked2[:, CHUNK * c : CHUNK * (c + 1)], turned)
         warm_up(4, 0, 3)
-        last_turned = [turn_old(last, CHUNK * c, CHUNK, c) for c in range(2)]
+        last_turned = [turn_old(last, first, width, c) for c, (first, width) in enumerate(PIECES[:3])]
         scatter(3, BANK, last_deltas[:])
 
         z_codes = held([P, M], U32, "z_codes")
@@ -327,8 +330,10 @@ def tile_list_schema_drift_scores_kernel(
         z_rounded = [held([P, width, PACK], BF16, "z_rounded%d" % first) for first, width in Z_PARTS]
 
         def turn_back(c):
-            back = bank(BACK_BANKS[c], [P, 2, 2, P])
-            for s in range(2):
+            first, width = PIECES[c]
+            subs = width // P
+            back = bank(BACK_BANKS[c], [P, subs, 2, P])
+            for s in range(subs):
                 for u in range(2):
                     nc.tensor.transpose(
                         back[:, s, u, :],
@@ -337,8 +342,9 @@ def tile_list_schema_drift_scores_kernel(
                     )
             part = min(c, len(Z_PARTS) - 1)
             words = z_rounded[part][:].rearrange("p m t -> p (m t)").bitcast(F32)
+            own = first - Z_PARTS[part][0]
             nc.scalar.copy(
-                out=words[:, 2 * CHUNK * (c - part) : 2 * CHUNK * (c - part + 1)].rearrange("p (s m u) -> p s m u", s=2, u=2),
+                out=words[:, 2 * own : 2 * (own + width)].rearrange("p (s m u) -> p s m u", s=subs, u=2),
                 in_=back[:].rearrange("p s u m -> p s m u"),
             )
 
@@ -359,12 +365,11 @@ def tile_list_schema_drift_scores_kernel(
                 in_=w3_rounded[g][:].rearrange("p t m j -> p (t m j)"),
             )
 
-        for c in range(2):
-            turn_picked(last, CHUNK * c, fetch(last, CHUNK * c, CHUNK, "picked3_%d" % c)[:], last_turned[c])
-        for c in range(2, CHUNKS):
-            picked = fetch(last, CHUNK * c, CHUNK, "picked3_%d" % c)
-            turn_back(c - 2)
-            turn_picked(last, CHUNK * c, picked[:], turn_old(last, CHUNK * c, CHUNK, c - 2))
+        for c, (first, width) in enumerate(PIECES):
+            picked = fetch(last, first, width, "picked3_%d" % c)
+            if c >= 2:
+                turn_back(c - 2)
+            turn_picked(last, first, picked[:], last_turned[c] if c < 3 else turn_old(last, first, width, c - 3))
         quantise_w3(0, "gains")
         quantise_z(0)
         w8_plane = held([P, GROUPS, PACK, P], U8, "w8_plane", tag="z_rounded0")
@@ -372,15 +377,17 @@ def tile_list_schema_drift_scores_kernel(
             out=w8_plane[:].rearrange("p g t (c i) -> p g c t i", i=16),
             in_=w8_plane_raw[:, 0, :].rearrange("p (g c i t) -> p g c t i", g=GROUPS, i=16, t=PACK),
         )
-        for c in range(2, CHUNKS):
+        for c in range(len(PIECES) - 2, len(PIECES)):
             turn_back(c)
         quantise_z(1)
-        quantise_w3(1, "z_rounded256")
         quantise_z(2)
+        quantise_w3(1, "z_rounded256")
+        quantise_z(3)
 
         y = [held([P, PACK, M], F32, "y", tag="table%d" % g) for g in range(GROUPS)]
         last_bounded = held([P, 1, BANK], F32, "last_bounded")
-        steps = [(0, t, first, CHUNK) for first in (0, CHUNK) for t in (0, 2)]
+        steps = [(0, 0, first, P) for first in (0, P)]
+        steps.extend((0, t, CHUNK, CHUNK) for t in (0, 2))
         steps.extend((0, t, BANK, BANK) for t in range(PACK))
         steps.extend((1, t, first, BANK) for t in range(PACK) for first in (0, BANK))
         by_gpsimd = [(0, t, first, end) for first, end in ((0, CHUNK), (CHUNK, M)) for t in range(PACK)]

@@ -171,7 +171,7 @@ def tile_list_schema_drift_scores_kernel(
         quantise_w1(0, 2, round_w1(0, 2, "rounded", 3))
         gather_words(2, BANK, BANK, "w1_raw0_2")
         late_planes = shared.tile([P, late_bytes], U8, name="late_planes", align_bytes=64, offset=4 * T2)
-        nc.vector.memset(late_planes[:].bitcast(I32), 0)
+        nc.gpsimd.memset(late_planes[:].bitcast(I32), 0)
         pages.append(shared.tile([P, T2], F32, name="page1", align_bytes=64, offset=0))
         nc.gpsimd.memset(pages[1][:].bitcast(I32), 0)
         w4_plane_rest = late_planes[:, 0 : PASSES * (H - P)].rearrange("p (a c) -> p a c", a=PASSES)
@@ -377,12 +377,10 @@ def tile_list_schema_drift_scores_kernel(
             out=w8_plane[:].rearrange("p g t (c i) -> p g c t i", i=16),
             in_=w8_plane_raw[:, 0, :].rearrange("p (g c i t) -> p g c t i", g=GROUPS, i=16, t=PACK),
         )
-        for c in range(len(PIECES) - 2, len(PIECES)):
-            turn_back(c)
+        turn_back(len(PIECES) - 2)
         quantise_z(1)
         quantise_z(2)
         quantise_w3(1, "z_rounded256")
-        quantise_z(3)
 
         y = [held([P, PACK, M], F32, "y", tag="table%d" % g) for g in range(GROUPS)]
         last_bounded = held([P, 1, BANK], F32, "last_bounded")
@@ -420,6 +418,10 @@ def tile_list_schema_drift_scores_kernel(
             bounded = last_bounded[:] if n == len(steps) - 1 else own
             nc.scalar.activation(out=bounded, in_=bounded_sum[:], func=ACT.Tanh)
             nc.vector.tensor_tensor(out=own, in0=bounded, in1=direct_sum[:], op=ALU.add)
+            if n == 0:
+                turn_back(len(PIECES) - 1)
+            if n == 1:
+                quantise_z(len(Z_PARTS) - 1)
         for g, t, first, end in by_gpsimd:
             nc.gpsimd.tensor_scalar(
                 out=y[g][:, t, first:end], in0=y[g][:, t, first:end], scalar1=amp_cols[:, g, t : t + 1], scalar2=0.0,
@@ -469,8 +471,9 @@ def tile_list_schema_drift_scores_kernel(
         quantise_y(1, 0, BANK)
         store_codes(1, 0, BANK)
         quantise_y(1, BANK, M - CHUNK)
+        store_codes(1, BANK, M - CHUNK)
         quantise_y(1, M - CHUNK, M)
-        store_codes(1, BANK, M)
+        store_codes(1, M - CHUNK, M)
         for q in (0, 2, 1, 3):
             [nc.sync, nc.scalar][q % 2].dma_start(
                 out=out_2[:, QUADS * q : QUADS * (q + 1), :].bitcast(I32),

@@ -180,7 +180,7 @@ def tile_list_schema_drift_scores_kernel(
         load_scale_rows(nc.sync, w4_plane_rest, w4_scales[:, :, P:H])
         nc.sync.dma_start(out=gains[:, BANK:S], in_=wgs[:, BANK:S])
         nc.sync.dma_start(pinned_list[:], offs3)
-        for a in range(PASSES):
+        for a in range(PASSES - 1):
             load_w1(2, a)
         load_scale_rows(nc.sync, w8_plane_raw, w8_scales)
         w8_raw = held([P, N], U32, "w8_raw")
@@ -191,6 +191,8 @@ def tile_list_schema_drift_scores_kernel(
                 out=w3_raw[g][:],
                 in_=w3[:, K_PASS * g : K_PASS * (g + 1)].rearrange("(p j) c -> p j c", j=PACK),
             )
+            if g == 0:
+                load_w1(2, PASSES - 1)
         old_rows = [held([P, M], F32, "old%d" % b) for b in range(BLOCKS)]
         for b in range(BLOCKS):
             nc.sync.dma_start(out=old_rows[b][:], in_=old[P * b : P * (b + 1), :])
@@ -199,7 +201,7 @@ def tile_list_schema_drift_scores_kernel(
 
 
         def encode(b, half, order, into):
-            sums = bank(2 if b == 1 else half, [P, BANK])
+            sums = bank((half, 2, half, 4 + half)[b], [P, BANK])
             cols = slice(BANK * half, BANK * (half + 1))
             for a, old_schema in order:
                 if old_schema:
@@ -310,7 +312,7 @@ def tile_list_schema_drift_scores_kernel(
         round_w3(1)
         last_deltas = held([P, BANK], F32, "deltas", tag="w3_raw1")
         encode(3, 1, old_passes + new_passes, last_deltas[:])
-        w8_codes = held([P, GROUPS, PACK, P], U32, "w8_codes", tag="w1_raw0_2")
+        w8_codes = held([P, GROUPS, PACK, P], U32, "w8_codes")
         nc.scalar.copy(
             out=w8_codes[:].rearrange("p g t (c i) -> p g c t i", i=4),
             in_=w8_raw[:].rearrange("p (g c i t) -> p g c t i", g=GROUPS, i=4, t=PACK),

@@ -129,8 +129,8 @@ def tile_list_schema_drift_scores_kernel(
                 out=v_plane[32 * r : 32 * r + 4].bitcast(I32),
                 in_=picked_scales[P - 32 + 8 * r : P - 32 + 8 * (r + 1), :].bitcast(I32),
             )
-        load_table(2)
         load_w1(0, 2)
+        load_table(2)
         w4_rows = w4_words.rearrange("a p c -> p a c")
         w4_first = held([P, PASSES, 2 * P], U8, "w4_first")
         w4_rest = held([P, PASSES, 2 * (H - P)], U8, "w4_rest")
@@ -167,9 +167,14 @@ def tile_list_schema_drift_scores_kernel(
         quantise_w1(0, 0, round_w1(0, 0, "rounded", 3))
         gather_words(1, 0, S, "v_codes1")
         quantise_w1(0, 1, round_w1(0, 1, "rounded", 3))
-        gather_words(2, 0, BANK, "v_codes2_0")
         quantise_w1(0, 2, round_w1(0, 2, "rounded", 3))
-        gather_words(2, BANK, BANK, "w1_raw0_2")
+        last_first = held([P, BANK], U32, "v_codes", tag="v_codes2_0")
+        for first in (0, CHUNK):
+            nc.vector.tensor_copy(
+                out=last_first[:, first : first + CHUNK], in_=table[2][:].indirect(entries(picked_list, first, CHUNK))
+            )
+        v_codes[2, 0] = last_first[:]
+        gather_words(2, BANK, BANK, "v_codes2_1")
         late_planes = shared.tile([P, late_bytes], U8, name="late_planes", align_bytes=64, offset=4 * T2)
         nc.gpsimd.memset(late_planes[:].bitcast(I32), 0)
         pages.append(shared.tile([P, T2], F32, name="page1", align_bytes=64, offset=0))
@@ -200,9 +205,10 @@ def tile_list_schema_drift_scores_kernel(
         nc.sync.dma_start(out=amp_cols[:], in_=amp.rearrange("(g p t) -> p g t", p=P, t=PACK))
 
 
-        def encode(b, half, order, into):
-            sums = bank((half, 2, half, 4 + half)[b], [P, BANK])
-            cols = slice(BANK * half, BANK * (half + 1))
+        def encode(b, half, order, into, index=None, first=0):
+            width = into.shape[1]
+            sums = bank((half, 2, half, 4 + half)[b] if index is None else index, [P, width])
+            cols = slice(BANK * half + first, BANK * half + first + width)
             for a, old_schema in order:
                 if old_schema:
                     words = w4_first[:, a, :] if b == 0 else w4_rest[:, a, 2 * P * (b - 1) : 2 * P * b]
@@ -214,7 +220,7 @@ def tile_list_schema_drift_scores_kernel(
                     codes, plane = w1_codes[span][:, a, own].bitcast(FP8X4), w1_plane[span][:, a, own]
                 nc.tensor.matmul_mx(
                     out=sums[:], lhsT=codes, lhsT_scale=plane,
-                    rhs=v_codes[a, half].bitcast(FP8X4), rhs_scale=(v_plane[:, a, cols] if a < 2 else v_plane_last[:, cols]),
+                    rhs=v_codes[a, half][:, first : first + width].bitcast(FP8X4), rhs_scale=(v_plane[:, a, cols] if a < 2 else v_plane_last[:, cols]),
                     start=((a, old_schema) == order[0]), stop=((a, old_schema) == order[-1]),
                 )
             nc.scalar.copy(out=into, in_=sums[:])
@@ -293,10 +299,14 @@ def tile_list_schema_drift_scores_kernel(
                     start=True, stop=True,
                 )
 
-        put_half(0, 0, new_passes[:2] + old_passes + new_passes[2:], "deltas0_0")
+        first_deltas = held([P, BANK], F32, "deltas", tag="deltas0_0")
+        for index, first in ((0, 0), (4, CHUNK)):
+            order = new_passes[:2] + old_passes[:2] + new_passes[2:] + old_passes[2:]
+            encode(0, 0, order, first_deltas[:, first : first + CHUNK], index, first)
+        scatter(0, 0, first_deltas[:])
         for a in range(PASSES):
             quantise_w1(1, a, round_w1(1, a, "rounded", 3))
-        put_half(0, 1, new_passes + old_passes, "w1_raw1_2")
+        put_half(0, 1, new_passes[:2] + old_passes[2:] + new_passes[2:] + old_passes[:2], "w1_raw1_2")
         warm_up(3, 1, 2)
         put_half(1, 0, old_passes + new_passes, "deltas1_0")
         quantise_w1(2, 0, round_w1(2, 0, "rounded", 3))
@@ -471,9 +481,8 @@ def tile_list_schema_drift_scores_kernel(
         quantise_y(0, BANK, M)
         store_codes(0, 0, M)
         quantise_y(1, 0, BANK)
-        store_codes(1, 0, BANK)
         quantise_y(1, BANK, M - CHUNK)
-        store_codes(1, BANK, M - CHUNK)
+        store_codes(1, 0, M - CHUNK)
         quantise_y(1, M - CHUNK, M)
         store_codes(1, M - CHUNK, M)
         for q in (0, 2, 1, 3):

@@ -307,7 +307,6 @@ def tile_list_schema_drift_scores_kernel(
         for a in range(PASSES):
             quantise_w1(1, a, round_w1(1, a, "rounded", 3))
         put_half(0, 1, new_passes[:2] + old_passes[2:] + new_passes[2:] + old_passes[:2], "w1_raw1_2")
-        warm_up(3, 1, 2)
         put_half(1, 0, old_passes + new_passes, "deltas1_0")
         quantise_w1(2, 0, round_w1(2, 0, "rounded", 3))
         put_half(1, 1, old_passes + new_passes, "w1_raw2_0")

@@ -332,7 +332,7 @@ def tile_list_schema_drift_scores_kernel(
         for c, index in enumerate((4, 5, 0, 1)):
             turned = turn_old(2, CHUNK * c, CHUNK, index)
             turn_picked(2, CHUNK * c, picked2[:, CHUNK * c : CHUNK * (c + 1)], turned)
-        warm_up(4, 0, 3)
+        warm_up(4, 0, 5)
         last_turned = [turn_old(last, first, width, c) for c, (first, width) in enumerate(PIECES[:3])]
         scatter(3, BANK, last_deltas[:])
 

from contextlib import ExitStack

import concourse.mybir as mybir
from concourse.masks import make_identity

K, H, N, T, S, T2, M = 1536, 512, 1024, 2048, 1024, 2048, 1024
FLOPS = 2 * (2 * K * H * S + 2 * H * N * M)

F32 = mybir.dt.float32
BF16 = mybir.dt.bfloat16
I32 = mybir.dt.int32
U32 = mybir.dt.uint32
U16 = mybir.dt.uint16
U8 = mybir.dt.uint8
FP8X4 = mybir.dt.float8_e4m3fn_x4
FP4X4 = mybir.dt.float4_e2m1fn_x4
ALU = mybir.AluOpType
ACT = mybir.ActivationFunctionType

P = 128
PACK = 4
K_PASS = P * PACK
PASSES = K // K_PASS
BLOCKS = H // P
GROUPS = N // K_PASS
BANK = 512
HALVES = S // BANK
QUADS = 4
LIST = 16
SCALE_ROW0 = P - 16 * PASSES
W1_SPANS = ((0, 128), (128, 128), (256, 256))
CHUNK = 256
CHUNKS = M // CHUNK
SCALAR_COLUMNS = 832
PIECES = ((0, 128), (128, 128), (256, 256), (512, 256), (768, 256))
Z_PARTS = ((0, 128), (128, 128), (256, 256), (512, 512))
BACK_BANKS = (6, 7, 3, 2, 3)
STEP_BANKS = (4, 6, 0, 2)


def tile_list_schema_drift_scores_kernel(
    tc, tab_words, tab_scales, offs, offs2, offs3, w1, w4_words, w4_scales, wgs, old, w3,
    w8_words, w8_scales, amp, out_0, out_1, out_2,
):
    nc = tc.nc
    with ExitStack() as ctx:
        lists = ctx.enter_context(tc.tile_pool(name="lists", bufs=1))
        keep = ctx.enter_context(tc.tile_pool(name="keep", bufs=1))
        shared = ctx.enter_context(tc.tile_pool(name="shared", bufs=1))
        psum = ctx.enter_context(tc.psum_pool(name="psum", bufs=1))

        def held(shape, dtype, name, tag=None, bufs=1):
            return keep.tile(shape, dtype, name=name, tag=tag or name, bufs=bufs, align_bytes=64)

        def bank(index, shape):
            return psum.tile(shape, F32, name="bank%d" % index, tag="bank%d" % index)

        def entries(list_tile, first, count):
            return list_tile[:, first // LIST : (first + count) // LIST]

        def load_scale_rows(queue, plane, rows):
            for r in range(QUADS):
                queue.dma_start(
                    out=plane[r:P:32].bitcast(I32),
                    in_=rows.rearrange("a (q r) c -> r q a c", r=QUADS)[r].bitcast(I32),
                )

        picked_list = lists.tile([P, S // LIST], U16, name="picked_list")
        slot_list = lists.tile([P, S // LIST], U16, name="slot_list")
        pinned_list = lists.tile([P, M // LIST], U16, name="pinned_list")

        table_scales = held([P, T], U8, "table_scales")
        v_plane = held([P, 2, S], U8, "v_plane")
        v_plane_last = held([P, S], U8, "v_plane_last")
        w4_plane_first = held([P, PASSES, P], U8, "w4_plane_first")
        pages = [held([P, T2], F32, "page0")]
        nc.vector.memset(w4_plane_first[:].bitcast(I32), 0)
        nc.vector.memset(table_scales[0:SCALE_ROW0, :].bitcast(I32), 0)
        nc.vector.memset(v_plane[:].bitcast(I32), 0)
        nc.vector.memset(pages[0][:].bitcast(I32), 0)
        nc.vector.memset(v_plane_last[:].bitcast(I32), 0)
        ident = held([P, P], F32, "ident")
        make_identity(nc, ident[:])

        late_bytes = PASSES * (H - P) + N
        table = [held([P, T], U32, "table%d" % a) for a in range(PASSES - 1)]
        table.append(shared.tile([P, T], U32, name="table_last", align_bytes=64, offset=late_bytes))
        w1_raw = {}

        def load_table(a):
            nc.sync.dma_start(
                out=table[a][:].bitcast(I32),
                in_=tab_words[a].rearrange("p t i -> p (t i)").bitcast(I32),
            )

        def load_w1(span, a):
            first, width = W1_SPANS[span]
            w1_raw[span, a] = held([P, PACK, width], F32, "w1_raw%d_%d" % (span, a))
            nc.sync.dma_start(
                out=w1_raw[span, a][:],
                in_=w1[K_PASS * a : K_PASS * (a + 1), first : first + width].rearrange("(p j) c -> p j c", j=PACK),
            )

        def round_w1(span, a, tag, bufs):
            rounded = held([P, W1_SPANS[span][1], PACK], BF16, "w1_rounded", tag=tag, bufs=bufs)
            nc.scalar.activation(
                out=rounded[:].rearrange("p (c i) j -> p c j i", i=4),
                in_=w1_raw[span, a][:].rearrange("p j (c i) -> p c j i", i=4),
                func=ACT.Copy,
                scale=-1.0,
            )
            return rounded

        nc.sync.dma_start(picked_list[:], offs)
        nc.sync.dma_start(
            out=table_scales[P - 32 : P, :].bitcast(I32),
            in_=tab_scales[0:2].rearrange("a k c -> k a c").bitcast(I32),
        )
        nc.sync.dma_start(out=table_scales[SCALE_ROW0 : P - 32, :].bitcast(I32), in_=tab_scales[2].bitcast(I32))
        load_table(0)
        load_scale_rows(nc.scalar, w4_plane_first, w4_scales[:, :, 0:P])
        load_w1(0, 0)
        load_table(1)
        load_w1(0, 1)
        picked_scales = held([P, S], U8, "picked_scales")
        nc.vector.tensor_copy(out=picked_scales[:], in_=table_scales[:].indirect(picked_list[:]))
        for r in (0, 2, 1, 3):
            nc.sync.dma_start(
                out=v_plane[32 * r : 32 * r + 4].bitcast(I32),
                in_=picked_scales[P - 32 + 8 * r : P - 32 + 8 * (r + 1), :].bitcast(I32),
            )
        load_w1(0, 2)
        load_table(2)
        w4_rows = w4_words.rearrange("a p c -> p a c")
        w4_first = held([P, PASSES, 2 * P], U8, "w4_first")
        w4_rest = held([P, PASSES, 2 * (H - P)], U8, "w4_rest")
        nc.sync.dma_start(out=w4_first[:].bitcast(I32), in_=w4_rows[:, :, 0 : 2 * P].bitcast(I32))
        for r in (0, 2, 1, 3):
            nc.sync.dma_start(
                out=v_plane_last[32 * r : 32 * r + 4].bitcast(I32),
                in_=picked_scales[SCALE_ROW0 + 4 * r : SCALE_ROW0 + 4 * (r + 1), :].bitcast(I32),
            )
        nc.sync.dma_start(slot_list[:], offs2)
        gains = held([P, S], F32, "gains")
        nc.sync.dma_start(out=gains[:, 0:BANK], in_=wgs[:, 0:BANK])
        for a in range(PASSES):
            load_w1(1, a)

        w1_codes = [held([P, PASSES, width], U32, "w1_codes%d" % first) for first, width in W1_SPANS]
        w1_plane = [held([P, PASSES, width], U8, "w1_plane%d" % first) for first, width in W1_SPANS]
        v_codes = {}

        def gather_words(a, first, count, tag):
            codes = held([P, count], U32, "v_codes", tag=tag)
            nc.vector.tensor_copy(out=codes[:], in_=table[a][:].indirect(entries(picked_list, first, count)))
            for half in range(first // BANK, (first + count) // BANK):
                v_codes[a, half] = codes[:, BANK * half - first : BANK * (half + 1) - first]

        def quantise_w1(span, a, rounded):
            nc.vector.quantize_mx(
                out=w1_codes[span][:, a, :].bitcast(FP8X4),
                scales=w1_plane[span][:, a, :],
                in_=rounded[:].rearrange("p c j -> p (c j)"),
            )

        gather_words(0, 0, S, "v_codes0")
        quantise_w1(0, 0, round_w1(0, 0, "rounded", 3))
        gather_words(1, 0, S, "v_codes1")
        quantise_w1(0, 1, round_w1(0, 1, "rounded", 3))
        quantise_w1(0, 2, round_w1(0, 2, "rounded", 3))
        last_first = held([P, BANK], U32, "v_codes", tag="v_codes2_0")
        for first in (0, CHUNK):
            nc.vector.tensor_copy(
                out=last_first[:, first : first + CHUNK], in_=table[2][:].indirect(entries(picked_list, first, CHUNK))
            )
        v_codes[2, 0] = last_first[:]
        gather_words(2, BANK, BANK, "v_codes2_1")
        late_planes = shared.tile([P, late_bytes], U8, name="late_planes", align_bytes=64, offset=4 * T2)
        nc.gpsimd.memset(late_planes[:].bitcast(I32), 0)
        pages.append(shared.tile([P, T2], F32, name="page1", align_bytes=64, offset=0))
        nc.gpsimd.memset(pages[1][:].bitcast(I32), 0)
        w4_plane_rest = late_planes[:, 0 : PASSES * (H - P)].rearrange("p (a c) -> p a c", a=PASSES)
        w8_plane_raw = late_planes[:, PASSES * (H - P) :].rearrange("p (a c) -> p a c", a=1)
        nc.sync.dma_start(out=w4_rest[:].bitcast(I32), in_=w4_rows[:, :, 2 * P : 2 * H].bitcast(I32))
        load_scale_rows(nc.sync, w4_plane_rest, w4_scales[:, :, P:H])
        nc.sync.dma_start(out=gains[:, BANK:S], in_=wgs[:, BANK:S])
        nc.sync.dma_start(pinned_list[:], offs3)
        for a in range(PASSES - 1):
            load_w1(2, a)
        load_scale_rows(nc.sync, w8_plane_raw, w8_scales)
        w8_raw = held([P, N], U32, "w8_raw")
        nc.sync.dma_start(out=w8_raw[:].bitcast(I32), in_=w8_words[0].rearrange("p c i -> p (c i)").bitcast(I32))
        w3_raw = [held([P, PACK, K_PASS], F32, "w3_raw%d" % g) for g in range(GROUPS)]
        for g in range(GROUPS):
            nc.sync.dma_start(
                out=w3_raw[g][:],
                in_=w3[:, K_PASS * g : K_PASS * (g + 1)].rearrange("(p j) c -> p j c", j=PACK),
            )
            if g == 0:
                load_w1(2, PASSES - 1)
        old_rows = [held([P, M], F32, "old%d" % b) for b in range(BLOCKS)]
        for b in range(BLOCKS):
            nc.sync.dma_start(out=old_rows[b][:], in_=old[P * b : P * (b + 1), :])
        amp_cols = held([P, GROUPS, PACK], F32, "amp_cols")
        nc.sync.dma_start(out=amp_cols[:], in_=amp.rearrange("(g p t) -> p g t", p=P, t=PACK))


        def encode(b, half, order, into, index=None, first=0):
            width = into.shape[1]
            sums = bank((half, 2, half, 4 + half)[b] if index is None else index, [P, width])
            cols = slice(BANK * half + first, BANK * half + first + width)
            for a, old_schema in order:
                if old_schema:
                    words = w4_first[:, a, :] if b == 0 else w4_rest[:, a, 2 * P * (b - 1) : 2 * P * b]
                    plane = w4_plane_first[:, a, :] if b == 0 else w4_plane_rest[:, a, P * (b - 1) : P * b]
                    codes = words.bitcast(FP4X4)
                else:
                    span = min(b, len(W1_SPANS) - 1)
                    own = slice(P * b - W1_SPANS[span][0], P * (b + 1) - W1_SPANS[span][0])
                    codes, plane = w1_codes[span][:, a, own].bitcast(FP8X4), w1_plane[span][:, a, own]
                nc.tensor.matmul_mx(
                    out=sums[:], lhsT=codes, lhsT_scale=plane,
                    rhs=v_codes[a, half][:, first : first + width].bitcast(FP8X4), rhs_scale=(v_plane[:, a, cols] if a < 2 else v_plane_last[:, cols]),
                    start=((a, old_schema) == order[0]), stop=((a, old_schema) == order[-1]),
                )
            nc.scalar.copy(out=into, in_=sums[:])

        def scatter(b, first, deltas):
            count = deltas.shape[1]
            nc.vector.tensor_tensor(
                out=pages[b % 2][:].indirect(entries(slot_list, first, count)),
                in0=deltas, in1=gains[:, first : first + count], op=ALU.mult,
            )

        def put_half(b, half, order, tag):
            deltas = held([P, BANK], F32, "deltas", tag=tag)
            encode(b, half, order, deltas[:])
            scatter(b, BANK * half, deltas[:])

        def encode_block(b, tag):
            deltas = held([P, S], F32, "deltas", tag=tag)
            for half in range(HALVES):
                encode(b, half, old_passes + new_passes, deltas[:, BANK * half : BANK * (half + 1)])
            return deltas

        new_passes = [(a, False) for a in range(PASSES)]
        old_passes = [(a, True) for a in range(PASSES)]

        z_turned = [held([P, width // P, 2, P, 2], BF16, "z_turned%d" % first) for first, width in PIECES]

        def fetch(b, first, count, tag):
            picked = held([P, count], F32, "picked", tag=tag)
            nc.vector.tensor_copy(out=picked[:], in_=pages[b % 2][:].indirect(entries(pinned_list, first, count)))
            return picked

        def turn_old(b, first, count, index):
            turned = bank(index, [P, count // P, P])
            for s in range(count // P):
                nc.tensor.matmul(
                    out=turned[:, s, :], lhsT=old_rows[b][:, first + P * s : first + P * (s + 1)],
                    rhs=ident[:], is_transpose=True, start=(s == 0), stop=False,
                )
            return turned

        def turn_picked(b, first, picked, turned):
            subs = picked.shape[1] // P
            for s in range(subs):
                nc.tensor.matmul(
                    out=turned[:, s, :], lhsT=picked[:, P * s : P * (s + 1)],
                    rhs=ident[:], is_transpose=True, start=False, stop=(s == subs - 1),
                )
            for c, (start, width) in enumerate(PIECES):
                if first <= start < first + P * subs:
                    own = slice((start - first) // P, (start + width - first) // P)
                    nc.scalar.copy(
                        out=z_turned[c][:, :, :, 32 * b : 32 * (b + 1), :],
                        in_=turned[:, own, :].rearrange("m s (q u e) -> m s u q e", u=2, e=2),
                    )

        def turn(b, picked):
            for half in range(M // BANK):
                turned = turn_old(b, BANK * half, BANK, 2 * b + half)
                turn_picked(b, BANK * half, picked[:, BANK * half : BANK * (half + 1)], turned)

        w3_rounded = [held([P, PACK, P, PACK], BF16, "w3_rounded%d" % g) for g in range(GROUPS)]

        def round_w3(g):
            nc.scalar.copy(
                out=w3_rounded[g][:].rearrange("p t m j -> p m t j"),
                in_=w3_raw[g][:].rearrange("p j (m t) -> p m t j", t=PACK),
            )

        def warm_up(index, a, count):
            warm = bank(index, [P, BANK])
            for n in range(count):
                nc.tensor.matmul_mx(
                    out=warm[:], lhsT=w1_codes[0][:, a, :].bitcast(FP8X4), lhsT_scale=w1_plane[0][:, a, :],
                    rhs=v_codes[a, 0].bitcast(FP8X4), rhs_scale=v_plane[:, a, 0:BANK],
                    start=True, stop=True,
                )

        first_deltas = held([P, BANK], F32, "deltas", tag="deltas0_0")
        for index, first in ((0, 0), (4, CHUNK)):
            order = new_passes[:2] + old_passes[:2] + new_passes[2:] + old_passes[2:]
            encode(0, 0, order, first_deltas[:, first : first + CHUNK], index, first)
        scatter(0, 0, first_deltas[:])
        for a in range(PASSES):
            quantise_w1(1, a, round_w1(1, a, "rounded", 3))
        put_half(0, 1, new_passes[:2] + old_passes[2:] + new_passes[2:] + old_passes[:2], "w1_raw1_2")
        put_half(1, 0, old_passes + new_passes, "deltas1_0")
        quantise_w1(2, 0, round_w1(2, 0, "rounded", 3))
        put_half(1, 1, old_passes + new_passes, "w1_raw2_0")
        quantise_w1(2, 1, round_w1(2, 1, "rounded", 3))
        picked0 = fetch(0, 0, M, "w1_raw2_1")
        quantise_w1(2, 2, round_w1(2, 2, "rounded", 3))
        picked1 = fetch(1, 0, M, "w1_raw2_2")
        scatter(2, 0, encode_block(2, "deltas2")[:])
        put_half(3, 0, old_passes + new_passes, "deltas0_0")
        round_w3(0)
        picked2 = fetch(2, 0, M, "w3_raw0")
        round_w3(1)
        last_deltas = held([P, BANK], F32, "deltas", tag="w3_raw1")
        encode(3, 1, old_passes + new_passes, last_deltas[:])
        w8_codes = held([P, GROUPS, PACK, P], U32, "w8_codes")
        nc.scalar.copy(
            out=w8_codes[:].rearrange("p g t (c i) -> p g c t i", i=4),
            in_=w8_raw[:].rearrange("p (g c i t) -> p g c t i", g=GROUPS, i=4, t=PACK),
        )
        turn(0, picked0)
        turn(1, picked1)
        last = BLOCKS - 1
        for c, index in enumerate((4, 5, 0, 1)):
            turned = turn_old(2, CHUNK * c, CHUNK, index)
            turn_picked(2, CHUNK * c, picked2[:, CHUNK * c : CHUNK * (c + 1)], turned)
        warm_up(4, 0, 5)
        last_turned = [turn_old(last, first, width, c) for c, (first, width) in enumerate(PIECES[:3])]
        scatter(3, BANK, last_deltas[:])

        z_codes = held([P, M], U32, "z_codes")
        z_plane = held([P, M], U8, "z_plane")
        z_rounded = [held([P, width, PACK], BF16, "z_rounded%d" % first) for first, width in Z_PARTS]

        def turn_back(c):
            first, width = PIECES[c]
            subs = width // P
            back = bank(BACK_BANKS[c], [P, subs, 2, P])
            for s in range(subs):
                for u in range(2):
                    nc.tensor.transpose(
                        back[:, s, u, :],
                        z_turned[c][:, s, u].rearrange("m p e -> m (p e)").bitcast(F32),
                        ident[:],
                    )
            part = min(c, len(Z_PARTS) - 1)
            words = z_rounded[part][:].rearrange("p m t -> p (m t)").bitcast(F32)
            own = first - Z_PARTS[part][0]
            nc.scalar.copy(
                out=words[:, 2 * own : 2 * (own + width)].rearrange("p (s m u) -> p s m u", s=subs, u=2),
                in_=back[:].rearrange("p s u m -> p s m u"),
            )

        def quantise_z(part):
            cols = slice(Z_PARTS[part][0], sum(Z_PARTS[part]))
            nc.vector.quantize_mx(
                out=z_codes[:, cols].bitcast(FP8X4), scales=z_plane[:, cols],
                in_=z_rounded[part][:].rearrange("p m t -> p (m t)"),
            )

        w3_codes, w3_plane = {}, {}

        def quantise_w3(g, tag):
            w3_codes[g] = held([P, K_PASS], U32, "w3_codes", tag=tag)
            w3_plane[g] = held([P, K_PASS], U8, "w3_plane%d" % g)
            nc.vector.quantize_mx(
                out=w3_codes[g][:].bitcast(FP8X4), scales=w3_plane[g][:],
                in_=w3_rounded[g][:].rearrange("p t m j -> p (t m j)"),
            )

        for c, (first, width) in enumerate(PIECES):
            picked = fetch(last, first, width, "picked3_%d" % c)
            if c >= 2:
                turn_back(c - 2)
            turn_picked(last, first, picked[:], last_turned[c] if c < 3 else turn_old(last, first, width, c - 3))
        quantise_w3(0, "gains")
        quantise_z(0)
        w8_plane = held([P, GROUPS, PACK, P], U8, "w8_plane", tag="z_rounded0")
        nc.vector.tensor_copy(
            out=w8_plane[:].rearrange("p g t (c i) -> p g c t i", i=16),
            in_=w8_plane_raw[:, 0, :].rearrange("p (g c i t) -> p g c t i", g=GROUPS, i=16, t=PACK),
        )
        turn_back(len(PIECES) - 2)
        quantise_z(1)
        quantise_z(2)
        quantise_w3(1, "z_rounded256")

        y = [held([P, PACK, M], F32, "y", tag="table%d" % g) for g in range(GROUPS)]
        last_bounded = held([P, 1, BANK], F32, "last_bounded")
        steps = [(0, 0, first, P) for first in (0, P)]
        steps.extend((0, t, CHUNK, CHUNK) for t in (0, 2))
        steps.extend((0, t, BANK, BANK) for t in range(PACK))
        steps.extend((1, t, first, BANK) for t in range(PACK) for first in (0, BANK))
        by_gpsimd = [(0, t, first, end) for first, end in ((0, CHUNK), (CHUNK, M)) for t in range(PACK)]
        by_gpsimd.extend((1, t, 0, M) for t in range(2))
        by_scalar = [(1, t, 0, M) for t in range(2, PACK)]

        def store_row(g, t, queue=nc.sync):
            queue.dma_start(
                out=out_0[K_PASS * g : K_PASS * (g + 1), :].rearrange("(p t) m -> p t m", t=PACK)[:, t, :],
                in_=y[g][:, t, :],
            )

        for n, (g, t0, first, width) in enumerate(steps):
            cols = slice(first, first + width)
            count = BANK // width
            bounded_sum = bank(STEP_BANKS[n % 4], [P, count, width])
            direct_sum = bank(STEP_BANKS[n % 4] + 1, [P, count, width])
            for sums, codes, plane in (
                (bounded_sum, w3_codes[g][:], w3_plane[g][:]),
                (direct_sum, w8_codes[:, g].rearrange("p t m -> p (t m)"), w8_plane[:, g].rearrange("p t m -> p (t m)")),
            ):
                for i in range(count):
                    n_cols = slice(P * (t0 + i), P * (t0 + i + 1))
                    nc.tensor.matmul_mx(
                        out=sums[:, i, :], lhsT=codes[:, n_cols].bitcast(FP8X4), lhsT_scale=plane[:, n_cols],
                        rhs=z_codes[:, cols].bitcast(FP8X4), rhs_scale=z_plane[:, cols],
                        start=True, stop=True,
                    )
            own = y[g][:, t0 : t0 + count, cols]
            bounded = last_bounded[:] if n == len(steps) - 1 else own
            nc.scalar.activation(out=bounded, in_=bounded_sum[:], func=ACT.Tanh)
            nc.vector.tensor_tensor(out=own, in0=bounded, in1=direct_sum[:], op=ALU.add)
            if n == 0:
                turn_back(len(PIECES) - 1)
            if n == 1:
                quantise_z(len(Z_PARTS) - 1)
        for g, t, first, end in by_gpsimd:
            nc.gpsimd.tensor_scalar(
                out=y[g][:, t, first:end], in0=y[g][:, t, first:end], scalar1=amp_cols[:, g, t : t + 1], scalar2=0.0,
                op0=ALU.mult, op1=ALU.add,
            )
            if end == M:
                store_row(g, t)
        for g, t, first, end in by_scalar:
            nc.scalar.activation(
                out=y[g][:, t, first:end], in_=y[g][:, t, first:end], func=ACT.Copy, scale=amp_cols[:, g, t : t + 1]
            )
            store_row(g, t, nc.scalar if t < PACK - 1 else nc.sync)

        y_plane = held([P, M], U8, "y_plane")
        y_rounded = held([P, GROUPS, M, PACK], BF16, "y_rounded", tag="last_bounded")

        y_codes = [held([P, M], U32, "y_codes%d" % g) for g in range(GROUPS)]

        def round_y(copy, g, first, end):
            copy(
                out=y_rounded[:, g, first:end, :].rearrange("p (c i) t -> p c t i", i=4),
                in_=y[g][:, :, first:end].rearrange("p t (c i) -> p c t i", i=4),
            )

        def quantise_y(g, first, end):
            cols = slice(first, end)
            nc.vector.quantize_mx(
                out=y_codes[g][:, cols].bitcast(FP8X4), scales=y_plane[QUADS * g : P, cols],
                in_=y_rounded[:, g, cols, :].rearrange("p m t -> p (m t)"),
            )

        def store_codes(g, first, end):
            nc.sync.dma_start(
                out=out_1[g].rearrange("p m t -> p (m t)").bitcast(I32)[:, first:end],
                in_=y_codes[g][:, first:end].bitcast(I32),
            )

        round_y(nc.vector.tensor_copy, 0, 0, BANK)
        round_y(nc.vector.tensor_copy, 0, BANK, M)
        quantise_y(0, 0, BANK)
        round_y(nc.vector.tensor_copy, 1, 0, M - SCALAR_COLUMNS)
        round_y(nc.scalar.copy, 1, M - SCALAR_COLUMNS, BANK)
        round_y(nc.scalar.copy, 1, BANK, M - CHUNK)
        round_y(nc.scalar.copy, 1, M - CHUNK, M)
        quantise_y(0, BANK, M)
        store_codes(0, 0, M)
        quantise_y(1, 0, BANK)
        quantise_y(1, BANK, M - CHUNK)
        store_codes(1, 0, M - CHUNK)
        quantise_y(1, M - CHUNK, M)
        store_codes(1, M - CHUNK, M)
        for q in (0, 2, 1, 3):
            [nc.sync, nc.scalar][q % 2].dma_start(
                out=out_2[:, QUADS * q : QUADS * (q + 1), :].bitcast(I32),
                in_=y_plane[32 * q : 32 * q + QUADS * GROUPS, :].bitcast(I32),
            )
